import numpy as np
import ml_dtypes


def mxq(x, axis, fmt="e4m3"):
    dtype, down = {"e4m3": (ml_dtypes.float8_e4m3fn, 7), "e5m2": (ml_dtypes.float8_e5m2, 14)}[fmt]
    v = np.moveaxis(np.asarray(x, np.float32).astype(ml_dtypes.bfloat16).astype(np.float64), axis, -1)
    blocks = v.reshape(v.shape[:-1] + (-1, 32))
    amax = np.abs(blocks).max(-1, keepdims=True)
    byte = np.maximum(np.where(amax > 0, np.frexp(amax)[1] - 1 + 127, 0) - down, 1)
    scale = np.exp2(byte - 127.0)
    codes = (blocks / scale).astype(np.float32).astype(dtype).astype(np.float64)
    return np.moveaxis((codes * scale).reshape(v.shape), -1, axis)


WIDE = False


def mx_kscale(k):
    if not WIDE:
        return np.ones(k)
    levels = np.array([18, -18])
    if k % 512:
        return np.exp2(np.random.permutation(np.resize(levels, k // 32))).repeat(32)
    a = np.empty((k // 512, 16))
    for p in range(k // 512):
        a[p, :8] = np.random.permutation(np.resize(levels, 8))
        for g in range(8):
            far = levels[np.abs(levels - a[p, g]) >= 10]
            a[p, g + 8] = far[np.random.randint(len(far))]
    return np.exp2(a.ravel()).repeat(32)


def f64(x):
    return np.asarray(x).astype(np.float64)


def striped(idx):
    return np.tile(np.asarray(idx).reshape(-1, 16).T, (8, 1)).astype(np.uint16)


def unstriped(offs):
    return offs[:16].T.reshape(-1).astype(np.int64)

def planes(y):
    n, m = y.shape
    v = y.astype(np.float32).astype(ml_dtypes.bfloat16).astype(np.float64).reshape(n // 32, 32, m)
    top = np.abs(v).max(1)
    byte = np.clip(np.where(top > 0, np.frexp(top)[1] - 1 + 127 - 7, 1), 1, 254)
    codes = (v * np.exp2(127.0 - byte)[:, None, :]).reshape(n, m).astype(np.float32).astype(ml_dtypes.float8_e4m3fn).view(np.uint8)
    words = codes.reshape(n // 512, 128, 4, m).transpose(0, 1, 3, 2)
    return np.ascontiguousarray(words), np.ascontiguousarray(byte.astype(np.uint8).reshape(n // 512, 16, m))


B, N, T, D, DV = 1, 1024, 2048, 512, 512


def setup_inputs():
    n = np.random.standard_normal
    idx = np.random.permutation(T)[:B * N]
    v = mx_kscale(DV)[:, None]
    coarse = lambda x: x.astype(np.float32).astype(ml_dtypes.bfloat16).astype(np.float64)
    r = np.random.randint(8, 33, T) / 16.0
    return {
        "dyT": (coarse(n((DV, T))) * v).astype(np.float32),
        "hT": (np.random.randint(-15, 16, (DV, T)) / 16.0).astype(np.float32),
        "ts": np.tile(r, (128, 1)).astype(np.float32),
        "wm": (n((B, DV, D)) / np.sqrt(DV) / v).astype(np.float32),
        "offs": striped(idx),
    }


def reference(dyT, hT, ts, wm, offs):
    idx = unstriped(offs)
    pick = lambda x: x[:, idx].reshape(x.shape[0], B, N).transpose(1, 0, 2)
    h = pick(f64(hT))
    dz = pick(f64(ts))[:, :1, :] * pick(f64(dyT)) * (1.0 - h * h)
    dx = mxq(f64(wm), 1, "e4m3").transpose(0, 2, 1) @ mxq(dz, 1, "e5m2")
    gx = np.zeros((D, T))
    gx[:, idx] = dx.transpose(1, 0, 2).reshape(D, B * N)
    out_0 = gx
    return (out_0,) + planes(out_0)

@@ -1,0 +1,176 @@
+from contextlib import ExitStack
+
+import concourse.mybir as mybir
+from concourse.masks import make_identity
+
+N, T, D, DV = 1024, 2048, 512, 512
+FLOPS = 2 * DV * D * N
+
+F32 = mybir.dt.float32
+BF16 = mybir.dt.bfloat16
+I32 = mybir.dt.int32
+U32 = mybir.dt.uint32
+U16 = mybir.dt.uint16
+U8 = mybir.dt.uint8
+E4M3 = mybir.dt.float8_e4m3fn_x4
+E5M2 = mybir.dt.float8_e5m2_x4
+ALU = mybir.AluOpType
+ACT = mybir.ActivationFunctionType
+
+P = 128
+PACK = 4
+HALF = 512
+QUAD = 32
+
+
+def tile_attend_gex_pl_tnh_x_kernel(tc, dyT, hT, ts, wm, offs, out_0, out_1, out_2):
+    nc = tc.nc
+    with ExitStack() as ctx:
+        keep = ctx.enter_context(tc.tile_pool(name="keep", bufs=1))
+        psum = ctx.enter_context(tc.psum_pool(name="psum", bufs=1))
+
+        offsets = keep.tile([P, N // 16], U16, name="offsets")
+        nc.sync.dma_start(offsets[:], offs)
+
+        def listed(s):
+            return offsets[:, s * (HALF // 16) : (s + 1) * (HALF // 16)]
+
+        banks = [psum.tile([P, HALF], F32, name="bank%d" % i) for i in range(8)]
+
+        ts_window = keep.tile([P, T], F32, name="ts_window", tag="ts_window")
+        nc.sync.dma_start(ts_window[96:P, :], ts[96:P, :])
+        nc.vector.memset(ts_window[0:96, :], 0.0)
+
+        h_rows = hT.rearrange("(p j) c -> p j c", j=PACK)
+        dy_rows = dyT.rearrange("(p j) c -> p j c", j=PACK)
+        h_window = [keep.tile([P, T], F32, name="h_window%d" % t, tag="h_window%d" % t) for t in range(PACK)]
+        dy_window = [keep.tile([P, T], F32, name="dy_window%d" % t, tag="dy_window%d" % t) for t in range(PACK)]
+        w_raw = keep.tile([P, PACK, D], F32, name="w_raw")
+        nc.sync.dma_start(h_window[0][:], h_rows[:, 0, :])
+        for t in range(1, PACK):
+            if t == PACK - 1:
+                nc.sync.dma_start(w_raw[:], wm[0].rearrange("(p j) d -> p j d", j=PACK))
+            nc.sync.dma_start(h_window[t][:], h_rows[:, t, :])
+            nc.sync.dma_start(dy_window[t - 1][:], dy_rows[:, t - 1, :])
+        nc.sync.dma_start(dy_window[PACK - 1][:], dy_rows[:, PACK - 1, :])
+
+        identity = keep.tile([P, P], F32, name="identity")
+        make_identity(nc, identity[:])
+
+        windows = [keep.tile([P, T], F32, name="window0")]
+        nc.vector.memset(windows[0][:], 0.0)
+
+        def zeroed_window(freed):
+            window = keep.tile([P, T], F32, name="window%d" % len(windows), tag=freed)
+            nc.gpsimd.memset(window[:], 0.0)
+            windows.append(window)
+
+        ts_listed = keep.tile([P, N], F32, name="ts_listed")
+        nc.vector.tensor_copy(ts_listed[:], ts_window[:].indirect(offsets[:]))
+        minus_ts = keep.tile([P, N // P], F32, name="minus_ts")
+        for s in range(2):
+            for c in range(4):
+                nc.tensor.transpose(banks[s][:, c * P : (c + 1) * P], ts_listed[:, s * HALF + c * P : s * HALF + (c + 1) * P], identity[:])
+            nc.scalar.activation(minus_ts[:, 4 * s : 4 * s + 4], banks[s][:, 96:HALF:P], ACT.Copy, scale=-1.0)
+            for c in range(4):
+                column = minus_ts[:, 4 * s + c : 4 * s + c + 1].to_broadcast([P, P])
+                nc.tensor.transpose(banks[2 + s][:, c * P : (c + 1) * P], column, identity[:])
+
+        dz = [keep.tile([P, PACK, HALF], F32, name="dz%d" % s) for s in range(2)]
+        factor_b = keep.tile([P, HALF], F32, name="factor_b")
+        factor = [dz[1][:, 2, :], factor_b[:]]
+        squares = {}
+        h_listed = keep.tile([P, 2, HALF], F32, name="h_listed", tag="ts_window")
+
+        def gather_h(t, s):
+            nc.vector.tensor_copy(h_listed[:, s, :], h_window[t][:].indirect(listed(s)))
+            squares[t, s] = keep.tile([P, HALF], F32, name="square%d%d" % (t, s))
+            nc.scalar.activation(squares[t, s][:], h_listed[:, s, :], ACT.Square)
+
+        def make_factor(t, s):
+            nc.vector.scalar_tensor_tensor(factor[s], squares[t, s][:], 1.0, banks[2 + s][:], ALU.subtract, ALU.mult)
+
+        grouped = [keep.tile([P, HALF, PACK], BF16, name="grouped%d" % s, align_bytes=64) for s in range(2)]
+
+        def gather_dy(t, s):
+            nc.vector.tensor_tensor(dz[s][:, t, :], dy_window[t][:].indirect(listed(s)), factor[s], ALU.mult)
+            if t % 2 == 1:
+                nc.scalar.copy(grouped[s][:, :, t - 1 : t + 1], dz[s][:, t - 1 : t + 1, :].rearrange("p e c -> p c e"))
+
+        dz_codes = [keep.tile([P, HALF], U32, name="dz_codes%d" % s, align_bytes=64) for s in range(2)]
+        dz_scales = [keep.tile([P, HALF], U8, name="dz_scales%d" % s, align_bytes=64) for s in range(2)]
+
+        def quantize_dz(s):
+            nc.vector.quantize_mx(dz_codes[s][:].bitcast(E5M2), dz_scales[s][:], grouped[s][:].rearrange("p c j -> p (c j)"))
+
+        w_grouped = keep.tile([P, D, PACK], BF16, name="w_grouped", align_bytes=64)
+        w_codes = keep.tile([P, D], U32, name="w_codes", align_bytes=64)
+        w_scales = keep.tile([P, D], U8, name="w_scales", align_bytes=64)
+
+        for t in range(PACK):
+            for s in range(2):
+                gather_h(t, s)
+            if t < PACK - 1:
+                zeroed_window("h_window%d" % t)
+            if t == PACK - 1:
+                nc.scalar.copy(w_grouped[:], w_raw[:].rearrange("p j d -> p d j"))
+                nc.vector.quantize_mx(w_codes[:].bitcast(E4M3), w_scales[:], w_grouped[:].rearrange("p d j -> p (d j)"))
+                break
+            for s in range(2):
+                if t > 0:
+                    gather_dy(t - 1, s)
+            for s in range(2):
+                make_factor(t, s)
+        for s in range(2):
+            gather_dy(PACK - 2, s)
+            make_factor(PACK - 1, s)
+            gather_dy(PACK - 1, s)
+            quantize_dz(s)
+
+        def multiply_and_scatter(w, s, bank):
+            cols = slice(w * P, (w + 1) * P)
+            nc.tensor.matmul_mx(bank[:], lhsT=w_codes[:, cols].bitcast(E4M3), lhsT_scale=w_scales[:, cols],
+                                rhs=dz_codes[s][:].bitcast(E5M2), rhs_scale=dz_scales[s][:], start=True, stop=True)
+            dx = keep.tile([P, HALF], F32, name="dx%d%d" % (w, s))
+            nc.scalar.copy(dx[:], bank[:])
+            nc.vector.tensor_copy(windows[w][:].indirect(listed(s)), dx[:])
+            if s == 1:
+                nc.sync.dma_start(out_0[cols, :], windows[w][:])
+
+        words_out = out_1[0].rearrange("p t l -> p (t l)").bitcast(I32)
+        scales_out = out_2[0].bitcast(I32)
+        out_scales = keep.tile([P, HALF], U8, name="out_scales", align_bytes=64)
+        turn_banks = [banks[0], banks[1], banks[6], banks[7]]
+
+        def quantize_window(w):
+            regrouped = keep.tile([P, HALF * PACK], BF16, name="regrouped%d" % w, align_bytes=64)
+            for j in range(4):
+                turned = turn_banks[j]
+                for b in range(4):
+                    first = b * HALF + j * P
+                    nc.tensor.transpose(turned[:, b * P : (b + 1) * P], windows[w][:, first : first + P], identity[:])
+                rounded = keep.tile([P, HALF], BF16, name="rounded%d%d" % (w, j))
+                copy = nc.vector.tensor_copy if (w == 3 and j >= 2) else nc.scalar.copy
+                copy(rounded[:].rearrange("t (u q e) -> t u q e", u=2, e=2), turned[:].rearrange("t (q u e) -> t u q e", u=2, e=2))
+                back = banks[2 + j // 2]
+                for u in range(2):
+                    first = (j % 2) * 256 + u * P
+                    nc.tensor.transpose(back[:, first : first + P], rounded[:].bitcast(F32)[:, u * P : (u + 1) * P], identity[:])
+                if j % 2 == 1:
+                    target = regrouped[:].bitcast(F32)[:, (j // 2) * HALF : (j // 2 + 1) * HALF]
+                    copy(target.rearrange("q (j t u) -> q j t u", j=2, u=2), back[:].rearrange("q (j u t) -> q j t u", j=2, u=2))
+            codes = keep.tile([P, HALF], U32, name="codes%d" % w, align_bytes=64)
+            nc.vector.quantize_mx(codes[:].bitcast(E4M3), out_scales[4 * w : P, :], regrouped[:])
+            for b in range(4):
+                nc.sync.dma_start(words_out[w * QUAD : (w + 1) * QUAD, b * HALF : (b + 1) * HALF], codes[b * QUAD : (b + 1) * QUAD, :].bitcast(I32))
+
+        for i, (w, s) in enumerate([(0, 0), (1, 0), (0, 1), (1, 1), (2, 0), (2, 1)]):
+            multiply_and_scatter(w, s, banks[4 + i % 2])
+        quantize_window(0)
+        multiply_and_scatter(3, 0, banks[3])
+        quantize_window(1)
+        multiply_and_scatter(3, 1, banks[3])
+        quantize_window(2)
+        quantize_window(3)
+        for b in range(4):
+            nc.sync.dma_start(scales_out[:, b * P : (b + 1) * P], out_scales[b * QUAD : b * QUAD + 16, :].bitcast(I32))

@@ -39,35 +39,39 @@ def tile_attend_gex_pl_tnh_x_kernel(tc, dyT, hT, ts, wm, offs, out_0, out_1, out
 
         ts_window = keep.tile([P, T], F32, name="ts_window", tag="ts_window")
         nc.sync.dma_start(ts_window[96:P, :], ts[96:P, :])
-        nc.vector.memset(ts_window[0:96, :], 0.0)
+        nc.gpsimd.memset(ts_window[0:96, :], 0.0)
 
         h_rows = hT.rearrange("(p j) c -> p j c", j=PACK)
         dy_rows = dyT.rearrange("(p j) c -> p j c", j=PACK)
         h_window = [keep.tile([P, T], F32, name="h_window%d" % t, tag="h_window%d" % t) for t in range(PACK)]
         dy_window = [keep.tile([P, T], F32, name="dy_window%d" % t, tag="dy_window%d" % t) for t in range(PACK)]
-        w_raw = keep.tile([P, PACK, D], F32, name="w_raw")
+        w_rows = wm[0].rearrange("(p j) d -> p j d", j=PACK)
+        w_raw = [keep.tile([P, PACK, D // 2], F32, name="w_raw%d" % g) for g in range(2)]
         nc.sync.dma_start(h_window[0][:], h_rows[:, 0, :])
         for t in range(1, PACK):
-            if t == PACK - 1:
-                nc.sync.dma_start(w_raw[:], wm[0].rearrange("(p j) d -> p j d", j=PACK))
             nc.sync.dma_start(h_window[t][:], h_rows[:, t, :])
             nc.sync.dma_start(dy_window[t - 1][:], dy_rows[:, t - 1, :])
+        nc.sync.dma_start(w_raw[0][:], w_rows[:, :, 0 : D // 2])
         nc.sync.dma_start(dy_window[PACK - 1][:], dy_rows[:, PACK - 1, :])
+        nc.sync.dma_start(w_raw[1][:], w_rows[:, :, D // 2 : D])
 
         identity = keep.tile([P, P], F32, name="identity")
         make_identity(nc, identity[:])
 
-        windows = [keep.tile([P, T], F32, name="window0")]
-        nc.vector.memset(windows[0][:], 0.0)
+        windows = []
 
-        def zeroed_window(freed):
-            window = keep.tile([P, T], F32, name="window%d" % len(windows), tag=freed)
+        def zeroed_window(slot):
+            window = keep.tile([P, T], F32, name="window%d" % len(windows), tag=slot, align_bytes=64)
             nc.gpsimd.memset(window[:], 0.0)
             windows.append(window)
 
+        zeroed_window("window0")
+        zeroed_window("window1")
+
         ts_listed = keep.tile([P, N], F32, name="ts_listed")
         nc.vector.tensor_copy(ts_listed[:], ts_window[:].indirect(offsets[:]))
-        minus_ts = keep.tile([P, N // P], F32, name="minus_ts")
+        minus_ts_rows = keep.tile([P, 2, HALF], F32, name="minus_ts_rows")
+        minus_ts = keep.tile([P, N // P], F32, name="minus_ts", tag="minus_ts")
         for s in range(2):
             for c in range(4):
                 nc.tensor.transpose(banks[s][:, c * P : (c + 1) * P], ts_listed[:, s * HALF + c * P : s * HALF + (c + 1) * P], identity[:])
@@ -75,63 +79,72 @@ def tile_attend_gex_pl_tnh_x_kernel(tc, dyT, hT, ts, wm, offs, out_0, out_1, out
             for c in range(4):
                 column = minus_ts[:, 4 * s + c : 4 * s + c + 1].to_broadcast([P, P])
                 nc.tensor.transpose(banks[2 + s][:, c * P : (c + 1) * P], column, identity[:])
+            nc.scalar.copy(minus_ts_rows[:, s, :], banks[2 + s][:])
 
-        dz = [keep.tile([P, PACK, HALF], F32, name="dz%d" % s) for s in range(2)]
-        factor_b = keep.tile([P, HALF], F32, name="factor_b")
-        factor = [dz[1][:, 2, :], factor_b[:]]
-        squares = {}
-        h_listed = keep.tile([P, 2, HALF], F32, name="h_listed", tag="ts_window")
-
-        def gather_h(t, s):
-            nc.vector.tensor_copy(h_listed[:, s, :], h_window[t][:].indirect(listed(s)))
-            squares[t, s] = keep.tile([P, HALF], F32, name="square%d%d" % (t, s))
-            nc.scalar.activation(squares[t, s][:], h_listed[:, s, :], ACT.Square)
-
-        def make_factor(t, s):
-            nc.vector.scalar_tensor_tensor(factor[s], squares[t, s][:], 1.0, banks[2 + s][:], ALU.subtract, ALU.mult)
-
-        grouped = [keep.tile([P, HALF, PACK], BF16, name="grouped%d" % s, align_bytes=64) for s in range(2)]
-
-        def gather_dy(t, s):
-            nc.vector.tensor_tensor(dz[s][:, t, :], dy_window[t][:].indirect(listed(s)), factor[s], ALU.mult)
-            if t % 2 == 1:
-                nc.scalar.copy(grouped[s][:, :, t - 1 : t + 1], dz[s][:, t - 1 : t + 1, :].rearrange("p e c -> p c e"))
-
+        dz = [keep.tile([P, PACK, HALF], F32, name="dz%d" % s, tag="dz%d" % s, align_bytes=64) for s in range(2)]
+        h_listed = keep.tile([P, 2, 2, HALF], F32, name="h_listed", tag="ts_window")
+        factors = keep.tile([P, PACK, 2, HALF], F32, name="factors", tag="minus_ts")
+        factor = [factors[:, t, :, :] for t in range(PACK)]
+        grouped = [keep.tile([P, HALF, PACK], BF16, name="grouped%d" % s, tag="grouped%d" % s, align_bytes=64) for s in range(2)]
         dz_codes = [keep.tile([P, HALF], U32, name="dz_codes%d" % s, align_bytes=64) for s in range(2)]
         dz_scales = [keep.tile([P, HALF], U8, name="dz_scales%d" % s, align_bytes=64) for s in range(2)]
+        w_codes = keep.tile([P, D], U32, name="w_codes", align_bytes=64)
+        w_scales = keep.tile([P, D], U8, name="w_scales", align_bytes=64)
+        last = PACK - 1
+
+        def gather_h(t, s):
+            f = factor[t][:, s, :]
+            nc.vector.tensor_copy(h_listed[:, t % 2, s, :], h_window[t][:].indirect(listed(s)))
+            nc.scalar.activation(f, h_listed[:, t % 2, s, :], ACT.Square)
+            if t < last:
+                nc.scalar.activation(f, f, ACT.Identity, bias=-1.0)
+                nc.gpsimd.tensor_tensor(f, f, minus_ts_rows[:, s, :], ALU.mult)
+
+        def gather_dy(t, s):
+            nc.vector.tensor_copy(dz[s][:, t, :], dy_window[t][:].indirect(listed(s)))
+            nc.gpsimd.tensor_tensor(dz[s][:, t, :], dz[s][:, t, :], factor[t][:, s, :], ALU.mult)
+
+        def gather_dy_times(t, s, f):
+            nc.vector.tensor_tensor(dz[s][:, t, :], dy_window[t][:].indirect(listed(s)), f, ALU.mult)
+
+        def last_factor(s, f):
+            nc.vector.scalar_tensor_tensor(f, factor[last][:, s, :], 1.0, banks[2 + s][:], ALU.subtract, ALU.mult)
+
+        def interleave(s, first, count):
+            nc.scalar.copy(grouped[s][:, :, first : first + count], dz[s][:, first : first + count, :].rearrange("p e c -> p c e"))
 
         def quantize_dz(s):
             nc.vector.quantize_mx(dz_codes[s][:].bitcast(E5M2), dz_scales[s][:], grouped[s][:].rearrange("p c j -> p (c j)"))
 
-        w_grouped = keep.tile([P, D, PACK], BF16, name="w_grouped", align_bytes=64)
-        w_codes = keep.tile([P, D], U32, name="w_codes", align_bytes=64)
-        w_scales = keep.tile([P, D], U8, name="w_scales", align_bytes=64)
+        def quantize_w(g):
+            cols = slice(g * D // 2, (g + 1) * D // 2)
+            w_grouped = keep.tile([P, D // 2, PACK], BF16, name="w_grouped%d" % g, align_bytes=64)
+            nc.scalar.copy(w_grouped[:], w_raw[g][:].rearrange("p j d -> p d j"))
+            nc.vector.quantize_mx(w_codes[:, cols].bitcast(E4M3), w_scales[:, cols], w_grouped[:].rearrange("p d j -> p (d j)"))
 
         for t in range(PACK):
             for s in range(2):
                 gather_h(t, s)
-            if t < PACK - 1:
-                zeroed_window("h_window%d" % t)
-            if t == PACK - 1:
-                nc.scalar.copy(w_grouped[:], w_raw[:].rearrange("p j d -> p d j"))
-                nc.vector.quantize_mx(w_codes[:].bitcast(E4M3), w_scales[:], w_grouped[:].rearrange("p d j -> p (d j)"))
-                break
             for s in range(2):
-                if t > 0:
+                if 0 < t < last:
                     gather_dy(t - 1, s)
-            for s in range(2):
-                make_factor(t, s)
-        for s in range(2):
-            gather_dy(PACK - 2, s)
-            make_factor(PACK - 1, s)
-            gather_dy(PACK - 1, s)
-            quantize_dz(s)
+        interleave(0, 0, 2)
+        gather_dy(2, 0)
+        last_factor(0, dz[1][:, 2, :])
+        quantize_w(0)
+        gather_dy_times(last, 0, dz[1][:, 2, :])
+        interleave(0, 2, 2)
+        gather_dy_times(2, 1, factor[2][:, 1, :])
+        quantize_dz(0)
+        factor_b = keep.tile([P, HALF], F32, name="factor_b", tag="grouped0", align_bytes=64)
+        last_factor(1, factor_b[:])
+        gather_dy_times(last, 1, factor_b[:])
 
-        def multiply_and_scatter(w, s, bank):
+        def multiply_and_scatter(w, s, bank, slot=None):
             cols = slice(w * P, (w + 1) * P)
             nc.tensor.matmul_mx(bank[:], lhsT=w_codes[:, cols].bitcast(E4M3), lhsT_scale=w_scales[:, cols],
                                 rhs=dz_codes[s][:].bitcast(E5M2), rhs_scale=dz_scales[s][:], start=True, stop=True)
-            dx = keep.tile([P, HALF], F32, name="dx%d%d" % (w, s))
+            dx = keep.tile([P, HALF], F32, name="dx%d%d" % (w, s), tag=slot or "dx%d%d" % (w, s), align_bytes=64)
             nc.scalar.copy(dx[:], bank[:])
             nc.vector.tensor_copy(windows[w][:].indirect(listed(s)), dx[:])
             if s == 1:
@@ -143,20 +156,21 @@ def tile_attend_gex_pl_tnh_x_kernel(tc, dyT, hT, ts, wm, offs, out_0, out_1, out
         turn_banks = [banks[0], banks[1], banks[6], banks[7]]
 
         def quantize_window(w):
-            regrouped = keep.tile([P, HALF * PACK], BF16, name="regrouped%d" % w, align_bytes=64)
+            regrouped = keep.tile([P, HALF * PACK], BF16, name="regrouped%d" % w, tag="regrouped%d" % (w % 2), align_bytes=64)
             for j in range(4):
-                turned = turn_banks[j]
                 for b in range(4):
                     first = b * HALF + j * P
-                    nc.tensor.transpose(turned[:, b * P : (b + 1) * P], windows[w][:, first : first + P], identity[:])
-                rounded = keep.tile([P, HALF], BF16, name="rounded%d%d" % (w, j))
-                copy = nc.vector.tensor_copy if (w == 3 and j >= 2) else nc.scalar.copy
-                copy(rounded[:].rearrange("t (u q e) -> t u q e", u=2, e=2), turned[:].rearrange("t (q u e) -> t u q e", u=2, e=2))
+                    nc.tensor.transpose(turn_banks[j][:, b * P : (b + 1) * P], windows[w][:, first : first + P], identity[:])
+            for j in range(4):
+                rounded = keep.tile([P, HALF], BF16, name="rounded%d%d" % (w, j), tag="rounded%d" % j)
+                copy = nc.vector.tensor_copy if (w == 3 and j % 2 == 1) else nc.scalar.copy
+                copy(rounded[:].rearrange("t (u q e) -> t u q e", u=2, e=2), turn_banks[j][:].rearrange("t (q u e) -> t u q e", u=2, e=2))
                 back = banks[2 + j // 2]
                 for u in range(2):
                     first = (j % 2) * 256 + u * P
                     nc.tensor.transpose(back[:, first : first + P], rounded[:].bitcast(F32)[:, u * P : (u + 1) * P], identity[:])
                 if j % 2 == 1:
+                    copy = nc.vector.tensor_copy if (w == 3 and j == 3) else nc.scalar.copy
                     target = regrouped[:].bitcast(F32)[:, (j // 2) * HALF : (j // 2 + 1) * HALF]
                     copy(target.rearrange("q (j t u) -> q j t u", j=2, u=2), back[:].rearrange("q (j u t) -> q j t u", j=2, u=2))
             codes = keep.tile([P, HALF], U32, name="codes%d" % w, align_bytes=64)
@@ -164,8 +178,17 @@ def tile_attend_gex_pl_tnh_x_kernel(tc, dyT, hT, ts, wm, offs, out_0, out_1, out
             for b in range(4):
                 nc.sync.dma_start(words_out[w * QUAD : (w + 1) * QUAD, b * HALF : (b + 1) * HALF], codes[b * QUAD : (b + 1) * QUAD, :].bitcast(I32))
 
-        for i, (w, s) in enumerate([(0, 0), (1, 0), (0, 1), (1, 1), (2, 0), (2, 1)]):
-            multiply_and_scatter(w, s, banks[4 + i % 2])
+        multiply_and_scatter(0, 0, banks[4])
+        interleave(1, 0, PACK)
+        quantize_dz(1)
+        quantize_w(1)
+        zeroed_window("grouped1")
+        multiply_and_scatter(1, 0, banks[5], "dz1")
+        multiply_and_scatter(0, 1, banks[4])
+        zeroed_window("dx01")
+        multiply_and_scatter(1, 1, banks[5])
+        multiply_and_scatter(2, 0, banks[4])
+        multiply_and_scatter(2, 1, banks[5])
         quantize_window(0)
         multiply_and_scatter(3, 0, banks[3])
         quantize_window(1)
@@ -173,4 +196,4 @@ def tile_attend_gex_pl_tnh_x_kernel(tc, dyT, hT, ts, wm, offs, out_0, out_1, out
         quantize_window(2)
         quantize_window(3)
         for b in range(4):
-            nc.sync.dma_start(scales_out[:, b * P : (b + 1) * P], out_scales[b * QUAD : b * QUAD + 16, :].bitcast(I32))
+            nc.scalar.dma_start(scales_out[:, b * P : (b + 1) * P], out_scales[b * QUAD : b * QUAD + 16, :].bitcast(I32))

@@ -37,6 +37,9 @@ def tile_attend_gex_pl_tnh_x_kernel(tc, dyT, hT, ts, wm, offs, out_0, out_1, out
 
         banks = [psum.tile([P, HALF], F32, name="bank%d" % i) for i in range(8)]
 
+        identity = keep.tile([P, P], F32, name="identity")
+        make_identity(nc, identity[:])
+
         ts_window = keep.tile([P, T], F32, name="ts_window", tag="ts_window")
         nc.sync.dma_start(ts_window[96:P, :], ts[96:P, :])
         nc.gpsimd.memset(ts_window[0:96, :], 0.0)
@@ -51,12 +54,9 @@ def tile_attend_gex_pl_tnh_x_kernel(tc, dyT, hT, ts, wm, offs, out_0, out_1, out
         for t in range(1, PACK):
             nc.sync.dma_start(h_window[t][:], h_rows[:, t, :])
             nc.sync.dma_start(dy_window[t - 1][:], dy_rows[:, t - 1, :])
-        nc.sync.dma_start(w_raw[0][:], w_rows[:, :, 0 : D // 2])
         nc.sync.dma_start(dy_window[PACK - 1][:], dy_rows[:, PACK - 1, :])
+        nc.sync.dma_start(w_raw[0][:], w_rows[:, :, 0 : D // 2])
         nc.sync.dma_start(w_raw[1][:], w_rows[:, :, D // 2 : D])
-
-        identity = keep.tile([P, P], F32, name="identity")
-        make_identity(nc, identity[:])
 
         windows = []
 
@@ -67,12 +67,13 @@ def tile_attend_gex_pl_tnh_x_kernel(tc, dyT, hT, ts, wm, offs, out_0, out_1, out
 
         zeroed_window("window0")
         zeroed_window("window1")
+        zeroed_window("window2")
 
         ts_listed = keep.tile([P, N], F32, name="ts_listed")
-        nc.vector.tensor_copy(ts_listed[:], ts_window[:].indirect(offsets[:]))
         minus_ts_rows = keep.tile([P, 2, HALF], F32, name="minus_ts_rows")
         minus_ts = keep.tile([P, N // P], F32, name="minus_ts", tag="minus_ts")
         for s in range(2):
+            nc.vector.tensor_copy(ts_listed[:, s * HALF : (s + 1) * HALF], ts_window[:].indirect(listed(s)))
             for c in range(4):
                 nc.tensor.transpose(banks[s][:, c * P : (c + 1) * P], ts_listed[:, s * HALF + c * P : s * HALF + (c + 1) * P], identity[:])
             nc.scalar.activation(minus_ts[:, 4 * s : 4 * s + 4], banks[s][:, 96:HALF:P], ACT.Copy, scale=-1.0)
@@ -96,8 +97,9 @@ def tile_attend_gex_pl_tnh_x_kernel(tc, dyT, hT, ts, wm, offs, out_0, out_1, out
             f = factor[t][:, s, :]
             nc.vector.tensor_copy(h_listed[:, t % 2, s, :], h_window[t][:].indirect(listed(s)))
             nc.scalar.activation(f, h_listed[:, t % 2, s, :], ACT.Square)
-            if t < last:
+            if (t, s) != (last, 0):
                 nc.scalar.activation(f, f, ACT.Identity, bias=-1.0)
+            if t + s < last:
                 nc.gpsimd.tensor_tensor(f, f, minus_ts_rows[:, s, :], ALU.mult)
 
         def gather_dy(t, s):
@@ -107,8 +109,8 @@ def tile_attend_gex_pl_tnh_x_kernel(tc, dyT, hT, ts, wm, offs, out_0, out_1, out
         def gather_dy_times(t, s, f):
             nc.vector.tensor_tensor(dz[s][:, t, :], dy_window[t][:].indirect(listed(s)), f, ALU.mult)
 
-        def last_factor(s, f):
-            nc.vector.scalar_tensor_tensor(f, factor[last][:, s, :], 1.0, banks[2 + s][:], ALU.subtract, ALU.mult)
+        def late_factor(t, s, f):
+            nc.vector.scalar_tensor_tensor(f, factor[t][:, s, :], 1.0, banks[2 + s][:], ALU.subtract, ALU.mult)
 
         def interleave(s, first, count):
             nc.scalar.copy(grouped[s][:, :, first : first + count], dz[s][:, first : first + count, :].rearrange("p e c -> p c e"))
@@ -118,8 +120,9 @@ def tile_attend_gex_pl_tnh_x_kernel(tc, dyT, hT, ts, wm, offs, out_0, out_1, out
 
         def quantize_w(g):
             cols = slice(g * D // 2, (g + 1) * D // 2)
-            w_grouped = keep.tile([P, D // 2, PACK], BF16, name="w_grouped%d" % g, align_bytes=64)
-            nc.scalar.copy(w_grouped[:], w_raw[g][:].rearrange("p j d -> p d j"))
+            w_grouped = keep.tile([P, D // 2, PACK], BF16, name="w_grouped%d" % g, tag="dz0" if g else "w_grouped0", align_bytes=64)
+            copy = nc.scalar.copy if g else nc.vector.tensor_copy
+            copy(w_grouped[:].rearrange("p (c i) j -> p c j i", i=4), w_raw[g][:].rearrange("p j (c i) -> p c j i", i=4))
             nc.vector.quantize_mx(w_codes[:, cols].bitcast(E4M3), w_scales[:, cols], w_grouped[:].rearrange("p d j -> p (d j)"))
 
         for t in range(PACK):
@@ -130,15 +133,20 @@ def tile_attend_gex_pl_tnh_x_kernel(tc, dyT, hT, ts, wm, offs, out_0, out_1, out
                     gather_dy(t - 1, s)
         interleave(0, 0, 2)
         gather_dy(2, 0)
-        last_factor(0, dz[1][:, 2, :])
-        quantize_w(0)
+        late_factor(last, 0, dz[1][:, 2, :])
         gather_dy_times(last, 0, dz[1][:, 2, :])
         interleave(0, 2, 2)
-        gather_dy_times(2, 1, factor[2][:, 1, :])
+        quantize_w(0)
+        interleave(1, 0, 2)
+        nc.vector.tensor_copy(dz[1][:, 2, :], dy_window[2][:].indirect(listed(1)))
         quantize_dz(0)
-        factor_b = keep.tile([P, HALF], F32, name="factor_b", tag="grouped0", align_bytes=64)
-        last_factor(1, factor_b[:])
-        gather_dy_times(last, 1, factor_b[:])
+        last_dy = keep.tile([P, HALF], F32, name="last_dy", tag="grouped0", align_bytes=64)
+        nc.vector.tensor_copy(last_dy[:], dy_window[last][:].indirect(listed(1)))
+        quantize_w(1)
+        late_factors = keep.tile([P, 2, HALF], F32, name="late_factors", tag="dz0", align_bytes=64)
+        for t, dy_listed in ((2, dz[1][:, 2, :]), (last, last_dy[:])):
+            nc.gpsimd.tensor_tensor(late_factors[:, t - 2, :], factor[t][:, 1, :], minus_ts_rows[:, 1, :], ALU.mult)
+            nc.gpsimd.tensor_tensor(dz[1][:, t, :], dy_listed, late_factors[:, t - 2, :], ALU.mult)
 
         def multiply_and_scatter(w, s, bank, slot=None):
             cols = slice(w * P, (w + 1) * P)
@@ -155,45 +163,51 @@ def tile_attend_gex_pl_tnh_x_kernel(tc, dyT, hT, ts, wm, offs, out_0, out_1, out
         out_scales = keep.tile([P, HALF], U8, name="out_scales", align_bytes=64)
         turn_banks = [banks[0], banks[1], banks[6], banks[7]]
 
-        def quantize_window(w):
-            regrouped = keep.tile([P, HALF * PACK], BF16, name="regrouped%d" % w, tag="regrouped%d" % (w % 2), align_bytes=64)
+        last_codes = keep.tile([P, HALF], U32, name="last_codes", align_bytes=64)
+
+        def quantize_columns(w, regrouped, codes, first, count):
+            cols = slice(first, first + count)
+            nc.vector.quantize_mx(codes[:, cols].bitcast(E4M3), out_scales[4 * w : P, cols], regrouped[:, PACK * first : PACK * (first + count)])
+
+        def regroup_window(w):
+            regrouped = keep.tile([P, HALF * PACK], BF16, name="regrouped%d" % w, align_bytes=64)
             for j in range(4):
                 for b in range(4):
                     first = b * HALF + j * P
                     nc.tensor.transpose(turn_banks[j][:, b * P : (b + 1) * P], windows[w][:, first : first + P], identity[:])
             for j in range(4):
                 rounded = keep.tile([P, HALF], BF16, name="rounded%d%d" % (w, j), tag="rounded%d" % j)
-                copy = nc.vector.tensor_copy if (w == 3 and j % 2 == 1) else nc.scalar.copy
+                copy = nc.vector.tensor_copy if (w == 3 and j % 2) else nc.scalar.copy
                 copy(rounded[:].rearrange("t (u q e) -> t u q e", u=2, e=2), turn_banks[j][:].rearrange("t (q u e) -> t u q e", u=2, e=2))
-                back = banks[2 + j // 2]
+                back = banks[2 + j][:, 0 : 2 * P]
                 for u in range(2):
-                    first = (j % 2) * 256 + u * P
-                    nc.tensor.transpose(back[:, first : first + P], rounded[:].bitcast(F32)[:, u * P : (u + 1) * P], identity[:])
-                if j % 2 == 1:
-                    copy = nc.vector.tensor_copy if (w == 3 and j == 3) else nc.scalar.copy
-                    target = regrouped[:].bitcast(F32)[:, (j // 2) * HALF : (j // 2 + 1) * HALF]
-                    copy(target.rearrange("q (j t u) -> q j t u", j=2, u=2), back[:].rearrange("q (j u t) -> q j t u", j=2, u=2))
-            codes = keep.tile([P, HALF], U32, name="codes%d" % w, align_bytes=64)
-            nc.vector.quantize_mx(codes[:].bitcast(E4M3), out_scales[4 * w : P, :], regrouped[:])
-            for b in range(4):
-                nc.sync.dma_start(words_out[w * QUAD : (w + 1) * QUAD, b * HALF : (b + 1) * HALF], codes[b * QUAD : (b + 1) * QUAD, :].bitcast(I32))
+                    nc.tensor.transpose(back[:, u * P : (u + 1) * P], rounded[:].bitcast(F32)[:, u * P : (u + 1) * P], identity[:])
+                copy = nc.vector.tensor_copy if (w, j) == (3, 3) else nc.scalar.copy
+                target = regrouped[:].bitcast(F32)[:, 2 * P * j : 2 * P * (j + 1)]
+                copy(target.rearrange("q (t u) -> q t u", u=2), back.rearrange("q (u t) -> q t u", u=2))
+                if w == 3:
+                    quantize_columns(w, regrouped, last_codes, j * P, P)
+            return regrouped
 
         multiply_and_scatter(0, 0, banks[4])
-        interleave(1, 0, PACK)
+        multiply_and_scatter(1, 0, banks[5])
+        interleave(1, 2, 2)
         quantize_dz(1)
-        quantize_w(1)
         zeroed_window("grouped1")
-        multiply_and_scatter(1, 0, banks[5], "dz1")
-        multiply_and_scatter(0, 1, banks[4])
-        zeroed_window("dx01")
-        multiply_and_scatter(1, 1, banks[5])
-        multiply_and_scatter(2, 0, banks[4])
+        multiply_and_scatter(2, 0, banks[4], "dz1")
+        multiply_and_scatter(0, 1, banks[5])
+        multiply_and_scatter(1, 1, banks[4])
         multiply_and_scatter(2, 1, banks[5])
-        quantize_window(0)
-        multiply_and_scatter(3, 0, banks[3])
-        quantize_window(1)
-        multiply_and_scatter(3, 1, banks[3])
-        quantize_window(2)
-        quantize_window(3)
+        multiply_and_scatter(3, 0, banks[4])
+        multiply_and_scatter(3, 1, banks[5])
+        words_by_window = words_out.rearrange("(w p) t -> p w t", p=QUAD)
+        early_codes = keep.tile([P, 3, HALF], U32, name="early_codes", align_bytes=64)
+        for w in range(3):
+            quantize_columns(w, regroup_window(w), early_codes[:, w, :], 0, HALF)
+        for b in range(4):
+            nc.sync.dma_start(words_by_window[:, 0:3, b * HALF : (b + 1) * HALF], early_codes[b * QUAD : (b + 1) * QUAD, :, :].bitcast(I32))
+        regroup_window(3)
+        for b in range(4):
+            nc.sync.dma_start(words_by_window[:, 3, b * HALF : (b + 1) * HALF], last_codes[b * QUAD : (b + 1) * QUAD, :].bitcast(I32))
         for b in range(4):
             nc.scalar.dma_start(scales_out[:, b * P : (b + 1) * P], out_scales[b * QUAD : b * QUAD + 16, :].bitcast(I32))

@@ -19,8 +19,15 @@ ACT = mybir.ActivationFunctionType
 
 P = 128
 PACK = 4
+LAST = PACK - 1
 HALF = 512
 QUAD = 32
+QUADS = P // QUAD
+RUN = T // QUADS
+BLOCKS = HALF // P
+STRIPE = 16
+TS_ROW = P - QUAD
+ALIGN = 64
 
 
 def tile_attend_gex_pl_tnh_x_kernel(tc, dyT, hT, ts, wm, offs, out_0, out_1, out_2):
@@ -29,185 +36,201 @@ def tile_attend_gex_pl_tnh_x_kernel(tc, dyT, hT, ts, wm, offs, out_0, out_1, out
         keep = ctx.enter_context(tc.tile_pool(name="keep", bufs=1))
         psum = ctx.enter_context(tc.psum_pool(name="psum", bufs=1))
 
-        offsets = keep.tile([P, N // 16], U16, name="offsets")
+        offsets = keep.tile([P, N // STRIPE], U16, name="offsets")
         nc.sync.dma_start(offsets[:], offs)
 
+        def entries(first, count):
+            return offsets[:, first // STRIPE : (first + count) // STRIPE]
+
         def listed(s):
-            return offsets[:, s * (HALF // 16) : (s + 1) * (HALF // 16)]
+            return entries(s * HALF, HALF)
 
         banks = [psum.tile([P, HALF], F32, name="bank%d" % i) for i in range(8)]
+        column_banks, spread_banks, product_banks = banks[0:2], banks[2:4], banks[4:6]
+        first_turn_banks, second_turn_banks = banks[0:2] + banks[6:8], banks[2:6]
 
         identity = keep.tile([P, P], F32, name="identity")
         make_identity(nc, identity[:])
 
         ts_window = keep.tile([P, T], F32, name="ts_window", tag="ts_window")
-        nc.sync.dma_start(ts_window[96:P, :], ts[96:P, :])
-        nc.gpsimd.memset(ts_window[0:96, :], 0.0)
+        nc.sync.dma_start(ts_window[TS_ROW:P, :], ts[TS_ROW:P, :])
+        nc.gpsimd.memset(ts_window[0:TS_ROW, :], 0.0)
 
         h_rows = hT.rearrange("(p j) c -> p j c", j=PACK)
         dy_rows = dyT.rearrange("(p j) c -> p j c", j=PACK)
-        h_window = [keep.tile([P, T], F32, name="h_window%d" % t, tag="h_window%d" % t) for t in range(PACK)]
-        dy_window = [keep.tile([P, T], F32, name="dy_window%d" % t, tag="dy_window%d" % t) for t in range(PACK)]
+        h_planes = [keep.tile([P, T], F32, name="h_plane%d" % t) for t in range(PACK)]
+        dy_planes = [keep.tile([P, T], F32, name="dy_plane%d" % t) for t in range(PACK)]
         w_rows = wm[0].rearrange("(p j) d -> p j d", j=PACK)
         w_raw = [keep.tile([P, PACK, D // 2], F32, name="w_raw%d" % g) for g in range(2)]
-        nc.sync.dma_start(h_window[0][:], h_rows[:, 0, :])
+        nc.sync.dma_start(h_planes[0][:], h_rows[:, 0, :])
         for t in range(1, PACK):
-            nc.sync.dma_start(h_window[t][:], h_rows[:, t, :])
-            nc.sync.dma_start(dy_window[t - 1][:], dy_rows[:, t - 1, :])
-        nc.sync.dma_start(dy_window[PACK - 1][:], dy_rows[:, PACK - 1, :])
+            nc.sync.dma_start(h_planes[t][:], h_rows[:, t, :])
+            nc.sync.dma_start(dy_planes[t - 1][:], dy_rows[:, t - 1, :])
+        nc.sync.dma_start(dy_planes[LAST][:], dy_rows[:, LAST, :])
         nc.sync.dma_start(w_raw[0][:], w_rows[:, :, 0 : D // 2])
         nc.sync.dma_start(w_raw[1][:], w_rows[:, :, D // 2 : D])
 
         windows = []
 
         def zeroed_window(slot):
-            window = keep.tile([P, T], F32, name="window%d" % len(windows), tag=slot, align_bytes=64)
+            window = keep.tile([P, T], F32, name="window%d" % len(windows), tag=slot, align_bytes=ALIGN)
             nc.gpsimd.memset(window[:], 0.0)
             windows.append(window)
 
         zeroed_window("window0")
         zeroed_window("window1")
-        zeroed_window("window2")
+        windows.append(keep.tile([P, T], F32, name="window2"))
+        nc.vector.memset(windows[2][:, 0 : T // 2 - 1], 0.0)
+        nc.vector.memset(windows[2][:, T // 2 - 1 : T], 0.0)
 
         ts_listed = keep.tile([P, N], F32, name="ts_listed")
         minus_ts_rows = keep.tile([P, 2, HALF], F32, name="minus_ts_rows")
-        minus_ts = keep.tile([P, N // P], F32, name="minus_ts", tag="minus_ts")
+        minus_ts_columns = keep.tile([P, N // P], F32, name="minus_ts_columns", tag="minus_ts_columns")
         for s in range(2):
             nc.vector.tensor_copy(ts_listed[:, s * HALF : (s + 1) * HALF], ts_window[:].indirect(listed(s)))
-            for c in range(4):
-                nc.tensor.transpose(banks[s][:, c * P : (c + 1) * P], ts_listed[:, s * HALF + c * P : s * HALF + (c + 1) * P], identity[:])
-            nc.scalar.activation(minus_ts[:, 4 * s : 4 * s + 4], banks[s][:, 96:HALF:P], ACT.Copy, scale=-1.0)
-            for c in range(4):
-                column = minus_ts[:, 4 * s + c : 4 * s + c + 1].to_broadcast([P, P])
-                nc.tensor.transpose(banks[2 + s][:, c * P : (c + 1) * P], column, identity[:])
-            nc.scalar.copy(minus_ts_rows[:, s, :], banks[2 + s][:])
+            for c in range(BLOCKS):
+                first = s * HALF + c * P
+                nc.tensor.transpose(column_banks[s][:, c * P : (c + 1) * P], ts_listed[:, first : first + P], identity[:])
+            columns = minus_ts_columns[:, BLOCKS * s : BLOCKS * (s + 1)]
+            nc.scalar.activation(columns, column_banks[s][:, TS_ROW:HALF:P], ACT.Copy, scale=-1.0)
+            for c in range(BLOCKS):
+                column = columns[:, c : c + 1].to_broadcast([P, P])
+                nc.tensor.transpose(spread_banks[s][:, c * P : (c + 1) * P], column, identity[:])
+            nc.scalar.copy(minus_ts_rows[:, s, :], spread_banks[s][:])
 
-        dz = [keep.tile([P, PACK, HALF], F32, name="dz%d" % s, tag="dz%d" % s, align_bytes=64) for s in range(2)]
+        dz_low = keep.tile([P, 2, N], F32, name="dz_low")
+        dz_high = [keep.tile([P, 2, HALF], F32, name="dz_high%d" % s, tag="dz_high%d" % s, align_bytes=ALIGN) for s in range(2)]
         h_listed = keep.tile([P, 2, 2, HALF], F32, name="h_listed", tag="ts_window")
-        factors = keep.tile([P, PACK, 2, HALF], F32, name="factors", tag="minus_ts")
-        factor = [factors[:, t, :, :] for t in range(PACK)]
-        grouped = [keep.tile([P, HALF, PACK], BF16, name="grouped%d" % s, tag="grouped%d" % s, align_bytes=64) for s in range(2)]
-        dz_codes = [keep.tile([P, HALF], U32, name="dz_codes%d" % s, align_bytes=64) for s in range(2)]
-        dz_scales = [keep.tile([P, HALF], U8, name="dz_scales%d" % s, align_bytes=64) for s in range(2)]
-        w_codes = keep.tile([P, D], U32, name="w_codes", align_bytes=64)
-        w_scales = keep.tile([P, D], U8, name="w_scales", align_bytes=64)
-        last = PACK - 1
+        factors = keep.tile([P, PACK, 2, HALF], F32, name="factors", tag="minus_ts_columns")
+        grouped = [keep.tile([P, HALF, PACK], BF16, name="grouped%d" % s, tag="grouped%d" % s, align_bytes=ALIGN) for s in range(2)]
+        dz_codes = [keep.tile([P, HALF], U32, name="dz_codes%d" % s, align_bytes=ALIGN) for s in range(2)]
+        dz_scales = [keep.tile([P, HALF], U8, name="dz_scales%d" % s, align_bytes=ALIGN) for s in range(2)]
+        w_codes = keep.tile([P, D], U32, name="w_codes", align_bytes=ALIGN)
+        w_scales = keep.tile([P, D], U8, name="w_scales", align_bytes=ALIGN)
 
         def gather_h(t, s):
-            f = factor[t][:, s, :]
-            nc.vector.tensor_copy(h_listed[:, t % 2, s, :], h_window[t][:].indirect(listed(s)))
-            nc.scalar.activation(f, h_listed[:, t % 2, s, :], ACT.Square)
-            if (t, s) != (last, 0):
-                nc.scalar.activation(f, f, ACT.Identity, bias=-1.0)
-            if t + s < last:
-                nc.gpsimd.tensor_tensor(f, f, minus_ts_rows[:, s, :], ALU.mult)
+            factor = factors[:, t, s, :]
+            nc.vector.tensor_copy(h_listed[:, t % 2, s, :], h_planes[t][:].indirect(listed(s)))
+            nc.scalar.activation(factor, h_listed[:, t % 2, s, :], ACT.Square)
+            if (t, s) != (LAST, 0):
+                nc.scalar.activation(factor, factor, ACT.Identity, bias=-1.0)
+            if t + s < LAST:
+                nc.gpsimd.tensor_tensor(factor, factor, minus_ts_rows[:, s, :], ALU.mult)
 
-        def gather_dy(t, s):
-            nc.vector.tensor_copy(dz[s][:, t, :], dy_window[t][:].indirect(listed(s)))
-            nc.gpsimd.tensor_tensor(dz[s][:, t, :], dz[s][:, t, :], factor[t][:, s, :], ALU.mult)
+        def gather_dy(target, t, offsets_part, factor):
+            nc.vector.tensor_copy(target, dy_planes[t][:].indirect(offsets_part))
+            nc.gpsimd.tensor_tensor(target, target, factor, ALU.mult)
 
-        def gather_dy_times(t, s, f):
-            nc.vector.tensor_tensor(dz[s][:, t, :], dy_window[t][:].indirect(listed(s)), f, ALU.mult)
-
-        def late_factor(t, s, f):
-            nc.vector.scalar_tensor_tensor(f, factor[t][:, s, :], 1.0, banks[2 + s][:], ALU.subtract, ALU.mult)
-
-        def interleave(s, first, count):
-            nc.scalar.copy(grouped[s][:, :, first : first + count], dz[s][:, first : first + count, :].rearrange("p e c -> p c e"))
+        def interleave(s, first, pair):
+            nc.scalar.copy(grouped[s][:, :, first : first + 2], pair.rearrange("p e c -> p c e"))
 
         def quantize_dz(s):
             nc.vector.quantize_mx(dz_codes[s][:].bitcast(E5M2), dz_scales[s][:], grouped[s][:].rearrange("p c j -> p (c j)"))
 
-        def quantize_w(g):
+        def quantize_w(g, copy, slot):
             cols = slice(g * D // 2, (g + 1) * D // 2)
-            w_grouped = keep.tile([P, D // 2, PACK], BF16, name="w_grouped%d" % g, tag="dz0" if g else "w_grouped0", align_bytes=64)
-            copy = nc.scalar.copy if g else nc.vector.tensor_copy
+            w_grouped = keep.tile([P, D // 2, PACK], BF16, name="w_grouped%d" % g, tag=slot, align_bytes=ALIGN)
             copy(w_grouped[:].rearrange("p (c i) j -> p c j i", i=4), w_raw[g][:].rearrange("p j (c i) -> p c j i", i=4))
             nc.vector.quantize_mx(w_codes[:, cols].bitcast(E4M3), w_scales[:, cols], w_grouped[:].rearrange("p d j -> p (d j)"))
 
-        for t in range(PACK):
+        for t in range(2):
             for s in range(2):
                 gather_h(t, s)
-            for s in range(2):
-                if 0 < t < last:
-                    gather_dy(t - 1, s)
-        interleave(0, 0, 2)
-        gather_dy(2, 0)
-        late_factor(last, 0, dz[1][:, 2, :])
-        gather_dy_times(last, 0, dz[1][:, 2, :])
-        interleave(0, 2, 2)
-        quantize_w(0)
-        interleave(1, 0, 2)
-        nc.vector.tensor_copy(dz[1][:, 2, :], dy_window[2][:].indirect(listed(1)))
-        quantize_dz(0)
-        last_dy = keep.tile([P, HALF], F32, name="last_dy", tag="grouped0", align_bytes=64)
-        nc.vector.tensor_copy(last_dy[:], dy_window[last][:].indirect(listed(1)))
-        quantize_w(1)
-        late_factors = keep.tile([P, 2, HALF], F32, name="late_factors", tag="dz0", align_bytes=64)
-        for t, dy_listed in ((2, dz[1][:, 2, :]), (last, last_dy[:])):
-            nc.gpsimd.tensor_tensor(late_factors[:, t - 2, :], factor[t][:, 1, :], minus_ts_rows[:, 1, :], ALU.mult)
-            nc.gpsimd.tensor_tensor(dz[1][:, t, :], dy_listed, late_factors[:, t - 2, :], ALU.mult)
+        gather_dy(dz_low[:, 0, :], 0, offsets[:], factors[:, 0, :, :].rearrange("p s c -> p (s c)"))
+        for s in range(2):
+            gather_h(2, s)
+        for s in range(2):
+            gather_dy(dz_low[:, 1, s * HALF : (s + 1) * HALF], 1, listed(s), factors[:, 1, s, :])
+        for s in range(2):
+            gather_h(LAST, s)
+        for s in range(2):
+            interleave(s, 0, dz_low[:, :, s * HALF : (s + 1) * HALF])
+        gather_dy(dz_high[0][:, 0, :], 2, listed(0), factors[:, 2, 0, :])
 
-        def multiply_and_scatter(w, s, bank, slot=None):
+        last_factor = dz_high[1][:, 0, :]
+        nc.vector.scalar_tensor_tensor(last_factor, factors[:, LAST, 0, :], 1.0, spread_banks[0][:], ALU.subtract, ALU.mult)
+        nc.vector.tensor_tensor(dz_high[0][:, 1, :], dy_planes[LAST][:].indirect(listed(0)), last_factor, ALU.mult)
+        interleave(0, 2, dz_high[0][:])
+        quantize_w(0, nc.vector.tensor_copy, "w_grouped0")
+        nc.vector.tensor_copy(dz_high[1][:, 0, :], dy_planes[2][:].indirect(listed(1)))
+        quantize_dz(0)
+        last_dy = keep.tile([P, HALF], F32, name="last_dy", tag="grouped0", align_bytes=ALIGN)
+        nc.vector.tensor_copy(last_dy[:], dy_planes[LAST][:].indirect(listed(1)))
+        quantize_w(1, nc.scalar.copy, "dz_high0")
+        late_factors = keep.tile([P, 2, HALF], F32, name="late_factors", tag="dz_high0", align_bytes=ALIGN)
+        minus_ts_twice = minus_ts_rows[:, 1:2, :].to_broadcast([P, 2, HALF])
+        nc.gpsimd.tensor_tensor(late_factors[:], factors[:, 2:PACK, 1, :], minus_ts_twice, ALU.mult)
+        for e, dy_listed in enumerate((dz_high[1][:, 0, :], last_dy[:])):
+            nc.gpsimd.tensor_tensor(dz_high[1][:, e, :], dy_listed, late_factors[:, e, :], ALU.mult)
+
+        def multiply(w, s, bank):
             cols = slice(w * P, (w + 1) * P)
             nc.tensor.matmul_mx(bank[:], lhsT=w_codes[:, cols].bitcast(E4M3), lhsT_scale=w_scales[:, cols],
                                 rhs=dz_codes[s][:].bitcast(E5M2), rhs_scale=dz_scales[s][:], start=True, stop=True)
-            dx = keep.tile([P, HALF], F32, name="dx%d%d" % (w, s), tag=slot or "dx%d%d" % (w, s), align_bytes=64)
-            nc.scalar.copy(dx[:], bank[:])
-            nc.vector.tensor_copy(windows[w][:].indirect(listed(s)), dx[:])
+
+        def scatter(w, s, bank, first, count, slot=None):
+            name = "dx%d_%d" % (w, s * HALF + first)
+            dx = keep.tile([P, count], F32, name=name, tag=slot or name, align_bytes=ALIGN)
+            nc.scalar.copy(dx[:], bank[:, first : first + count])
+            nc.vector.tensor_copy(windows[w][:].indirect(entries(s * HALF + first, count)), dx[:])
+
+        def multiply_and_scatter(w, s, bank):
+            multiply(w, s, bank)
+            scatter(w, s, bank, 0, HALF)
             if s == 1:
-                nc.sync.dma_start(out_0[cols, :], windows[w][:])
+                nc.sync.dma_start(out_0[w * P : (w + 1) * P, :], windows[w][:])
 
         words_out = out_1[0].rearrange("p t l -> p (t l)").bitcast(I32)
         scales_out = out_2[0].bitcast(I32)
-        out_scales = keep.tile([P, HALF], U8, name="out_scales", align_bytes=64)
-        turn_banks = [banks[0], banks[1], banks[6], banks[7]]
-
-        last_codes = keep.tile([P, HALF], U32, name="last_codes", align_bytes=64)
+        out_scales = keep.tile([P, RUN], U8, name="out_scales", align_bytes=ALIGN)
+        last_codes = keep.tile([P, RUN], U32, name="last_codes", align_bytes=ALIGN)
 
         def quantize_columns(w, regrouped, codes, first, count):
             cols = slice(first, first + count)
-            nc.vector.quantize_mx(codes[:, cols].bitcast(E4M3), out_scales[4 * w : P, cols], regrouped[:, PACK * first : PACK * (first + count)])
+            nc.vector.quantize_mx(codes[:, cols].bitcast(E4M3), out_scales[PACK * w : P, cols], regrouped[:, PACK * first : PACK * (first + count)])
 
         def regroup_window(w):
-            regrouped = keep.tile([P, HALF * PACK], BF16, name="regrouped%d" % w, align_bytes=64)
-            for j in range(4):
-                for b in range(4):
-                    first = b * HALF + j * P
-                    nc.tensor.transpose(turn_banks[j][:, b * P : (b + 1) * P], windows[w][:, first : first + P], identity[:])
-            for j in range(4):
+            regrouped = keep.tile([P, RUN * PACK], BF16, name="regrouped%d" % w, align_bytes=ALIGN)
+            for j in range(BLOCKS):
+                for b in range(QUADS):
+                    first = b * RUN + j * P
+                    nc.tensor.transpose(first_turn_banks[j][:, b * P : (b + 1) * P], windows[w][:, first : first + P], identity[:])
+            for j in range(BLOCKS):
                 rounded = keep.tile([P, HALF], BF16, name="rounded%d%d" % (w, j), tag="rounded%d" % j)
-                copy = nc.vector.tensor_copy if (w == 3 and j % 2) else nc.scalar.copy
-                copy(rounded[:].rearrange("t (u q e) -> t u q e", u=2, e=2), turn_banks[j][:].rearrange("t (q u e) -> t u q e", u=2, e=2))
-                back = banks[2 + j][:, 0 : 2 * P]
+                round_copy = nc.vector.tensor_copy if (w == LAST and j % 2) else nc.scalar.copy
+                round_copy(rounded[:].rearrange("t (u q e) -> t u q e", u=2, e=2), first_turn_banks[j][:].rearrange("t (q u e) -> t u q e", u=2, e=2))
+                pairs = second_turn_banks[j][:, 0 : 2 * P]
                 for u in range(2):
-                    nc.tensor.transpose(back[:, u * P : (u + 1) * P], rounded[:].bitcast(F32)[:, u * P : (u + 1) * P], identity[:])
-                copy = nc.vector.tensor_copy if (w, j) == (3, 3) else nc.scalar.copy
+                    nc.tensor.transpose(pairs[:, u * P : (u + 1) * P], rounded[:].bitcast(F32)[:, u * P : (u + 1) * P], identity[:])
+                join_copy = nc.vector.tensor_copy if (w, j) == (LAST, BLOCKS - 1) else nc.scalar.copy
                 target = regrouped[:].bitcast(F32)[:, 2 * P * j : 2 * P * (j + 1)]
-                copy(target.rearrange("q (t u) -> q t u", u=2), back.rearrange("q (u t) -> q t u", u=2))
-                if w == 3:
+                join_copy(target.rearrange("q (t u) -> q t u", u=2), pairs.rearrange("q (u t) -> q t u", u=2))
+                if w == LAST:
                     quantize_columns(w, regrouped, last_codes, j * P, P)
             return regrouped
 
-        multiply_and_scatter(0, 0, banks[4])
-        multiply_and_scatter(1, 0, banks[5])
-        interleave(1, 2, 2)
+        multiply_and_scatter(0, 0, product_banks[0])
+        multiply_and_scatter(1, 0, product_banks[1])
+        multiply(2, 0, product_banks[0])
+        scatter(2, 0, product_banks[0], 0, HALF // 2)
+        interleave(1, 2, dz_high[1][:])
         quantize_dz(1)
         zeroed_window("grouped1")
-        multiply_and_scatter(2, 0, banks[4], "dz1")
-        multiply_and_scatter(0, 1, banks[5])
-        multiply_and_scatter(1, 1, banks[4])
-        multiply_and_scatter(2, 1, banks[5])
-        multiply_and_scatter(3, 0, banks[4])
-        multiply_and_scatter(3, 1, banks[5])
-        words_by_window = words_out.rearrange("(w p) t -> p w t", p=QUAD)
-        early_codes = keep.tile([P, 3, HALF], U32, name="early_codes", align_bytes=64)
-        for w in range(3):
-            quantize_columns(w, regroup_window(w), early_codes[:, w, :], 0, HALF)
-        for b in range(4):
-            nc.sync.dma_start(words_by_window[:, 0:3, b * HALF : (b + 1) * HALF], early_codes[b * QUAD : (b + 1) * QUAD, :, :].bitcast(I32))
-        regroup_window(3)
-        for b in range(4):
-            nc.sync.dma_start(words_by_window[:, 3, b * HALF : (b + 1) * HALF], last_codes[b * QUAD : (b + 1) * QUAD, :].bitcast(I32))
-        for b in range(4):
-            nc.scalar.dma_start(scales_out[:, b * P : (b + 1) * P], out_scales[b * QUAD : b * QUAD + 16, :].bitcast(I32))
+        scatter(2, 0, product_banks[0], HALF // 2, HALF // 2, "dz_high1")
+        for w in range(LAST):
+            multiply_and_scatter(w, 1, product_banks[(w + 1) % 2])
+        for s in range(2):
+            multiply_and_scatter(LAST, s, product_banks[s])
+
+        words_by_window = words_out.rearrange("(w r) t -> r w t", r=QUAD)
+        early_codes = keep.tile([P, LAST, RUN], U32, name="early_codes", align_bytes=ALIGN)
+        for w in range(LAST):
+            quantize_columns(w, regroup_window(w), early_codes[:, w, :], 0, RUN)
+        for b in range(QUADS):
+            nc.sync.dma_start(words_by_window[:, 0:LAST, b * RUN : (b + 1) * RUN], early_codes[b * QUAD : (b + 1) * QUAD, :, :].bitcast(I32))
+        regroup_window(LAST)
+        for b in range(QUADS):
+            nc.sync.dma_start(words_by_window[:, LAST, b * RUN : (b + 1) * RUN], last_codes[b * QUAD : (b + 1) * QUAD, :].bitcast(I32))
+        scale_rows, scale_words = D // QUAD, RUN // 4
+        for b in range(QUADS):
+            nc.scalar.dma_start(scales_out[:, b * scale_words : (b + 1) * scale_words], out_scales[b * QUAD : b * QUAD + scale_rows, :].bitcast(I32))

@@ -26,7 +26,8 @@ QUADS = P // QUAD
 RUN = T // QUADS
 BLOCKS = HALF // P
 STRIPE = 16
-TS_ROW = P - QUAD
+TS_ROW = P - 1
+PLAIN = 2
 ALIGN = 64
 
 
@@ -62,12 +63,12 @@ def tile_attend_gex_pl_tnh_x_kernel(tc, dyT, hT, ts, wm, offs, out_0, out_1, out
         dy_planes = [keep.tile([P, T], F32, name="dy_plane%d" % t) for t in range(PACK)]
         w_rows = wm[0].rearrange("(p j) d -> p j d", j=PACK)
         w_raw = [keep.tile([P, PACK, D // 2], F32, name="w_raw%d" % g) for g in range(2)]
-        nc.sync.dma_start(h_planes[0][:], h_rows[:, 0, :])
-        for t in range(1, PACK):
+        for t in range(PACK):
             nc.sync.dma_start(h_planes[t][:], h_rows[:, t, :])
-            nc.sync.dma_start(dy_planes[t - 1][:], dy_rows[:, t - 1, :])
-        nc.sync.dma_start(dy_planes[LAST][:], dy_rows[:, LAST, :])
+        for t in range(LAST):
+            nc.sync.dma_start(dy_planes[t][:], dy_rows[:, t, :])
         nc.sync.dma_start(w_raw[0][:], w_rows[:, :, 0 : D // 2])
+        nc.sync.dma_start(dy_planes[LAST][:], dy_rows[:, LAST, :])
         nc.sync.dma_start(w_raw[1][:], w_rows[:, :, D // 2 : D])
 
         windows = []
@@ -84,84 +85,77 @@ def tile_attend_gex_pl_tnh_x_kernel(tc, dyT, hT, ts, wm, offs, out_0, out_1, out
         nc.vector.memset(windows[2][:, T // 2 - 1 : T], 0.0)
 
         ts_listed = keep.tile([P, N], F32, name="ts_listed")
-        minus_ts_rows = keep.tile([P, 2, HALF], F32, name="minus_ts_rows")
-        minus_ts_columns = keep.tile([P, N // P], F32, name="minus_ts_columns", tag="minus_ts_columns")
+        ts_rows = keep.tile([P, 2, HALF], F32, name="ts_rows")
+        ts_columns = keep.tile([P, N // P], F32, name="ts_columns", tag="ts_columns")
         for s in range(2):
             nc.vector.tensor_copy(ts_listed[:, s * HALF : (s + 1) * HALF], ts_window[:].indirect(listed(s)))
             for c in range(BLOCKS):
                 first = s * HALF + c * P
                 nc.tensor.transpose(column_banks[s][:, c * P : (c + 1) * P], ts_listed[:, first : first + P], identity[:])
-            columns = minus_ts_columns[:, BLOCKS * s : BLOCKS * (s + 1)]
-            nc.scalar.activation(columns, column_banks[s][:, TS_ROW:HALF:P], ACT.Copy, scale=-1.0)
+            columns = ts_columns[:, BLOCKS * s : BLOCKS * (s + 1)]
+            nc.scalar.copy(columns, column_banks[s][:, TS_ROW:HALF:P])
             for c in range(BLOCKS):
                 column = columns[:, c : c + 1].to_broadcast([P, P])
                 nc.tensor.transpose(spread_banks[s][:, c * P : (c + 1) * P], column, identity[:])
-            nc.scalar.copy(minus_ts_rows[:, s, :], spread_banks[s][:])
+            nc.scalar.copy(ts_rows[:, s, :], spread_banks[s][:])
 
-        dz_low = keep.tile([P, 2, N], F32, name="dz_low")
-        dz_high = [keep.tile([P, 2, HALF], F32, name="dz_high%d" % s, tag="dz_high%d" % s, align_bytes=ALIGN) for s in range(2)]
+        dz = [keep.tile([P, PACK * HALF], F32, name="dz%d" % s, tag="dz%d" % s, align_bytes=ALIGN) for s in range(2)]
+        dy_listed = keep.tile([P, PLAIN * HALF], F32, name="dy_listed")
         h_listed = keep.tile([P, 2, 2, HALF], F32, name="h_listed", tag="ts_window")
-        factors = keep.tile([P, PACK, 2, HALF], F32, name="factors", tag="minus_ts_columns")
+        all_factors = keep.tile([P, 2 * PACK * HALF], F32, name="all_factors", tag="ts_columns")
+        factors = [all_factors[:, s * PACK * HALF : (s + 1) * PACK * HALF] for s in range(2)]
         grouped = [keep.tile([P, HALF, PACK], BF16, name="grouped%d" % s, tag="grouped%d" % s, align_bytes=ALIGN) for s in range(2)]
         dz_codes = [keep.tile([P, HALF], U32, name="dz_codes%d" % s, align_bytes=ALIGN) for s in range(2)]
         dz_scales = [keep.tile([P, HALF], U8, name="dz_scales%d" % s, align_bytes=ALIGN) for s in range(2)]
         w_codes = keep.tile([P, D], U32, name="w_codes", align_bytes=ALIGN)
         w_scales = keep.tile([P, D], U8, name="w_scales", align_bytes=ALIGN)
 
-        def gather_h(t, s):
-            factor = factors[:, t, s, :]
+        def planes(tile, first, count=1):
+            return tile[:, first * HALF : (first + count) * HALF]
+
+        def gather_factor(t, s):
+            factor = planes(factors[s], t)
             nc.vector.tensor_copy(h_listed[:, t % 2, s, :], h_planes[t][:].indirect(listed(s)))
             nc.scalar.activation(factor, h_listed[:, t % 2, s, :], ACT.Square)
-            if (t, s) != (LAST, 0):
-                nc.scalar.activation(factor, factor, ACT.Identity, bias=-1.0)
-            if t + s < LAST:
-                nc.gpsimd.tensor_tensor(factor, factor, minus_ts_rows[:, s, :], ALU.mult)
+            nc.scalar.activation(factor, factor, ACT.Identity, scale=-1.0, bias=1.0)
+            nc.gpsimd.tensor_tensor(factor, factor, ts_rows[:, s, :], ALU.mult)
 
-        def gather_dy(target, t, offsets_part, factor):
-            nc.vector.tensor_copy(target, dy_planes[t][:].indirect(offsets_part))
-            nc.gpsimd.tensor_tensor(target, target, factor, ALU.mult)
+        def gather_dz(t, s, first=0, count=HALF):
+            cols = slice(t * HALF + first, t * HALF + first + count)
+            nc.vector.tensor_tensor(dz[s][:, cols], dy_planes[t][:].indirect(entries(s * HALF + first, count)), factors[s][:, cols], ALU.mult)
 
-        def interleave(s, first, pair):
-            nc.scalar.copy(grouped[s][:, :, first : first + 2], pair.rearrange("p e c -> p c e"))
+        def interleave_pair(t, first=0, count=HALF):
+            pair = planes(dz[0], t, 2).rearrange("p (e c) -> p c e", e=2)
+            nc.scalar.copy(grouped[0][:, first : first + count, t : t + 2], pair[:, first : first + count, :])
 
         def quantize_dz(s):
             nc.vector.quantize_mx(dz_codes[s][:].bitcast(E5M2), dz_scales[s][:], grouped[s][:].rearrange("p c j -> p (c j)"))
 
-        def quantize_w(g, copy, slot):
+        def quantize_w(g, w_grouped):
             cols = slice(g * D // 2, (g + 1) * D // 2)
-            w_grouped = keep.tile([P, D // 2, PACK], BF16, name="w_grouped%d" % g, tag=slot, align_bytes=ALIGN)
-            copy(w_grouped[:].rearrange("p (c i) j -> p c j i", i=4), w_raw[g][:].rearrange("p j (c i) -> p c j i", i=4))
-            nc.vector.quantize_mx(w_codes[:, cols].bitcast(E4M3), w_scales[:, cols], w_grouped[:].rearrange("p d j -> p (d j)"))
+            nc.scalar.copy(w_grouped.rearrange("p (c i j) -> p c j i", i=4, j=PACK), w_raw[g][:].rearrange("p j (c i) -> p c j i", i=4))
+            nc.vector.quantize_mx(w_codes[:, cols].bitcast(E4M3), w_scales[:, cols], w_grouped)
 
-        for t in range(2):
+        for t in range(PACK):
             for s in range(2):
-                gather_h(t, s)
-        gather_dy(dz_low[:, 0, :], 0, offsets[:], factors[:, 0, :, :].rearrange("p s c -> p (s c)"))
-        for s in range(2):
-            gather_h(2, s)
-        for s in range(2):
-            gather_dy(dz_low[:, 1, s * HALF : (s + 1) * HALF], 1, listed(s), factors[:, 1, s, :])
-        for s in range(2):
-            gather_h(LAST, s)
-        for s in range(2):
-            interleave(s, 0, dz_low[:, :, s * HALF : (s + 1) * HALF])
-        gather_dy(dz_high[0][:, 0, :], 2, listed(0), factors[:, 2, 0, :])
-
-        last_factor = dz_high[1][:, 0, :]
-        nc.vector.scalar_tensor_tensor(last_factor, factors[:, LAST, 0, :], 1.0, spread_banks[0][:], ALU.subtract, ALU.mult)
-        nc.vector.tensor_tensor(dz_high[0][:, 1, :], dy_planes[LAST][:].indirect(listed(0)), last_factor, ALU.mult)
-        interleave(0, 2, dz_high[0][:])
-        quantize_w(0, nc.vector.tensor_copy, "w_grouped0")
-        nc.vector.tensor_copy(dz_high[1][:, 0, :], dy_planes[2][:].indirect(listed(1)))
+                gather_factor(t, s)
+        for t in range(LAST):
+            if t < PLAIN:
+                nc.vector.tensor_copy(planes(dy_listed, t), dy_planes[t][:].indirect(listed(1)))
+            gather_dz(t, 0)
+            if t >= PLAIN:
+                gather_dz(t, 1)
+            if t == 1:
+                interleave_pair(0)
+        w_grouped = keep.tile([P, PACK * D // 2], BF16, name="w_grouped", align_bytes=ALIGN)
+        quantize_w(0, w_grouped[:])
+        for first in (0, HALF // 2):
+            gather_dz(LAST, 0, first, HALF // 2)
+            interleave_pair(2, first, HALF // 2)
+        gather_dz(LAST, 1)
         quantize_dz(0)
-        last_dy = keep.tile([P, HALF], F32, name="last_dy", tag="grouped0", align_bytes=ALIGN)
-        nc.vector.tensor_copy(last_dy[:], dy_planes[LAST][:].indirect(listed(1)))
-        quantize_w(1, nc.scalar.copy, "dz_high0")
-        late_factors = keep.tile([P, 2, HALF], F32, name="late_factors", tag="dz_high0", align_bytes=ALIGN)
-        minus_ts_twice = minus_ts_rows[:, 1:2, :].to_broadcast([P, 2, HALF])
-        nc.gpsimd.tensor_tensor(late_factors[:], factors[:, 2:PACK, 1, :], minus_ts_twice, ALU.mult)
-        for e, dy_listed in enumerate((dz_high[1][:, 0, :], last_dy[:])):
-            nc.gpsimd.tensor_tensor(dz_high[1][:, e, :], dy_listed, late_factors[:, e, :], ALU.mult)
+        quantize_w(1, planes(dz[1], 0).bitcast(BF16))
+        nc.gpsimd.tensor_tensor(planes(dz[1], 0, PLAIN), dy_listed[:], planes(factors[1], 0, PLAIN), ALU.mult)
 
         def multiply(w, s, bank):
             cols = slice(w * P, (w + 1) * P)
@@ -211,16 +205,19 @@ def tile_attend_gex_pl_tnh_x_kernel(tc, dyT, hT, ts, wm, offs, out_0, out_1, out
 
         multiply_and_scatter(0, 0, product_banks[0])
         multiply_and_scatter(1, 0, product_banks[1])
-        multiply(2, 0, product_banks[0])
-        scatter(2, 0, product_banks[0], 0, HALF // 2)
-        interleave(1, 2, dz_high[1][:])
+        nc.scalar.copy(grouped[1][:].rearrange("p (c i) t -> p c t i", i=4), dz[1][:].rearrange("p (t c i) -> p c t i", t=PACK, i=4))
         quantize_dz(1)
         zeroed_window("grouped1")
-        scatter(2, 0, product_banks[0], HALF // 2, HALF // 2, "dz_high1")
+        multiply(2, 0, product_banks[0])
+        scatter(2, 0, product_banks[0], 0, HALF, "dz1")
         for w in range(LAST):
             multiply_and_scatter(w, 1, product_banks[(w + 1) % 2])
+        dx_last = keep.tile([P, N], F32, name="dx_last")
         for s in range(2):
-            multiply_and_scatter(LAST, s, product_banks[s])
+            multiply(LAST, s, product_banks[s])
+            nc.scalar.copy(dx_last[:, s * HALF : (s + 1) * HALF], product_banks[s][:])
+        nc.vector.tensor_copy(windows[LAST][:].indirect(offsets[:]), dx_last[:])
+        nc.sync.dma_start(out_0[LAST * P : D, :], windows[LAST][:])
 
         words_by_window = words_out.rearrange("(w r) t -> r w t", r=QUAD)
         early_codes = keep.tile([P, LAST, RUN], U32, name="early_codes", align_bytes=ALIGN)

@@ -27,7 +27,6 @@ RUN = T // QUADS
 BLOCKS = HALF // P
 STRIPE = 16
 TS_ROW = P - 1
-PLAIN = 2
 ALIGN = 64
 
 
@@ -84,9 +83,9 @@ def tile_attend_gex_pl_tnh_x_kernel(tc, dyT, hT, ts, wm, offs, out_0, out_1, out
         nc.vector.memset(windows[2][:, 0 : T // 2 - 1], 0.0)
         nc.vector.memset(windows[2][:, T // 2 - 1 : T], 0.0)
 
-        ts_listed = keep.tile([P, N], F32, name="ts_listed")
+        ts_listed = keep.tile([P, N], F32, name="ts_listed", tag="ts_listed")
         ts_rows = keep.tile([P, 2, HALF], F32, name="ts_rows")
-        ts_columns = keep.tile([P, N // P], F32, name="ts_columns", tag="ts_columns")
+        ts_columns = keep.tile([P, N // P], F32, name="ts_columns")
         for s in range(2):
             nc.vector.tensor_copy(ts_listed[:, s * HALF : (s + 1) * HALF], ts_window[:].indirect(listed(s)))
             for c in range(BLOCKS):
@@ -99,34 +98,32 @@ def tile_attend_gex_pl_tnh_x_kernel(tc, dyT, hT, ts, wm, offs, out_0, out_1, out
                 nc.tensor.transpose(spread_banks[s][:, c * P : (c + 1) * P], column, identity[:])
             nc.scalar.copy(ts_rows[:, s, :], spread_banks[s][:])
 
-        dz = [keep.tile([P, PACK * HALF], F32, name="dz%d" % s, tag="dz%d" % s, align_bytes=ALIGN) for s in range(2)]
-        dy_listed = keep.tile([P, PLAIN * HALF], F32, name="dy_listed")
-        h_listed = keep.tile([P, 2, 2, HALF], F32, name="h_listed", tag="ts_window")
-        all_factors = keep.tile([P, 2 * PACK * HALF], F32, name="all_factors", tag="ts_columns")
-        factors = [all_factors[:, s * PACK * HALF : (s + 1) * PACK * HALF] for s in range(2)]
+        def planes(tile, first, count=1):
+            return tile[:, first * HALF : (first + count) * HALF]
+
+        h_listed = keep.tile([P, 2 * PACK * HALF], F32, name="h_listed", tag="ts_window")
+        all_factors = keep.tile([P, 2 * PACK * HALF], F32, name="all_factors", tag="ts_listed")
+        factors = [planes(all_factors, s * PACK, PACK) for s in range(2)]
+        dz_first = keep.tile([P, PACK * HALF], F32, name="dz_first")
+        late = keep.tile([P, LAST * HALF], F32, name="late", align_bytes=ALIGN)
+        dy_listed = keep.tile([P, LAST * HALF], F32, name="dy_listed")
         grouped = [keep.tile([P, HALF, PACK], BF16, name="grouped%d" % s, tag="grouped%d" % s, align_bytes=ALIGN) for s in range(2)]
         dz_codes = [keep.tile([P, HALF], U32, name="dz_codes%d" % s, align_bytes=ALIGN) for s in range(2)]
         dz_scales = [keep.tile([P, HALF], U8, name="dz_scales%d" % s, align_bytes=ALIGN) for s in range(2)]
         w_codes = keep.tile([P, D], U32, name="w_codes", align_bytes=ALIGN)
         w_scales = keep.tile([P, D], U8, name="w_scales", align_bytes=ALIGN)
 
-        def planes(tile, first, count=1):
-            return tile[:, first * HALF : (first + count) * HALF]
+        def gather_slope(t, s, slope):
+            listed_h = planes(h_listed, 2 * t + s)
+            nc.vector.tensor_copy(listed_h, h_planes[t][:].indirect(listed(s)))
+            nc.scalar.activation(slope, listed_h, ACT.Square)
+            nc.scalar.activation(slope, slope, ACT.Identity, scale=-1.0, bias=1.0)
 
-        def gather_factor(t, s):
-            factor = planes(factors[s], t)
-            nc.vector.tensor_copy(h_listed[:, t % 2, s, :], h_planes[t][:].indirect(listed(s)))
-            nc.scalar.activation(factor, h_listed[:, t % 2, s, :], ACT.Square)
-            nc.scalar.activation(factor, factor, ACT.Identity, scale=-1.0, bias=1.0)
-            nc.gpsimd.tensor_tensor(factor, factor, ts_rows[:, s, :], ALU.mult)
+        def gather_times(target, t, offsets_part, factor):
+            nc.vector.tensor_tensor(target, dy_planes[t][:].indirect(offsets_part), factor, ALU.mult)
 
-        def gather_dz(t, s, first=0, count=HALF):
-            cols = slice(t * HALF + first, t * HALF + first + count)
-            nc.vector.tensor_tensor(dz[s][:, cols], dy_planes[t][:].indirect(entries(s * HALF + first, count)), factors[s][:, cols], ALU.mult)
-
-        def interleave_pair(t, first=0, count=HALF):
-            pair = planes(dz[0], t, 2).rearrange("p (e c) -> p c e", e=2)
-            nc.scalar.copy(grouped[0][:, first : first + count, t : t + 2], pair[:, first : first + count, :])
+        def interleave(s, t, pair, first=0, count=HALF):
+            nc.scalar.copy(grouped[s][:, first : first + count, t : t + 2], pair.rearrange("p (e c) -> p c e", e=2)[:, first : first + count, :])
 
         def quantize_dz(s):
             nc.vector.quantize_mx(dz_codes[s][:].bitcast(E5M2), dz_scales[s][:], grouped[s][:].rearrange("p c j -> p (c j)"))
@@ -138,24 +135,31 @@ def tile_attend_gex_pl_tnh_x_kernel(tc, dyT, hT, ts, wm, offs, out_0, out_1, out
 
         for t in range(PACK):
             for s in range(2):
-                gather_factor(t, s)
+                factor = planes(factors[s], t)
+                slope = planes(dz_first, 0) if (t, s) == (LAST, 0) else factor
+                gather_slope(t, s, slope)
+                if (t, s) != (LAST, 1):
+                    nc.gpsimd.tensor_tensor(factor, slope, ts_rows[:, s, :], ALU.mult)
+        for t in range(2):
+            nc.vector.tensor_copy(planes(dy_listed, t), dy_planes[t][:].indirect(listed(1)))
         for t in range(LAST):
-            if t < PLAIN:
-                nc.vector.tensor_copy(planes(dy_listed, t), dy_planes[t][:].indirect(listed(1)))
-            gather_dz(t, 0)
-            if t >= PLAIN:
-                gather_dz(t, 1)
+            gather_times(planes(dz_first, t), t, listed(0), planes(factors[0], t))
             if t == 1:
-                interleave_pair(0)
+                interleave(0, 0, planes(dz_first, 0, 2))
+        dz_second_high = planes(factors[0], 0, 2)
+        gather_times(planes(dz_second_high, 0), 2, listed(1), planes(factors[1], 2))
         w_grouped = keep.tile([P, PACK * D // 2], BF16, name="w_grouped", align_bytes=ALIGN)
         quantize_w(0, w_grouped[:])
         for first in (0, HALF // 2):
-            gather_dz(LAST, 0, first, HALF // 2)
-            interleave_pair(2, first, HALF // 2)
-        gather_dz(LAST, 1)
+            cols = slice(first, first + HALF // 2)
+            gather_times(planes(dz_first, LAST)[:, cols], LAST, entries(first, HALF // 2), planes(factors[0], LAST)[:, cols])
+            interleave(0, 2, planes(dz_first, 2, 2), first, HALF // 2)
+        nc.vector.tensor_copy(planes(dy_listed, 2), dy_planes[LAST][:].indirect(listed(1)))
         quantize_dz(0)
-        quantize_w(1, planes(dz[1], 0).bitcast(BF16))
-        nc.gpsimd.tensor_tensor(planes(dz[1], 0, PLAIN), dy_listed[:], planes(factors[1], 0, PLAIN), ALU.mult)
+        quantize_w(1, late[:, 3 * HALF // 2 : 5 * HALF // 2].bitcast(BF16))
+        nc.gpsimd.tensor_tensor(planes(late, 0, 2), planes(dy_listed, 0, 2), planes(factors[1], 0, 2), ALU.mult)
+        nc.gpsimd.tensor_tensor(planes(late, 2), planes(factors[1], LAST), ts_rows[:, 1, :], ALU.mult)
+        nc.gpsimd.tensor_tensor(planes(dz_second_high, 1), planes(dy_listed, 2), planes(late, 2), ALU.mult)
 
         def multiply(w, s, bank):
             cols = slice(w * P, (w + 1) * P)
@@ -164,7 +168,7 @@ def tile_attend_gex_pl_tnh_x_kernel(tc, dyT, hT, ts, wm, offs, out_0, out_1, out
 
         def scatter(w, s, bank, first, count, slot=None):
             name = "dx%d_%d" % (w, s * HALF + first)
-            dx = keep.tile([P, count], F32, name=name, tag=slot or name, align_bytes=ALIGN)
+            dx = keep.tile([P, count], F32, name=name, tag=slot or name)
             nc.scalar.copy(dx[:], bank[:, first : first + count])
             nc.vector.tensor_copy(windows[w][:].indirect(entries(s * HALF + first, count)), dx[:])
 
@@ -205,11 +209,12 @@ def tile_attend_gex_pl_tnh_x_kernel(tc, dyT, hT, ts, wm, offs, out_0, out_1, out
 
         multiply_and_scatter(0, 0, product_banks[0])
         multiply_and_scatter(1, 0, product_banks[1])
-        nc.scalar.copy(grouped[1][:].rearrange("p (c i) t -> p c t i", i=4), dz[1][:].rearrange("p (t c i) -> p c t i", t=PACK, i=4))
+        interleave(1, 0, planes(late, 0, 2))
+        interleave(1, 2, dz_second_high)
         quantize_dz(1)
         zeroed_window("grouped1")
         multiply(2, 0, product_banks[0])
-        scatter(2, 0, product_banks[0], 0, HALF, "dz1")
+        scatter(2, 0, product_banks[0], 0, HALF, "ts_listed")
         for w in range(LAST):
             multiply_and_scatter(w, 1, product_banks[(w + 1) % 2])
         dx_last = keep.tile([P, N], F32, name="dx_last")

@@ -42,11 +42,8 @@ def tile_attend_gex_pl_tnh_x_kernel(tc, dyT, hT, ts, wm, offs, out_0, out_1, out
         def entries(first, count):
             return offsets[:, first // STRIPE : (first + count) // STRIPE]
 
-        def listed(s):
-            return entries(s * HALF, HALF)
-
         banks = [psum.tile([P, HALF], F32, name="bank%d" % i) for i in range(8)]
-        column_banks, spread_banks, product_banks = banks[0:2], banks[2:4], banks[4:6]
+        column_banks, spread_bank, product_banks = banks[0:2], banks[2], banks[4:6]
         first_turn_banks, second_turn_banks = banks[0:2] + banks[6:8], banks[2:6]
 
         identity = keep.tile([P, P], F32, name="identity")
@@ -73,7 +70,7 @@ def tile_attend_gex_pl_tnh_x_kernel(tc, dyT, hT, ts, wm, offs, out_0, out_1, out
         windows = []
 
         def zeroed_window(slot):
-            window = keep.tile([P, T], F32, name="window%d" % len(windows), tag=slot, align_bytes=ALIGN)
+            window = keep.tile([P, T], F32, name="window%d" % len(windows), tag=slot)
             nc.gpsimd.memset(window[:], 0.0)
             windows.append(window)
 
@@ -84,99 +81,120 @@ def tile_attend_gex_pl_tnh_x_kernel(tc, dyT, hT, ts, wm, offs, out_0, out_1, out
         nc.vector.memset(windows[2][:, T // 2 - 1 : T], 0.0)
 
         ts_listed = keep.tile([P, N], F32, name="ts_listed", tag="ts_listed")
-        ts_rows = keep.tile([P, 2, HALF], F32, name="ts_rows")
-        ts_columns = keep.tile([P, N // P], F32, name="ts_columns")
+        minus_ts_columns = [keep.tile([P, BLOCKS], F32, name="minus_ts_columns%d" % s) for s in range(2)]
+        minus_ts_rows = keep.tile([P, HALF], F32, name="minus_ts_rows", tag="minus_ts_rows")
         for s in range(2):
-            nc.vector.tensor_copy(ts_listed[:, s * HALF : (s + 1) * HALF], ts_window[:].indirect(listed(s)))
+            nc.vector.tensor_copy(ts_listed[:, s * HALF : (s + 1) * HALF], ts_window[:].indirect(entries(s * HALF, HALF)))
             for c in range(BLOCKS):
                 first = s * HALF + c * P
                 nc.tensor.transpose(column_banks[s][:, c * P : (c + 1) * P], ts_listed[:, first : first + P], identity[:])
-            columns = ts_columns[:, BLOCKS * s : BLOCKS * (s + 1)]
-            nc.scalar.copy(columns, column_banks[s][:, TS_ROW:HALF:P])
-            for c in range(BLOCKS):
-                column = columns[:, c : c + 1].to_broadcast([P, P])
-                nc.tensor.transpose(spread_banks[s][:, c * P : (c + 1) * P], column, identity[:])
-            nc.scalar.copy(ts_rows[:, s, :], spread_banks[s][:])
+            nc.scalar.activation(minus_ts_columns[s][:], column_banks[s][:, TS_ROW:HALF:P], ACT.Copy, scale=-1.0)
+        for c in range(BLOCKS):
+            column = minus_ts_columns[0][:, c : c + 1].to_broadcast([P, P])
+            nc.tensor.transpose(spread_bank[:, c * P : (c + 1) * P], column, identity[:])
+        nc.scalar.copy(minus_ts_rows[:], spread_bank[:])
 
-        def planes(tile, first, count=1):
-            return tile[:, first * HALF : (first + count) * HALF]
+        def part(tile, t, first, count):
+            return tile[:, t * N + first : t * N + first + count]
 
-        h_listed = keep.tile([P, 2 * PACK * HALF], F32, name="h_listed", tag="ts_window")
-        all_factors = keep.tile([P, 2 * PACK * HALF], F32, name="all_factors", tag="ts_listed")
-        factors = [planes(all_factors, s * PACK, PACK) for s in range(2)]
-        dz_first = keep.tile([P, PACK * HALF], F32, name="dz_first")
-        late = keep.tile([P, LAST * HALF], F32, name="late", align_bytes=ALIGN)
-        dy_listed = keep.tile([P, LAST * HALF], F32, name="dy_listed")
-        grouped = [keep.tile([P, HALF, PACK], BF16, name="grouped%d" % s, tag="grouped%d" % s, align_bytes=ALIGN) for s in range(2)]
+        h_listed = keep.tile([P, PACK * N], F32, name="h_listed", tag="ts_window")
+        factors = keep.tile([P, PACK * N], F32, name="factors", tag="ts_listed")
+        dz = keep.tile([P, PACK * N], F32, name="dz")
+        dz_planes = dz[:].rearrange("p (t c) -> p t c", t=PACK)
+        work = keep.tile([P, N], F32, name="work", align_bytes=ALIGN)
+        first_words = work[:].bitcast(BF16)
+        first_grouped = first_words.rearrange("p (c j) -> p c j", j=PACK)
         dz_codes = [keep.tile([P, HALF], U32, name="dz_codes%d" % s, align_bytes=ALIGN) for s in range(2)]
         dz_scales = [keep.tile([P, HALF], U8, name="dz_scales%d" % s, align_bytes=ALIGN) for s in range(2)]
         w_codes = keep.tile([P, D], U32, name="w_codes", align_bytes=ALIGN)
         w_scales = keep.tile([P, D], U8, name="w_scales", align_bytes=ALIGN)
 
-        def gather_slope(t, s, slope):
-            listed_h = planes(h_listed, 2 * t + s)
-            nc.vector.tensor_copy(listed_h, h_planes[t][:].indirect(listed(s)))
-            nc.scalar.activation(slope, listed_h, ACT.Square)
-            nc.scalar.activation(slope, slope, ACT.Identity, scale=-1.0, bias=1.0)
-
-        def gather_times(target, t, offsets_part, factor):
-            nc.vector.tensor_tensor(target, dy_planes[t][:].indirect(offsets_part), factor, ALU.mult)
-
-        def interleave(s, t, pair, first=0, count=HALF):
-            nc.scalar.copy(grouped[s][:, first : first + count, t : t + 2], pair.rearrange("p (e c) -> p c e", e=2)[:, first : first + count, :])
-
-        def quantize_dz(s):
-            nc.vector.quantize_mx(dz_codes[s][:].bitcast(E5M2), dz_scales[s][:], grouped[s][:].rearrange("p c j -> p (c j)"))
-
-        def quantize_w(g, w_grouped):
-            cols = slice(g * D // 2, (g + 1) * D // 2)
-            nc.scalar.copy(w_grouped.rearrange("p (c i j) -> p c j i", i=4, j=PACK), w_raw[g][:].rearrange("p j (c i) -> p c j i", i=4))
-            nc.vector.quantize_mx(w_codes[:, cols].bitcast(E4M3), w_scales[:, cols], w_grouped)
-
         for t in range(PACK):
             for s in range(2):
-                factor = planes(factors[s], t)
-                slope = planes(dz_first, 0) if (t, s) == (LAST, 0) else factor
-                gather_slope(t, s, slope)
-                if (t, s) != (LAST, 1):
-                    nc.gpsimd.tensor_tensor(factor, slope, ts_rows[:, s, :], ALU.mult)
-        for t in range(2):
-            nc.vector.tensor_copy(planes(dy_listed, t), dy_planes[t][:].indirect(listed(1)))
+                listed_h, factor = part(h_listed, t, s * HALF, HALF), part(factors, t, s * HALF, HALF)
+                nc.vector.tensor_copy(listed_h, h_planes[t][:].indirect(entries(s * HALF, HALF)))
+                nc.scalar.activation(factor, listed_h, ACT.Square)
+                if (t, s) == (LAST, 0):
+                    nc.vector.scalar_tensor_tensor(factor, factor, 1.0, spread_bank[:], ALU.subtract, ALU.mult)
+                elif s == 1:
+                    nc.scalar.activation(factor, factor, ACT.Identity, bias=-1.0)
+                else:
+                    slope = part(dz, 0, 0, HALF) if t == LAST - 1 else factor
+                    nc.scalar.activation(slope, factor, ACT.Identity, bias=-1.0)
+                    nc.gpsimd.tensor_tensor(factor, slope, minus_ts_rows[:], ALU.mult)
+        zeroed_window("minus_ts_rows")
+
+        def gather_times(target, t, first, count):
+            nc.vector.tensor_tensor(target, dy_planes[t][:].indirect(entries(first, count)), part(factors, t, first, count), ALU.mult)
+
+        def interleave_pair(t, first, count):
+            cols = slice(first, first + count)
+            nc.scalar.copy(first_grouped[:, cols, t : t + 2], dz_planes[:, t : t + 2, cols].rearrange("p e c -> p c e"))
+
+        def turn_second_half(t, plane):
+            for j in range(BLOCKS):
+                nc.tensor.transpose(first_turn_banks[j][:, t * P : (t + 1) * P], plane[:, j * P : (j + 1) * P], identity[:])
+
+        def quantize_dz(s, words):
+            nc.vector.quantize_mx(dz_codes[s][:].bitcast(E5M2), dz_scales[s][:], words)
+
+        def quantize_w(g):
+            cols = slice(g * D // 2, (g + 1) * D // 2)
+            w_grouped = keep.tile([P, D // 2, PACK], BF16, name="w_grouped%d" % g, align_bytes=ALIGN)
+            nc.scalar.copy(w_grouped[:].rearrange("p (c i) j -> p c j i", i=4), w_raw[g][:].rearrange("p j (c i) -> p c j i", i=4))
+            nc.vector.quantize_mx(w_codes[:, cols].bitcast(E4M3), w_scales[:, cols], w_grouped[:].rearrange("p d j -> p (d j)"))
+
+        def turn_pairs_back(rounded, bank, join_copy, target):
+            pairs = bank[:, 0 : 2 * P]
+            for u in range(2):
+                nc.tensor.transpose(pairs[:, u * P : (u + 1) * P], rounded[:].bitcast(F32)[:, u * P : (u + 1) * P], identity[:])
+            join_copy(target.rearrange("q (t u) -> q t u", u=2), pairs.rearrange("q (u t) -> q t u", u=2))
+
         for t in range(LAST):
-            gather_times(planes(dz_first, t), t, listed(0), planes(factors[0], t))
+            gather_times(part(dz, t, 0, N), t, 0, N)
+            turn_second_half(t, part(dz, t, HALF, HALF))
             if t == 1:
-                interleave(0, 0, planes(dz_first, 0, 2))
-        dz_second_high = planes(factors[0], 0, 2)
-        gather_times(planes(dz_second_high, 0), 2, listed(1), planes(factors[1], 2))
-        w_grouped = keep.tile([P, PACK * D // 2], BF16, name="w_grouped", align_bytes=ALIGN)
-        quantize_w(0, w_grouped[:])
+                interleave_pair(0, 0, HALF)
+        quantize_w(0)
         for first in (0, HALF // 2):
-            cols = slice(first, first + HALF // 2)
-            gather_times(planes(dz_first, LAST)[:, cols], LAST, entries(first, HALF // 2), planes(factors[0], LAST)[:, cols])
-            interleave(0, 2, planes(dz_first, 2, 2), first, HALF // 2)
-        nc.vector.tensor_copy(planes(dy_listed, 2), dy_planes[LAST][:].indirect(listed(1)))
-        quantize_dz(0)
-        quantize_w(1, late[:, 3 * HALF // 2 : 5 * HALF // 2].bitcast(BF16))
-        nc.gpsimd.tensor_tensor(planes(late, 0, 2), planes(dy_listed, 0, 2), planes(factors[1], 0, 2), ALU.mult)
-        nc.gpsimd.tensor_tensor(planes(late, 2), planes(factors[1], LAST), ts_rows[:, 1, :], ALU.mult)
-        nc.gpsimd.tensor_tensor(planes(dz_second_high, 1), planes(dy_listed, 2), planes(late, 2), ALU.mult)
+            gather_times(part(dz, LAST, first, HALF // 2), LAST, first, HALF // 2)
+            interleave_pair(2, first, HALF // 2)
+        quantize_dz(0, first_words)
+        gather_times(work[:, 0:HALF], LAST, HALF, HALF)
 
         def multiply(w, s, bank):
             cols = slice(w * P, (w + 1) * P)
             nc.tensor.matmul_mx(bank[:], lhsT=w_codes[:, cols].bitcast(E4M3), lhsT_scale=w_scales[:, cols],
                                 rhs=dz_codes[s][:].bitcast(E5M2), rhs_scale=dz_scales[s][:], start=True, stop=True)
 
-        def scatter(w, s, bank, first, count, slot=None):
-            name = "dx%d_%d" % (w, s * HALF + first)
-            dx = keep.tile([P, count], F32, name=name, tag=slot or name)
-            nc.scalar.copy(dx[:], bank[:, first : first + count])
-            nc.vector.tensor_copy(windows[w][:].indirect(entries(s * HALF + first, count)), dx[:])
-
-        def multiply_and_scatter(w, s, bank):
-            multiply(w, s, bank)
-            scatter(w, s, bank, 0, HALF)
-            if s == 1:
+        def multiply_and_scatter(w, halves, slot=None):
+            first, count = halves[0] * HALF, len(halves) * HALF
+            name = "dx%d_%d" % (w, first)
+            dx = keep.tile([P, count], F32, name=name, tag=slot or name, align_bytes=ALIGN)
+            for k, s in enumerate(halves):
+                bank = product_banks[(w + s) % 2]
+                multiply(w, s, bank)
+                nc.scalar.copy(dx[:, k * HALF : (k + 1) * HALF], bank[:])
+            nc.vector.tensor_copy(windows[w][:].indirect(entries(first, count)), dx[:])
+            if halves[-1] == 1:
                 nc.sync.dma_start(out_0[w * P : (w + 1) * P, :], windows[w][:])
+
+        multiply_and_scatter(0, [0])
+        quantize_w(1)
+        multiply_and_scatter(1, [0])
+
+        turn_second_half(LAST, work[:, 0:HALF])
+        second_words = keep.tile([P, PACK * HALF], BF16, name="second_words", align_bytes=ALIGN)
+        for j in range(BLOCKS):
+            rounded = keep.tile([P, HALF], BF16, name="rounded_dz%d" % j, tag="rounded%d" % j, align_bytes=ALIGN)
+            nc.scalar.activation(rounded[:].rearrange("c (u q e) -> c u q e", u=2, e=2), first_turn_banks[j][:].rearrange("c (u e q) -> c u q e", u=2, e=2),
+                                 ACT.Copy, scale=minus_ts_columns[1][:, j : j + 1])
+            turn_pairs_back(rounded, first_turn_banks[j], nc.scalar.copy, second_words[:].bitcast(F32)[:, 2 * P * j : 2 * P * (j + 1)])
+        quantize_dz(1, second_words[:])
+        multiply_and_scatter(2, [0], "rounded%d" % (BLOCKS - 1))
+        for w in range(LAST):
+            multiply_and_scatter(w, [1])
+        multiply_and_scatter(LAST, [0, 1])
 
         words_out = out_1[0].rearrange("p t l -> p (t l)").bitcast(I32)
         scales_out = out_2[0].bitcast(I32)
@@ -194,35 +212,14 @@ def tile_attend_gex_pl_tnh_x_kernel(tc, dyT, hT, ts, wm, offs, out_0, out_1, out
                     first = b * RUN + j * P
                     nc.tensor.transpose(first_turn_banks[j][:, b * P : (b + 1) * P], windows[w][:, first : first + P], identity[:])
             for j in range(BLOCKS):
-                rounded = keep.tile([P, HALF], BF16, name="rounded%d%d" % (w, j), tag="rounded%d" % j)
+                rounded = keep.tile([P, HALF], BF16, name="rounded%d%d" % (w, j), tag="rounded%d" % j, align_bytes=ALIGN)
                 round_copy = nc.vector.tensor_copy if (w == LAST and j % 2) else nc.scalar.copy
                 round_copy(rounded[:].rearrange("t (u q e) -> t u q e", u=2, e=2), first_turn_banks[j][:].rearrange("t (q u e) -> t u q e", u=2, e=2))
-                pairs = second_turn_banks[j][:, 0 : 2 * P]
-                for u in range(2):
-                    nc.tensor.transpose(pairs[:, u * P : (u + 1) * P], rounded[:].bitcast(F32)[:, u * P : (u + 1) * P], identity[:])
                 join_copy = nc.vector.tensor_copy if (w, j) == (LAST, BLOCKS - 1) else nc.scalar.copy
-                target = regrouped[:].bitcast(F32)[:, 2 * P * j : 2 * P * (j + 1)]
-                join_copy(target.rearrange("q (t u) -> q t u", u=2), pairs.rearrange("q (u t) -> q t u", u=2))
+                turn_pairs_back(rounded, second_turn_banks[j], join_copy, regrouped[:].bitcast(F32)[:, 2 * P * j : 2 * P * (j + 1)])
                 if w == LAST:
                     quantize_columns(w, regrouped, last_codes, j * P, P)
             return regrouped
-
-        multiply_and_scatter(0, 0, product_banks[0])
-        multiply_and_scatter(1, 0, product_banks[1])
-        interleave(1, 0, planes(late, 0, 2))
-        interleave(1, 2, dz_second_high)
-        quantize_dz(1)
-        zeroed_window("grouped1")
-        multiply(2, 0, product_banks[0])
-        scatter(2, 0, product_banks[0], 0, HALF, "ts_listed")
-        for w in range(LAST):
-            multiply_and_scatter(w, 1, product_banks[(w + 1) % 2])
-        dx_last = keep.tile([P, N], F32, name="dx_last")
-        for s in range(2):
-            multiply(LAST, s, product_banks[s])
-            nc.scalar.copy(dx_last[:, s * HALF : (s + 1) * HALF], product_banks[s][:])
-        nc.vector.tensor_copy(windows[LAST][:].indirect(offsets[:]), dx_last[:])
-        nc.sync.dma_start(out_0[LAST * P : D, :], windows[LAST][:])
 
         words_by_window = words_out.rearrange("(w r) t -> r w t", r=QUAD)
         early_codes = keep.tile([P, LAST, RUN], U32, name="early_codes", align_bytes=ALIGN)

@@ -43,8 +43,9 @@ def tile_attend_gex_pl_tnh_x_kernel(tc, dyT, hT, ts, wm, offs, out_0, out_1, out
             return offsets[:, first // STRIPE : (first + count) // STRIPE]
 
         banks = [psum.tile([P, HALF], F32, name="bank%d" % i) for i in range(8)]
-        column_banks, spread_bank, product_banks = banks[0:2], banks[2], banks[4:6]
-        first_turn_banks, second_turn_banks = banks[0:2] + banks[6:8], banks[2:6]
+        column_banks, spread_bank = banks[0:2], banks[2]
+        product_banks = [[banks[3], banks[4], banks[2], banks[5]], [banks[3], banks[0], banks[2], banks[1]]]
+        first_turn_banks = banks[0:2] + banks[6:8]
 
         identity = keep.tile([P, P], F32, name="identity")
         make_identity(nc, identity[:])
@@ -58,14 +59,13 @@ def tile_attend_gex_pl_tnh_x_kernel(tc, dyT, hT, ts, wm, offs, out_0, out_1, out
         h_planes = [keep.tile([P, T], F32, name="h_plane%d" % t) for t in range(PACK)]
         dy_planes = [keep.tile([P, T], F32, name="dy_plane%d" % t) for t in range(PACK)]
         w_rows = wm[0].rearrange("(p j) d -> p j d", j=PACK)
-        w_raw = [keep.tile([P, PACK, D // 2], F32, name="w_raw%d" % g) for g in range(2)]
+        w_raw = keep.tile([P, PACK, D], F32, name="w_raw")
         for t in range(PACK):
             nc.sync.dma_start(h_planes[t][:], h_rows[:, t, :])
-        for t in range(LAST):
+        nc.sync.dma_start(dy_planes[0][:], dy_rows[:, 0, :])
+        nc.sync.dma_start(w_raw[:], w_rows)
+        for t in range(1, PACK):
             nc.sync.dma_start(dy_planes[t][:], dy_rows[:, t, :])
-        nc.sync.dma_start(w_raw[0][:], w_rows[:, :, 0 : D // 2])
-        nc.sync.dma_start(dy_planes[LAST][:], dy_rows[:, LAST, :])
-        nc.sync.dma_start(w_raw[1][:], w_rows[:, :, D // 2 : D])
 
         windows = []
 
@@ -109,13 +109,14 @@ def tile_attend_gex_pl_tnh_x_kernel(tc, dyT, hT, ts, wm, offs, out_0, out_1, out
         w_codes = keep.tile([P, D], U32, name="w_codes", align_bytes=ALIGN)
         w_scales = keep.tile([P, D], U8, name="w_scales", align_bytes=ALIGN)
 
+        held_plane, last_factor = h_listed[:, 0:HALF], h_listed[:, HALF // 2 : HALF // 2 + HALF]
         for t in range(PACK):
             for s in range(2):
                 listed_h, factor = part(h_listed, t, s * HALF, HALF), part(factors, t, s * HALF, HALF)
                 nc.vector.tensor_copy(listed_h, h_planes[t][:].indirect(entries(s * HALF, HALF)))
                 nc.scalar.activation(factor, listed_h, ACT.Square)
                 if (t, s) == (LAST, 0):
-                    nc.vector.scalar_tensor_tensor(factor, factor, 1.0, spread_bank[:], ALU.subtract, ALU.mult)
+                    nc.vector.scalar_tensor_tensor(last_factor, factor, 1.0, spread_bank[:], ALU.subtract, ALU.mult)
                 elif s == 1:
                     nc.scalar.activation(factor, factor, ACT.Identity, bias=-1.0)
                 else:
@@ -124,8 +125,8 @@ def tile_attend_gex_pl_tnh_x_kernel(tc, dyT, hT, ts, wm, offs, out_0, out_1, out
                     nc.gpsimd.tensor_tensor(factor, slope, minus_ts_rows[:], ALU.mult)
         zeroed_window("minus_ts_rows")
 
-        def gather_times(target, t, first, count):
-            nc.vector.tensor_tensor(target, dy_planes[t][:].indirect(entries(first, count)), part(factors, t, first, count), ALU.mult)
+        def gather_times(target, t, first, count, factor):
+            nc.vector.tensor_tensor(target, dy_planes[t][:].indirect(entries(first, count)), factor, ALU.mult)
 
         def interleave_pair(t, first, count):
             cols = slice(first, first + count)
@@ -138,11 +139,10 @@ def tile_attend_gex_pl_tnh_x_kernel(tc, dyT, hT, ts, wm, offs, out_0, out_1, out
         def quantize_dz(s, words):
             nc.vector.quantize_mx(dz_codes[s][:].bitcast(E5M2), dz_scales[s][:], words)
 
-        def quantize_w(g):
-            cols = slice(g * D // 2, (g + 1) * D // 2)
-            w_grouped = keep.tile([P, D // 2, PACK], BF16, name="w_grouped%d" % g, align_bytes=ALIGN)
-            nc.scalar.copy(w_grouped[:].rearrange("p (c i) j -> p c j i", i=4), w_raw[g][:].rearrange("p j (c i) -> p c j i", i=4))
-            nc.vector.quantize_mx(w_codes[:, cols].bitcast(E4M3), w_scales[:, cols], w_grouped[:].rearrange("p d j -> p (d j)"))
+        def quantize_w():
+            w_grouped = keep.tile([P, D * PACK], BF16, name="w_grouped", align_bytes=ALIGN)
+            nc.scalar.copy(w_grouped[:].rearrange("p (t m j) -> p m j t", t=PACK, j=PACK), w_raw[:].rearrange("p j (m t) -> p m j t", t=PACK))
+            nc.vector.quantize_mx(w_codes[:].bitcast(E4M3), w_scales[:], w_grouped[:])
 
         def turn_pairs_back(rounded, bank, join_copy, target):
             pairs = bank[:, 0 : 2 * P]
@@ -150,40 +150,50 @@ def tile_attend_gex_pl_tnh_x_kernel(tc, dyT, hT, ts, wm, offs, out_0, out_1, out
                 nc.tensor.transpose(pairs[:, u * P : (u + 1) * P], rounded[:].bitcast(F32)[:, u * P : (u + 1) * P], identity[:])
             join_copy(target.rearrange("q (t u) -> q t u", u=2), pairs.rearrange("q (u t) -> q t u", u=2))
 
-        for t in range(LAST):
-            gather_times(part(dz, t, 0, N), t, 0, N)
+        for t in range(2):
+            gather_times(part(dz, t, 0, N), t, 0, N, part(factors, t, 0, N))
             turn_second_half(t, part(dz, t, HALF, HALF))
-            if t == 1:
-                interleave_pair(0, 0, HALF)
-        quantize_w(0)
+        quantize_w()
+        interleave_pair(0, 0, HALF)
+        gather_times(part(dz, 2, 0, HALF), 2, 0, HALF, part(factors, 2, 0, HALF))
         for first in (0, HALF // 2):
-            gather_times(part(dz, LAST, first, HALF // 2), LAST, first, HALF // 2)
+            gather_times(part(dz, LAST, first, HALF // 2), LAST, first, HALF // 2, last_factor[:, first : first + HALF // 2])
             interleave_pair(2, first, HALF // 2)
+        gather_times(held_plane, 2, HALF, HALF, part(factors, 2, HALF, HALF))
+        turn_second_half(2, held_plane)
         quantize_dz(0, first_words)
-        gather_times(work[:, 0:HALF], LAST, HALF, HALF)
+        last_plane = part(dz, LAST, HALF // 2, HALF)
+        gather_times(last_plane, LAST, HALF, HALF, part(factors, LAST, HALF, HALF))
 
         def multiply(w, s, bank):
             cols = slice(w * P, (w + 1) * P)
             nc.tensor.matmul_mx(bank[:], lhsT=w_codes[:, cols].bitcast(E4M3), lhsT_scale=w_scales[:, cols],
                                 rhs=dz_codes[s][:].bitcast(E5M2), rhs_scale=dz_scales[s][:], start=True, stop=True)
 
-        def multiply_and_scatter(w, halves, slot=None):
-            first, count = halves[0] * HALF, len(halves) * HALF
-            name = "dx%d_%d" % (w, first)
-            dx = keep.tile([P, count], F32, name=name, tag=slot or name, align_bytes=ALIGN)
-            for k, s in enumerate(halves):
-                bank = product_banks[(w + s) % 2]
-                multiply(w, s, bank)
-                nc.scalar.copy(dx[:, k * HALF : (k + 1) * HALF], bank[:])
-            nc.vector.tensor_copy(windows[w][:].indirect(entries(first, count)), dx[:])
-            if halves[-1] == 1:
-                nc.sync.dma_start(out_0[w * P : (w + 1) * P, :], windows[w][:])
+        out_lanes = out_0.rearrange("(p j) c -> p j c", j=PACK)
 
-        multiply_and_scatter(0, [0])
-        quantize_w(1)
-        multiply_and_scatter(1, [0])
+        def product(lane, s):
+            bank = product_banks[s][lane]
+            multiply(lane, s, bank)
+            return bank
 
-        turn_second_half(LAST, work[:, 0:HALF])
+        def scatter(lane, first, pieces, dx):
+            done = 0
+            for piece in pieces:
+                nc.scalar.copy(dx[:, done : done + piece.shape[1]], piece)
+                done += piece.shape[1]
+            nc.vector.tensor_copy(windows[lane][:].indirect(entries(first, done)), dx)
+            if first + done == N:
+                nc.sync.dma_start(out_lanes[:, lane, :], windows[lane][:])
+
+        def source(name, count, slot=None):
+            return keep.tile([P, count], F32, name=name, tag=slot or name, align_bytes=ALIGN)[:]
+
+        scatter(2, 0, [product(2, 0)[:]], source("dx2", HALF))
+        scatter(0, 0, [product(0, 0)[:]], source("dx0", HALF))
+        cut_bank = product(1, 0)
+
+        turn_second_half(LAST, last_plane)
         second_words = keep.tile([P, PACK * HALF], BF16, name="second_words", align_bytes=ALIGN)
         for j in range(BLOCKS):
             rounded = keep.tile([P, HALF], BF16, name="rounded_dz%d" % j, tag="rounded%d" % j, align_bytes=ALIGN)
@@ -191,45 +201,34 @@ def tile_attend_gex_pl_tnh_x_kernel(tc, dyT, hT, ts, wm, offs, out_0, out_1, out
                                  ACT.Copy, scale=minus_ts_columns[1][:, j : j + 1])
             turn_pairs_back(rounded, first_turn_banks[j], nc.scalar.copy, second_words[:].bitcast(F32)[:, 2 * P * j : 2 * P * (j + 1)])
         quantize_dz(1, second_words[:])
-        multiply_and_scatter(2, [0], "rounded%d" % (BLOCKS - 1))
-        for w in range(LAST):
-            multiply_and_scatter(w, [1])
-        multiply_and_scatter(LAST, [0, 1])
+        scatter(1, 0, [cut_bank[:, 0 : HALF // 2]], source("dx1", HALF // 2, "rounded%d" % (BLOCKS - 1)))
+        last_first_bank = product(LAST, 0)
+        last_dx = source("last_dx", N)
+        scatter(2, HALF, [product(2, 1)[:]], last_dx[:, HALF:N])
+        scatter(0, HALF, [product(0, 1)[:]], source("dx0_second", HALF))
+        scatter(1, HALF // 2, [cut_bank[:, HALF // 2 : HALF], product(1, 1)[:]], source("dx1_rest", N - HALF // 2))
 
+        words = keep.tile([P, T, PACK], BF16, name="words", align_bytes=ALIGN)
+        codes = keep.tile([P, T], U32, name="codes", align_bytes=ALIGN)
+        scales = keep.tile([P, T], U8, name="scales", align_bytes=ALIGN)
+        low, high = slice(0, T // 2), slice(T // 2, T)
+
+        def put_lane(copy, lane, cols):
+            copy(words[:, cols, lane], windows[lane][:, cols])
+
+        put_lane(nc.scalar.copy, 2, low)
+        scatter(LAST, 0, [last_first_bank[:], product(LAST, 1)[:]], last_dx)
+        put_lane(nc.scalar.copy, 2, high)
+        for lane in range(2):
+            put_lane(nc.scalar.copy, lane, low)
+            put_lane(nc.gpsimd.tensor_copy, lane, high)
+        runs = [slice(b * RUN, (b + 1) * RUN) for b in range(QUADS)]
+        for b, cols in enumerate(runs):
+            put_lane(nc.vector.tensor_copy if b < 2 else nc.scalar.copy, LAST, cols)
         words_out = out_1[0].rearrange("p t l -> p (t l)").bitcast(I32)
+        for cols in runs:
+            nc.vector.quantize_mx(codes[:, cols].bitcast(E4M3), scales[:, cols], words[:, cols, :].rearrange("p c j -> p (c j)"))
+            nc.sync.dma_start(words_out[:, cols], codes[:, cols].bitcast(I32))
         scales_out = out_2[0].bitcast(I32)
-        out_scales = keep.tile([P, RUN], U8, name="out_scales", align_bytes=ALIGN)
-        last_codes = keep.tile([P, RUN], U32, name="last_codes", align_bytes=ALIGN)
-
-        def quantize_columns(w, regrouped, codes, first, count):
-            cols = slice(first, first + count)
-            nc.vector.quantize_mx(codes[:, cols].bitcast(E4M3), out_scales[PACK * w : P, cols], regrouped[:, PACK * first : PACK * (first + count)])
-
-        def regroup_window(w):
-            regrouped = keep.tile([P, RUN * PACK], BF16, name="regrouped%d" % w, align_bytes=ALIGN)
-            for j in range(BLOCKS):
-                for b in range(QUADS):
-                    first = b * RUN + j * P
-                    nc.tensor.transpose(first_turn_banks[j][:, b * P : (b + 1) * P], windows[w][:, first : first + P], identity[:])
-            for j in range(BLOCKS):
-                rounded = keep.tile([P, HALF], BF16, name="rounded%d%d" % (w, j), tag="rounded%d" % j, align_bytes=ALIGN)
-                round_copy = nc.vector.tensor_copy if (w == LAST and j % 2) else nc.scalar.copy
-                round_copy(rounded[:].rearrange("t (u q e) -> t u q e", u=2, e=2), first_turn_banks[j][:].rearrange("t (q u e) -> t u q e", u=2, e=2))
-                join_copy = nc.vector.tensor_copy if (w, j) == (LAST, BLOCKS - 1) else nc.scalar.copy
-                turn_pairs_back(rounded, second_turn_banks[j], join_copy, regrouped[:].bitcast(F32)[:, 2 * P * j : 2 * P * (j + 1)])
-                if w == LAST:
-                    quantize_columns(w, regrouped, last_codes, j * P, P)
-            return regrouped
-
-        words_by_window = words_out.rearrange("(w r) t -> r w t", r=QUAD)
-        early_codes = keep.tile([P, LAST, RUN], U32, name="early_codes", align_bytes=ALIGN)
-        for w in range(LAST):
-            quantize_columns(w, regroup_window(w), early_codes[:, w, :], 0, RUN)
-        for b in range(QUADS):
-            nc.sync.dma_start(words_by_window[:, 0:LAST, b * RUN : (b + 1) * RUN], early_codes[b * QUAD : (b + 1) * QUAD, :, :].bitcast(I32))
-        regroup_window(LAST)
-        for b in range(QUADS):
-            nc.sync.dma_start(words_by_window[:, LAST, b * RUN : (b + 1) * RUN], last_codes[b * QUAD : (b + 1) * QUAD, :].bitcast(I32))
-        scale_rows, scale_words = D // QUAD, RUN // 4
-        for b in range(QUADS):
-            nc.scalar.dma_start(scales_out[:, b * scale_words : (b + 1) * scale_words], out_scales[b * QUAD : b * QUAD + scale_rows, :].bitcast(I32))
+        for q in range(QUADS):
+            nc.scalar.dma_start(scales_out[PACK * q : PACK * (q + 1), :], scales[QUAD * q : QUAD * q + PACK, :].bitcast(I32))

@@ -59,13 +59,14 @@ def tile_attend_gex_pl_tnh_x_kernel(tc, dyT, hT, ts, wm, offs, out_0, out_1, out
         h_planes = [keep.tile([P, T], F32, name="h_plane%d" % t) for t in range(PACK)]
         dy_planes = [keep.tile([P, T], F32, name="dy_plane%d" % t) for t in range(PACK)]
         w_rows = wm[0].rearrange("(p j) d -> p j d", j=PACK)
-        w_raw = keep.tile([P, PACK, D], F32, name="w_raw")
+        w_raw = [keep.tile([P, 2, D], F32, name="w_raw%d" % u) for u in range(2)]
         for t in range(PACK):
             nc.sync.dma_start(h_planes[t][:], h_rows[:, t, :])
         nc.sync.dma_start(dy_planes[0][:], dy_rows[:, 0, :])
-        nc.sync.dma_start(w_raw[:], w_rows)
+        nc.sync.dma_start(w_raw[0][:], w_rows[:, 0:2, :])
         for t in range(1, PACK):
             nc.sync.dma_start(dy_planes[t][:], dy_rows[:, t, :])
+        nc.sync.dma_start(w_raw[1][:], w_rows[:, 2:PACK, :])
 
         windows = []
 
@@ -139,10 +140,16 @@ def tile_attend_gex_pl_tnh_x_kernel(tc, dyT, hT, ts, wm, offs, out_0, out_1, out
         def quantize_dz(s, words):
             nc.vector.quantize_mx(dz_codes[s][:].bitcast(E5M2), dz_scales[s][:], words)
 
-        def quantize_w():
-            w_grouped = keep.tile([P, D * PACK], BF16, name="w_grouped", align_bytes=ALIGN)
-            nc.scalar.copy(w_grouped[:].rearrange("p (t m j) -> p m j t", t=PACK, j=PACK), w_raw[:].rearrange("p j (m t) -> p m j t", t=PACK))
-            nc.vector.quantize_mx(w_codes[:].bitcast(E4M3), w_scales[:], w_grouped[:])
+        w_grouped = keep.tile([P, D * PACK], BF16, name="w_grouped", align_bytes=ALIGN)
+
+        def regroup_w(u, lanes):
+            target = w_grouped[:].rearrange("p (t m j) -> p m j t", t=PACK, j=PACK)[:, :, 2 * u : 2 * u + 2, lanes]
+            nc.scalar.copy(target, w_raw[u][:].rearrange("p j (m t) -> p m j t", t=PACK)[:, :, :, lanes])
+
+        def quantize_w(lane):
+            regroup_w(1, slice(lane, lane + 2))
+            cols = slice(lane * P, (lane + 2) * P)
+            nc.vector.quantize_mx(w_codes[:, cols].bitcast(E4M3), w_scales[:, cols], w_grouped[:, PACK * cols.start : PACK * cols.stop])
 
         def turn_pairs_back(rounded, bank, join_copy, target):
             pairs = bank[:, 0 : 2 * P]
@@ -153,17 +160,20 @@ def tile_attend_gex_pl_tnh_x_kernel(tc, dyT, hT, ts, wm, offs, out_0, out_1, out
         for t in range(2):
             gather_times(part(dz, t, 0, N), t, 0, N, part(factors, t, 0, N))
             turn_second_half(t, part(dz, t, HALF, HALF))
-        quantize_w()
+        regroup_w(0, slice(0, PACK))
         interleave_pair(0, 0, HALF)
         gather_times(part(dz, 2, 0, HALF), 2, 0, HALF, part(factors, 2, 0, HALF))
         for first in (0, HALF // 2):
             gather_times(part(dz, LAST, first, HALF // 2), LAST, first, HALF // 2, last_factor[:, first : first + HALF // 2])
+            if first:
+                quantize_w(2)
             interleave_pair(2, first, HALF // 2)
         gather_times(held_plane, 2, HALF, HALF, part(factors, 2, HALF, HALF))
         turn_second_half(2, held_plane)
         quantize_dz(0, first_words)
         last_plane = part(dz, LAST, HALF // 2, HALF)
         gather_times(last_plane, LAST, HALF, HALF, part(factors, LAST, HALF, HALF))
+        quantize_w(0)
 
         def multiply(w, s, bank):
             cols = slice(w * P, (w + 1) * P)

@@ -50,22 +50,25 @@ def tile_attend_gex_pl_tnh_x_kernel(tc, dyT, hT, ts, wm, offs, out_0, out_1, out
         identity = keep.tile([P, P], F32, name="identity")
         make_identity(nc, identity[:])
 
-        ts_window = keep.tile([P, T], F32, name="ts_window", tag="ts_window")
+        ts_window = keep.tile([P, T], F32, name="ts_window")
         nc.sync.dma_start(ts_window[TS_ROW:P, :], ts[TS_ROW:P, :])
-        nc.gpsimd.memset(ts_window[0:TS_ROW, :], 0.0)
+        nc.gpsimd.memset(ts_window[0:TS_ROW, T // 2 : T], 0.0)
+        nc.vector.memset(ts_window[0:TS_ROW, 0 : T // 2 - 1], 0.0)
+        nc.vector.memset(ts_window[0:TS_ROW, T // 2 - 1 : T // 2], 0.0)
 
         h_rows = hT.rearrange("(p j) c -> p j c", j=PACK)
         dy_rows = dyT.rearrange("(p j) c -> p j c", j=PACK)
         h_planes = [keep.tile([P, T], F32, name="h_plane%d" % t) for t in range(PACK)]
-        dy_planes = [keep.tile([P, T], F32, name="dy_plane%d" % t) for t in range(PACK)]
+        dy_planes = [keep.tile([P, T], F32, name="dy_plane%d" % t, tag="dy_plane%d" % t) for t in range(PACK)]
         w_rows = wm[0].rearrange("(p j) d -> p j d", j=PACK)
         w_raw = [keep.tile([P, 2, D], F32, name="w_raw%d" % u) for u in range(2)]
-        for t in range(PACK):
-            nc.sync.dma_start(h_planes[t][:], h_rows[:, t, :])
-        nc.sync.dma_start(dy_planes[0][:], dy_rows[:, 0, :])
-        nc.sync.dma_start(w_raw[0][:], w_rows[:, 0:2, :])
+        nc.sync.dma_start(h_planes[0][:], h_rows[:, 0, :])
         for t in range(1, PACK):
-            nc.sync.dma_start(dy_planes[t][:], dy_rows[:, t, :])
+            nc.sync.dma_start(h_planes[t][:], h_rows[:, t, :])
+            if t == LAST:
+                nc.sync.dma_start(w_raw[0][:], w_rows[:, 0:2, :])
+            nc.sync.dma_start(dy_planes[t - 1][:], dy_rows[:, t - 1, :])
+        nc.sync.dma_start(dy_planes[LAST][:], dy_rows[:, LAST, :])
         nc.sync.dma_start(w_raw[1][:], w_rows[:, 2:PACK, :])
 
         windows = []
@@ -77,9 +80,7 @@ def tile_attend_gex_pl_tnh_x_kernel(tc, dyT, hT, ts, wm, offs, out_0, out_1, out
 
         zeroed_window("window0")
         zeroed_window("window1")
-        windows.append(keep.tile([P, T], F32, name="window2"))
-        nc.vector.memset(windows[2][:, 0 : T // 2 - 1], 0.0)
-        nc.vector.memset(windows[2][:, T // 2 - 1 : T], 0.0)
+        zeroed_window("window2")
 
         ts_listed = keep.tile([P, N], F32, name="ts_listed", tag="ts_listed")
         minus_ts_columns = [keep.tile([P, BLOCKS], F32, name="minus_ts_columns%d" % s) for s in range(2)]
@@ -98,7 +99,7 @@ def tile_attend_gex_pl_tnh_x_kernel(tc, dyT, hT, ts, wm, offs, out_0, out_1, out
         def part(tile, t, first, count):
             return tile[:, t * N + first : t * N + first + count]
 
-        h_listed = keep.tile([P, PACK * N], F32, name="h_listed", tag="ts_window")
+        h_listed = keep.tile([P, PACK * N], F32, name="h_listed")
         factors = keep.tile([P, PACK * N], F32, name="factors", tag="ts_listed")
         dz = keep.tile([P, PACK * N], F32, name="dz")
         dz_planes = dz[:].rearrange("p (t c) -> p t c", t=PACK)
@@ -111,20 +112,29 @@ def tile_attend_gex_pl_tnh_x_kernel(tc, dyT, hT, ts, wm, offs, out_0, out_1, out
         w_scales = keep.tile([P, D], U8, name="w_scales", align_bytes=ALIGN)
 
         held_plane, last_factor = h_listed[:, 0:HALF], h_listed[:, HALF // 2 : HALF // 2 + HALF]
-        for t in range(PACK):
+
+        def gather_factors(t):
             for s in range(2):
                 listed_h, factor = part(h_listed, t, s * HALF, HALF), part(factors, t, s * HALF, HALF)
                 nc.vector.tensor_copy(listed_h, h_planes[t][:].indirect(entries(s * HALF, HALF)))
-                nc.scalar.activation(factor, listed_h, ACT.Square)
-                if (t, s) == (LAST, 0):
-                    nc.vector.scalar_tensor_tensor(last_factor, factor, 1.0, spread_bank[:], ALU.subtract, ALU.mult)
-                elif s == 1:
+                if s == 1:
+                    nc.scalar.activation(factor, listed_h, ACT.Square)
                     nc.scalar.activation(factor, factor, ACT.Identity, bias=-1.0)
+                elif t == LAST:
+                    nc.scalar.activation(factor, listed_h, ACT.Square)
+                    nc.vector.scalar_tensor_tensor(last_factor, factor, 1.0, spread_bank[:], ALU.subtract, ALU.mult)
                 else:
-                    slope = part(dz, 0, 0, HALF) if t == LAST - 1 else factor
-                    nc.scalar.activation(slope, factor, ACT.Identity, bias=-1.0)
-                    nc.gpsimd.tensor_tensor(factor, slope, minus_ts_rows[:], ALU.mult)
-        zeroed_window("minus_ts_rows")
+                    low, high = slice(0, HALF // 2), slice(HALF // 2, HALF)
+                    first_square = part(factors, t, HALF, HALF // 2)
+                    nc.scalar.activation(first_square, listed_h[:, low], ACT.Square)
+                    nc.scalar.activation(factor[:, high], listed_h[:, high], ACT.Square)
+                    nc.scalar.activation(factor[:, low], first_square, ACT.Identity, bias=-1.0)
+                    nc.scalar.activation(factor[:, high], factor[:, high], ACT.Identity, bias=-1.0)
+                    nc.gpsimd.tensor_tensor(factor, factor, minus_ts_rows[:], ALU.mult)
+
+        def gather_dy(t, s, listed_dy):
+            nc.vector.tensor_copy(listed_dy, dy_planes[t][:].indirect(entries(s * HALF, HALF)))
+            nc.gpsimd.tensor_tensor(part(dz, t, s * HALF, HALF), listed_dy, part(factors, t, s * HALF, HALF), ALU.mult)
 
         def gather_times(target, t, first, count, factor):
             nc.vector.tensor_tensor(target, dy_planes[t][:].indirect(entries(first, count)), factor, ALU.mult)
@@ -157,11 +167,16 @@ def tile_attend_gex_pl_tnh_x_kernel(tc, dyT, hT, ts, wm, offs, out_0, out_1, out
                 nc.tensor.transpose(pairs[:, u * P : (u + 1) * P], rounded[:].bitcast(F32)[:, u * P : (u + 1) * P], identity[:])
             join_copy(target.rearrange("q (t u) -> q t u", u=2), pairs.rearrange("q (u t) -> q t u", u=2))
 
+        gather_factors(0)
         for t in range(2):
-            gather_times(part(dz, t, 0, N), t, 0, N, part(factors, t, 0, N))
+            gather_factors(t + 1)
+            for s in range(2):
+                gather_dy(t, s, part(dz, 2, 0, HALF) if t + s == 2 else part(dz, t, s * HALF, HALF))
             turn_second_half(t, part(dz, t, HALF, HALF))
-        regroup_w(0, slice(0, PACK))
+        zeroed_window("dy_plane1")
+        gather_factors(LAST)
         interleave_pair(0, 0, HALF)
+        regroup_w(0, slice(0, PACK))
         gather_times(part(dz, 2, 0, HALF), 2, 0, HALF, part(factors, 2, 0, HALF))
         for first in (0, HALF // 2):
             gather_times(part(dz, LAST, first, HALF // 2), LAST, first, HALF // 2, last_factor[:, first : first + HALF // 2])

@@ -156,9 +156,9 @@ def tile_attend_gex_pl_tnh_x_kernel(tc, dyT, hT, ts, wm, offs, out_0, out_1, out
             target = w_grouped[:].rearrange("p (t m j) -> p m j t", t=PACK, j=PACK)[:, :, 2 * u : 2 * u + 2, lanes]
             nc.scalar.copy(target, w_raw[u][:].rearrange("p j (m t) -> p m j t", t=PACK)[:, :, :, lanes])
 
-        def quantize_w(lane):
-            regroup_w(1, slice(lane, lane + 2))
-            cols = slice(lane * P, (lane + 2) * P)
+        def quantize_w(lane, count):
+            regroup_w(1, slice(lane, lane + count))
+            cols = slice(lane * P, (lane + count) * P)
             nc.vector.quantize_mx(w_codes[:, cols].bitcast(E4M3), w_scales[:, cols], w_grouped[:, PACK * cols.start : PACK * cols.stop])
 
         def turn_pairs_back(rounded, bank, join_copy, target):
@@ -180,15 +180,15 @@ def tile_attend_gex_pl_tnh_x_kernel(tc, dyT, hT, ts, wm, offs, out_0, out_1, out
         gather_times(part(dz, 2, 0, HALF), 2, 0, HALF, part(factors, 2, 0, HALF))
         for first in (0, HALF // 2):
             gather_times(part(dz, LAST, first, HALF // 2), LAST, first, HALF // 2, last_factor[:, first : first + HALF // 2])
-            if first:
-                quantize_w(2)
             interleave_pair(2, first, HALF // 2)
         gather_times(held_plane, 2, HALF, HALF, part(factors, 2, HALF, HALF))
         turn_second_half(2, held_plane)
         quantize_dz(0, first_words)
-        last_plane = part(dz, LAST, HALF // 2, HALF)
+        quantize_w(2, 1)
+        last_plane = work[:, 0:HALF]
         gather_times(last_plane, LAST, HALF, HALF, part(factors, LAST, HALF, HALF))
-        quantize_w(0)
+        quantize_w(0, 2)
+        quantize_w(LAST, 1)
 
         def multiply(w, s, bank):
             cols = slice(w * P, (w + 1) * P)
@@ -219,7 +219,7 @@ def tile_attend_gex_pl_tnh_x_kernel(tc, dyT, hT, ts, wm, offs, out_0, out_1, out
         cut_bank = product(1, 0)
 
         turn_second_half(LAST, last_plane)
-        second_words = keep.tile([P, PACK * HALF], BF16, name="second_words", align_bytes=ALIGN)
+        second_words = keep.tile([P, PACK * HALF], BF16, name="second_words", tag="second_words", align_bytes=ALIGN)
         for j in range(BLOCKS):
             rounded = keep.tile([P, HALF], BF16, name="rounded_dz%d" % j, tag="rounded%d" % j, align_bytes=ALIGN)
             nc.scalar.activation(rounded[:].rearrange("c (u q e) -> c u q e", u=2, e=2), first_turn_banks[j][:].rearrange("c (u e q) -> c u q e", u=2, e=2),
@@ -228,10 +228,11 @@ def tile_attend_gex_pl_tnh_x_kernel(tc, dyT, hT, ts, wm, offs, out_0, out_1, out
         quantize_dz(1, second_words[:])
         scatter(1, 0, [cut_bank[:, 0 : HALF // 2]], source("dx1", HALF // 2, "rounded%d" % (BLOCKS - 1)))
         last_first_bank = product(LAST, 0)
-        last_dx = source("last_dx", N)
+        late_dx = source("late_dx", 2 * N - HALF // 2, "second_words")
+        last_dx = late_dx[:, 0:N]
         scatter(2, HALF, [product(2, 1)[:]], last_dx[:, HALF:N])
         scatter(0, HALF, [product(0, 1)[:]], source("dx0_second", HALF))
-        scatter(1, HALF // 2, [cut_bank[:, HALF // 2 : HALF], product(1, 1)[:]], source("dx1_rest", N - HALF // 2))
+        scatter(1, HALF // 2, [cut_bank[:, HALF // 2 : HALF], product(1, 1)[:]], late_dx[:, N : 2 * N - HALF // 2])
 
         words = keep.tile([P, T, PACK], BF16, name="words", align_bytes=ALIGN)
         codes = keep.tile([P, T], U32, name="codes", align_bytes=ALIGN)
@@ -256,4 +257,5 @@ def tile_attend_gex_pl_tnh_x_kernel(tc, dyT, hT, ts, wm, offs, out_0, out_1, out
             nc.sync.dma_start(words_out[:, cols], codes[:, cols].bitcast(I32))
         scales_out = out_2[0].bitcast(I32)
         for q in range(QUADS):
-            nc.scalar.dma_start(scales_out[PACK * q : PACK * (q + 1), :], scales[QUAD * q : QUAD * q + PACK, :].bitcast(I32))
+            queue = nc.sync if q == LAST else nc.scalar
+            queue.dma_start(scales_out[PACK * q : PACK * (q + 1), :], scales[QUAD * q : QUAD * q + PACK, :].bitcast(I32))

@@ -27,6 +27,7 @@ RUN = T // QUADS
 BLOCKS = HALF // P
 STRIPE = 16
 TS_ROW = P - 1
+CUT = 352
 ALIGN = 64
 
 
@@ -226,13 +227,13 @@ def tile_attend_gex_pl_tnh_x_kernel(tc, dyT, hT, ts, wm, offs, out_0, out_1, out
                                  ACT.Copy, scale=minus_ts_columns[1][:, j : j + 1])
             turn_pairs_back(rounded, first_turn_banks[j], nc.scalar.copy, second_words[:].bitcast(F32)[:, 2 * P * j : 2 * P * (j + 1)])
         quantize_dz(1, second_words[:])
-        scatter(1, 0, [cut_bank[:, 0 : HALF // 2]], source("dx1", HALF // 2, "rounded%d" % (BLOCKS - 1)))
+        scatter(1, 0, [cut_bank[:, 0:CUT]], source("dx1", CUT, "rounded%d" % (BLOCKS - 1)))
         last_first_bank = product(LAST, 0)
-        late_dx = source("late_dx", 2 * N - HALF // 2, "second_words")
+        late_dx = source("late_dx", 2 * N - CUT, "second_words")
         last_dx = late_dx[:, 0:N]
         scatter(2, HALF, [product(2, 1)[:]], last_dx[:, HALF:N])
         scatter(0, HALF, [product(0, 1)[:]], source("dx0_second", HALF))
-        scatter(1, HALF // 2, [cut_bank[:, HALF // 2 : HALF], product(1, 1)[:]], late_dx[:, N : 2 * N - HALF // 2])
+        scatter(1, CUT, [cut_bank[:, CUT:HALF], product(1, 1)[:]], late_dx[:, N : 2 * N - CUT])
 
         words = keep.tile([P, T, PACK], BF16, name="words", align_bytes=ALIGN)
         codes = keep.tile([P, T], U32, name="codes", align_bytes=ALIGN)
@@ -245,10 +246,14 @@ def tile_attend_gex_pl_tnh_x_kernel(tc, dyT, hT, ts, wm, offs, out_0, out_1, out
         put_lane(nc.scalar.copy, 2, low)
         scatter(LAST, 0, [last_first_bank[:], product(LAST, 1)[:]], last_dx)
         put_lane(nc.scalar.copy, 2, high)
-        for lane in range(2):
-            put_lane(nc.scalar.copy, lane, low)
-            put_lane(nc.gpsimd.tensor_copy, lane, high)
+        staged = keep.tile([P, 2, T // 2], BF16, name="staged")
         runs = [slice(b * RUN, (b + 1) * RUN) for b in range(QUADS)]
+        for lane in range(2):
+            for cols in runs[0:2]:
+                nc.scalar.copy(staged[:, lane, cols], windows[lane][:, cols])
+            put_lane(nc.gpsimd.tensor_copy, lane, high)
+        for cols in runs[0:2]:
+            nc.scalar.copy(words[:, cols, 0:2], staged[:, :, cols].rearrange("p e c -> p c e"))
         for b, cols in enumerate(runs):
             put_lane(nc.vector.tensor_copy if b < 2 else nc.scalar.copy, LAST, cols)
         words_out = out_1[0].rearrange("p t l -> p (t l)").bitcast(I32)

@@ -27,7 +27,11 @@ RUN = T // QUADS
 BLOCKS = HALF // P
 STRIPE = 16
 TS_ROW = P - 1
-CUT = 352
+CUT = 256
+QUARTER = HALF // 2
+ROW = 5 * QUARTER
+W_LANES = (1, 2, 0, 3)
+LANES = (1, 2, 3, 0)
 ALIGN = 64
 
 
@@ -45,7 +49,7 @@ def tile_attend_gex_pl_tnh_x_kernel(tc, dyT, hT, ts, wm, offs, out_0, out_1, out
 
         banks = [psum.tile([P, HALF], F32, name="bank%d" % i) for i in range(8)]
         column_banks, spread_bank = banks[0:2], banks[2]
-        product_banks = [[banks[3], banks[4], banks[2], banks[5]], [banks[3], banks[0], banks[2], banks[1]]]
+        product_banks = [[banks[3], banks[4], banks[5], banks[2]], [banks[3], banks[4], banks[5], banks[0]]]
         first_turn_banks = banks[0:2] + banks[6:8]
 
         identity = keep.tile([P, P], F32, name="identity")
@@ -61,27 +65,21 @@ def tile_attend_gex_pl_tnh_x_kernel(tc, dyT, hT, ts, wm, offs, out_0, out_1, out
         dy_rows = dyT.rearrange("(p j) c -> p j c", j=PACK)
         h_planes = [keep.tile([P, T], F32, name="h_plane%d" % t) for t in range(PACK)]
         dy_planes = [keep.tile([P, T], F32, name="dy_plane%d" % t, tag="dy_plane%d" % t) for t in range(PACK)]
-        w_rows = wm[0].rearrange("(p j) d -> p j d", j=PACK)
-        w_raw = [keep.tile([P, 2, D], F32, name="w_raw%d" % u) for u in range(2)]
-        nc.sync.dma_start(h_planes[0][:], h_rows[:, 0, :])
-        for t in range(1, PACK):
+        w_raw = keep.tile([P, PACK, D], F32, name="w_raw")
+        for t in range(PACK):
             nc.sync.dma_start(h_planes[t][:], h_rows[:, t, :])
-            if t == LAST:
-                nc.sync.dma_start(w_raw[0][:], w_rows[:, 0:2, :])
-            nc.sync.dma_start(dy_planes[t - 1][:], dy_rows[:, t - 1, :])
-        nc.sync.dma_start(dy_planes[LAST][:], dy_rows[:, LAST, :])
-        nc.sync.dma_start(w_raw[1][:], w_rows[:, 2:PACK, :])
+        for t in range(PACK):
+            nc.sync.dma_start(dy_planes[t][:], dy_rows[:, t, :])
+        nc.sync.dma_start(w_raw[:], wm[0].rearrange("(p j) d -> p j d", j=PACK))
 
-        windows = []
+        windows = {}
 
-        def zeroed_window(slot):
-            window = keep.tile([P, T], F32, name="window%d" % len(windows), tag=slot)
-            nc.gpsimd.memset(window[:], 0.0)
-            windows.append(window)
+        def zeroed_window(lane, slot):
+            windows[lane] = keep.tile([P, T], F32, name="window%d" % lane, tag=slot)
+            nc.gpsimd.memset(windows[lane][:], 0.0)
 
-        zeroed_window("window0")
-        zeroed_window("window1")
-        zeroed_window("window2")
+        for lane in LANES[:LAST]:
+            zeroed_window(lane, "window%d" % lane)
 
         ts_listed = keep.tile([P, N], F32, name="ts_listed", tag="ts_listed")
         minus_ts_columns = [keep.tile([P, BLOCKS], F32, name="minus_ts_columns%d" % s) for s in range(2)]
@@ -102,105 +100,95 @@ def tile_attend_gex_pl_tnh_x_kernel(tc, dyT, hT, ts, wm, offs, out_0, out_1, out
 
         h_listed = keep.tile([P, PACK * N], F32, name="h_listed")
         factors = keep.tile([P, PACK * N], F32, name="factors", tag="ts_listed")
-        dz = keep.tile([P, PACK * N], F32, name="dz")
-        dz_planes = dz[:].rearrange("p (t c) -> p t c", t=PACK)
-        work = keep.tile([P, N], F32, name="work", align_bytes=ALIGN)
-        first_words = work[:].bitcast(BF16)
-        first_grouped = first_words.rearrange("p (c j) -> p c j", j=PACK)
+        low, high = slice(0, QUARTER), slice(QUARTER, HALF)
+        for t in range(PACK):
+            width = HALF if t == LAST else N
+            for first in range(0, N, width):
+                nc.vector.tensor_copy(part(h_listed, t, first, width), h_planes[t][:].indirect(entries(first, width)))
+            listed_h, factor = part(h_listed, t, 0, HALF), part(factors, t, 0, HALF)
+            first_square = part(factors, t, HALF, QUARTER)
+            nc.scalar.activation(first_square, listed_h[:, low], ACT.Square)
+            nc.scalar.activation(factor[:, high], listed_h[:, high], ACT.Square)
+            nc.scalar.activation(factor[:, low], first_square, ACT.Identity, bias=-1.0)
+            nc.scalar.activation(factor[:, high], factor[:, high], ACT.Identity, bias=-1.0)
+            nc.gpsimd.tensor_tensor(factor, factor, minus_ts_rows[:], ALU.mult)
+            nc.scalar.activation(part(factors, t, HALF, HALF), part(h_listed, t, HALF, HALF), ACT.Square)
+        late_factors = factors[:].rearrange("p (t c) -> p t c", t=PACK)[:, :, HALF:N]
+        nc.scalar.activation(late_factors, late_factors, ACT.Identity, bias=-1.0)
+
+        stage = keep.tile([P, PACK * ROW], F32, name="stage", align_bytes=ALIGN)
+        stage_rows = stage[:].rearrange("p (t c) -> p t c", t=PACK)
+        late_dy = stage_rows[:, :, 0:HALF]
+        late_products = stage_rows[:, :, ROW - HALF : ROW]
+        early_dz = keep.tile([P, 2, HALF], F32, name="early_dz", tag="early_dz")
+        third_dz = stage[:, HALF : 2 * HALF]
+        last_pairs = [stage[:, first : first + 2 * step].rearrange("p (e c) -> p e c", e=2)[:, :, low]
+                      for first, step in ((HALF, HALF), (HALF + QUARTER, ROW - HALF))]
+        w_grouped = stage[:, 2 * ROW + QUARTER : 3 * ROW].bitcast(BF16)
+
+        first_words = keep.tile([P, HALF * PACK], BF16, name="first_words", align_bytes=ALIGN)
+        first_grouped = first_words[:].rearrange("p (c j) -> p c j", j=PACK)
         dz_codes = [keep.tile([P, HALF], U32, name="dz_codes%d" % s, align_bytes=ALIGN) for s in range(2)]
         dz_scales = [keep.tile([P, HALF], U8, name="dz_scales%d" % s, align_bytes=ALIGN) for s in range(2)]
         w_codes = keep.tile([P, D], U32, name="w_codes", align_bytes=ALIGN)
         w_scales = keep.tile([P, D], U8, name="w_scales", align_bytes=ALIGN)
 
-        held_plane, last_factor = h_listed[:, 0:HALF], h_listed[:, HALF // 2 : HALF // 2 + HALF]
+        def gather_dy(target, t, first, count):
+            nc.vector.tensor_copy(target, dy_planes[t][:].indirect(entries(first, count)))
 
-        def gather_factors(t):
-            for s in range(2):
-                listed_h, factor = part(h_listed, t, s * HALF, HALF), part(factors, t, s * HALF, HALF)
-                nc.vector.tensor_copy(listed_h, h_planes[t][:].indirect(entries(s * HALF, HALF)))
-                if s == 1:
-                    nc.scalar.activation(factor, listed_h, ACT.Square)
-                    nc.scalar.activation(factor, factor, ACT.Identity, bias=-1.0)
-                elif t == LAST:
-                    nc.scalar.activation(factor, listed_h, ACT.Square)
-                    nc.vector.scalar_tensor_tensor(last_factor, factor, 1.0, spread_bank[:], ALU.subtract, ALU.mult)
-                else:
-                    low, high = slice(0, HALF // 2), slice(HALF // 2, HALF)
-                    first_square = part(factors, t, HALF, HALF // 2)
-                    nc.scalar.activation(first_square, listed_h[:, low], ACT.Square)
-                    nc.scalar.activation(factor[:, high], listed_h[:, high], ACT.Square)
-                    nc.scalar.activation(factor[:, low], first_square, ACT.Identity, bias=-1.0)
-                    nc.scalar.activation(factor[:, high], factor[:, high], ACT.Identity, bias=-1.0)
-                    nc.gpsimd.tensor_tensor(factor, factor, minus_ts_rows[:], ALU.mult)
+        def gather_times(target, t, first, count):
+            nc.vector.tensor_tensor(target, dy_planes[t][:].indirect(entries(first, count)), part(factors, t, first, count), ALU.mult)
 
-        def gather_dy(t, s, listed_dy):
-            nc.vector.tensor_copy(listed_dy, dy_planes[t][:].indirect(entries(s * HALF, HALF)))
-            nc.gpsimd.tensor_tensor(part(dz, t, s * HALF, HALF), listed_dy, part(factors, t, s * HALF, HALF), ALU.mult)
-
-        def gather_times(target, t, first, count, factor):
-            nc.vector.tensor_tensor(target, dy_planes[t][:].indirect(entries(first, count)), factor, ALU.mult)
-
-        def interleave_pair(t, first, count):
-            cols = slice(first, first + count)
-            nc.scalar.copy(first_grouped[:, cols, t : t + 2], dz_planes[:, t : t + 2, cols].rearrange("p e c -> p c e"))
-
-        def turn_second_half(t, plane):
-            for j in range(BLOCKS):
-                nc.tensor.transpose(first_turn_banks[j][:, t * P : (t + 1) * P], plane[:, j * P : (j + 1) * P], identity[:])
+        def interleave_pair(t, pair, cols):
+            nc.scalar.copy(first_grouped[:, cols, t : t + 2], pair.rearrange("p e c -> p c e"))
 
         def quantize_dz(s, words):
             nc.vector.quantize_mx(dz_codes[s][:].bitcast(E5M2), dz_scales[s][:], words)
 
-        w_grouped = keep.tile([P, D * PACK], BF16, name="w_grouped", align_bytes=ALIGN)
+        def regroup_w(place, lanes):
+            target = w_grouped.rearrange("p (t m j) -> p m j t", t=PACK, j=PACK)[:, :, :, place : place + 2]
+            nc.scalar.copy(target, w_raw[:].rearrange("p j (m t) -> p m j t", t=PACK)[:, :, :, lanes])
 
-        def regroup_w(u, lanes):
-            target = w_grouped[:].rearrange("p (t m j) -> p m j t", t=PACK, j=PACK)[:, :, 2 * u : 2 * u + 2, lanes]
-            nc.scalar.copy(target, w_raw[u][:].rearrange("p j (m t) -> p m j t", t=PACK)[:, :, :, lanes])
-
-        def quantize_w(lane, count):
-            regroup_w(1, slice(lane, lane + count))
-            cols = slice(lane * P, (lane + count) * P)
+        def quantize_w(place, count):
+            cols = slice(place * P, (place + count) * P)
             nc.vector.quantize_mx(w_codes[:, cols].bitcast(E4M3), w_scales[:, cols], w_grouped[:, PACK * cols.start : PACK * cols.stop])
 
-        def turn_pairs_back(rounded, bank, join_copy, target):
+        def turn_pairs_back(rounded, bank, target):
             pairs = bank[:, 0 : 2 * P]
             for u in range(2):
                 nc.tensor.transpose(pairs[:, u * P : (u + 1) * P], rounded[:].bitcast(F32)[:, u * P : (u + 1) * P], identity[:])
-            join_copy(target.rearrange("q (t u) -> q t u", u=2), pairs.rearrange("q (u t) -> q t u", u=2))
+            nc.scalar.copy(target.rearrange("q (t u) -> q t u", u=2), pairs.rearrange("q (u t) -> q t u", u=2))
 
-        gather_factors(0)
-        for t in range(2):
-            gather_factors(t + 1)
-            for s in range(2):
-                gather_dy(t, s, part(dz, 2, 0, HALF) if t + s == 2 else part(dz, t, s * HALF, HALF))
-            turn_second_half(t, part(dz, t, HALF, HALF))
-        zeroed_window("dy_plane1")
-        gather_factors(LAST)
-        interleave_pair(0, 0, HALF)
-        regroup_w(0, slice(0, PACK))
-        gather_times(part(dz, 2, 0, HALF), 2, 0, HALF, part(factors, 2, 0, HALF))
-        for first in (0, HALF // 2):
-            gather_times(part(dz, LAST, first, HALF // 2), LAST, first, HALF // 2, last_factor[:, first : first + HALF // 2])
-            interleave_pair(2, first, HALF // 2)
-        gather_times(held_plane, 2, HALF, HALF, part(factors, 2, HALF, HALF))
-        turn_second_half(2, held_plane)
-        quantize_dz(0, first_words)
-        quantize_w(2, 1)
-        last_plane = work[:, 0:HALF]
-        gather_times(last_plane, LAST, HALF, HALF, part(factors, LAST, HALF, HALF))
-        quantize_w(0, 2)
-        quantize_w(LAST, 1)
-
-        def multiply(w, s, bank):
-            cols = slice(w * P, (w + 1) * P)
-            nc.tensor.matmul_mx(bank[:], lhsT=w_codes[:, cols].bitcast(E4M3), lhsT_scale=w_scales[:, cols],
-                                rhs=dz_codes[s][:].bitcast(E5M2), rhs_scale=dz_scales[s][:], start=True, stop=True)
+        gather_dy(early_dz[:, 0, :], 0, 0, HALF)
+        nc.gpsimd.tensor_tensor(early_dz[:, 0, :], early_dz[:, 0, :], part(factors, 0, 0, HALF), ALU.mult)
+        gather_dy(late_dy[:, 0, :], 0, HALF, HALF)
+        for cols in (low, high):
+            gather_dy(early_dz[:, 1, cols], 1, cols.start, QUARTER)
+            nc.gpsimd.tensor_tensor(early_dz[:, 1, cols], early_dz[:, 1, cols], part(factors, 1, cols.start, QUARTER), ALU.mult)
+            interleave_pair(0, early_dz[:, :, cols], cols)
+        gather_dy(late_dy[:, 1, low], 1, HALF, QUARTER)
+        zeroed_window(LANES[LAST], "early_dz")
+        gather_times(third_dz, 2, 0, HALF)
+        for pair, cols in zip(last_pairs, (low, high)):
+            gather_times(pair[:, 1, :], LAST, cols.start, QUARTER)
+            interleave_pair(2, pair, cols)
+        gather_dy(late_dy[:, LAST, :], LAST, HALF, HALF)
+        quantize_dz(0, first_words[:])
+        gather_dy(late_dy[:, 1, high], 1, HALF + QUARTER, QUARTER)
+        regroup_w(0, slice(1, 3))
+        quantize_w(0, 1)
+        quantize_w(1, 1)
+        gather_dy(late_dy[:, 2, :], 2, HALF, HALF)
+        regroup_w(2, slice(0, PACK, LAST))
+        quantize_w(2, 2)
 
         out_lanes = out_0.rearrange("(p j) c -> p j c", j=PACK)
 
         def product(lane, s):
-            bank = product_banks[s][lane]
-            multiply(lane, s, bank)
+            place = W_LANES.index(lane)
+            bank, cols = product_banks[s][LANES.index(lane)], slice(place * P, (place + 1) * P)
+            nc.tensor.matmul_mx(bank[:], lhsT=w_codes[:, cols].bitcast(E4M3), lhsT_scale=w_scales[:, cols],
+                                rhs=dz_codes[s][:].bitcast(E5M2), rhs_scale=dz_scales[s][:], start=True, stop=True)
             return bank
 
         def scatter(lane, first, pieces, dx):
@@ -215,47 +203,51 @@ def tile_attend_gex_pl_tnh_x_kernel(tc, dyT, hT, ts, wm, offs, out_0, out_1, out
         def source(name, count, slot=None):
             return keep.tile([P, count], F32, name=name, tag=slot or name, align_bytes=ALIGN)[:]
 
-        scatter(2, 0, [product(2, 0)[:]], source("dx2", HALF))
-        scatter(0, 0, [product(0, 0)[:]], source("dx0", HALF))
-        cut_bank = product(1, 0)
+        for lane in LANES[:2]:
+            scatter(lane, 0, [product(lane, 0)[:]], source("dx%d" % lane, HALF))
+        cut_bank = product(3, 0)
+        scatter(3, 0, [cut_bank[:, 0:CUT]], source("dx3", CUT))
+        last_first_bank = product(0, 0)
 
-        turn_second_half(LAST, last_plane)
         second_words = keep.tile([P, PACK * HALF], BF16, name="second_words", tag="second_words", align_bytes=ALIGN)
         for j in range(BLOCKS):
+            cols = slice(j * P, (j + 1) * P)
+            nc.gpsimd.tensor_tensor(late_products[:, :, cols], late_dy[:, :, cols], late_factors[:, :, cols], ALU.mult)
+            for t in range(PACK):
+                nc.tensor.transpose(first_turn_banks[j][:, t * P : (t + 1) * P], late_products[:, t, cols], identity[:])
             rounded = keep.tile([P, HALF], BF16, name="rounded_dz%d" % j, tag="rounded%d" % j, align_bytes=ALIGN)
             nc.scalar.activation(rounded[:].rearrange("c (u q e) -> c u q e", u=2, e=2), first_turn_banks[j][:].rearrange("c (u e q) -> c u q e", u=2, e=2),
                                  ACT.Copy, scale=minus_ts_columns[1][:, j : j + 1])
-            turn_pairs_back(rounded, first_turn_banks[j], nc.scalar.copy, second_words[:].bitcast(F32)[:, 2 * P * j : 2 * P * (j + 1)])
+            turn_pairs_back(rounded, first_turn_banks[j], second_words[:].bitcast(F32)[:, 2 * P * j : 2 * P * (j + 1)])
         quantize_dz(1, second_words[:])
-        scatter(1, 0, [cut_bank[:, 0:CUT]], source("dx1", CUT, "rounded%d" % (BLOCKS - 1)))
-        last_first_bank = product(LAST, 0)
-        late_dx = source("late_dx", 2 * N - CUT, "second_words")
+        scatter(3, CUT, [cut_bank[:, CUT:HALF]], source("dx_cut", HALF - CUT, "rounded%d" % (BLOCKS - 1)))
+        late_dx = source("late_dx", 2 * N, "second_words")
         last_dx = late_dx[:, 0:N]
-        scatter(2, HALF, [product(2, 1)[:]], last_dx[:, HALF:N])
-        scatter(0, HALF, [product(0, 1)[:]], source("dx0_second", HALF))
-        scatter(1, CUT, [cut_bank[:, CUT:HALF], product(1, 1)[:]], late_dx[:, N : 2 * N - CUT])
+        scatter(1, HALF, [product(1, 1)[:]], last_dx[:, HALF:N])
+        scatter(2, HALF, [product(2, 1)[:]], late_dx[:, N : N + HALF])
+        scatter(3, HALF, [product(3, 1)[:]], late_dx[:, N + HALF : 2 * N])
 
         words = keep.tile([P, T, PACK], BF16, name="words", align_bytes=ALIGN)
         codes = keep.tile([P, T], U32, name="codes", align_bytes=ALIGN)
         scales = keep.tile([P, T], U8, name="scales", align_bytes=ALIGN)
-        low, high = slice(0, T // 2), slice(T // 2, T)
+        low_tokens, high_tokens = slice(0, T // 2), slice(T // 2, T)
 
         def put_lane(copy, lane, cols):
             copy(words[:, cols, lane], windows[lane][:, cols])
 
-        put_lane(nc.scalar.copy, 2, low)
-        scatter(LAST, 0, [last_first_bank[:], product(LAST, 1)[:]], last_dx)
-        put_lane(nc.scalar.copy, 2, high)
+        put_lane(nc.scalar.copy, 1, low_tokens)
+        scatter(0, 0, [last_first_bank[:], product(0, 1)[:]], last_dx)
+        put_lane(nc.scalar.copy, 1, high_tokens)
         staged = keep.tile([P, 2, T // 2], BF16, name="staged")
         runs = [slice(b * RUN, (b + 1) * RUN) for b in range(QUADS)]
-        for lane in range(2):
+        for lane in (2, 3):
             for cols in runs[0:2]:
-                nc.scalar.copy(staged[:, lane, cols], windows[lane][:, cols])
-            put_lane(nc.gpsimd.tensor_copy, lane, high)
+                nc.scalar.copy(staged[:, lane - 2, cols], windows[lane][:, cols])
+            put_lane(nc.gpsimd.tensor_copy, lane, high_tokens)
         for cols in runs[0:2]:
-            nc.scalar.copy(words[:, cols, 0:2], staged[:, :, cols].rearrange("p e c -> p c e"))
+            nc.scalar.copy(words[:, cols, 2:PACK], staged[:, :, cols].rearrange("p e c -> p c e"))
         for b, cols in enumerate(runs):
-            put_lane(nc.vector.tensor_copy if b < 2 else nc.scalar.copy, LAST, cols)
+            put_lane(nc.vector.tensor_copy if b < 2 else nc.scalar.copy, 0, cols)
         words_out = out_1[0].rearrange("p t l -> p (t l)").bitcast(I32)
         for cols in runs:
             nc.vector.quantize_mx(codes[:, cols].bitcast(E4M3), scales[:, cols], words[:, cols, :].rearrange("p c j -> p (c j)"))

@@ -75,7 +75,7 @@ def tile_attend_gex_pl_tnh_x_kernel(tc, dyT, hT, ts, wm, offs, out_0, out_1, out
         windows = {}
 
         def zeroed_window(lane, slot):
-            windows[lane] = keep.tile([P, T], F32, name="window%d" % lane, tag=slot)
+            windows[lane] = keep.tile([P, T], F32, name="window%d" % lane, tag=slot, align_bytes=ALIGN)
             nc.gpsimd.memset(windows[lane][:], 0.0)
 
         for lane in LANES[:LAST]:
@@ -162,12 +162,9 @@ def tile_attend_gex_pl_tnh_x_kernel(tc, dyT, hT, ts, wm, offs, out_0, out_1, out
         gather_dy(early_dz[:, 0, :], 0, 0, HALF)
         nc.gpsimd.tensor_tensor(early_dz[:, 0, :], early_dz[:, 0, :], part(factors, 0, 0, HALF), ALU.mult)
         gather_dy(late_dy[:, 0, :], 0, HALF, HALF)
-        for cols in (low, high):
-            gather_dy(early_dz[:, 1, cols], 1, cols.start, QUARTER)
-            nc.gpsimd.tensor_tensor(early_dz[:, 1, cols], early_dz[:, 1, cols], part(factors, 1, cols.start, QUARTER), ALU.mult)
-            interleave_pair(0, early_dz[:, :, cols], cols)
         gather_dy(late_dy[:, 1, low], 1, HALF, QUARTER)
-        zeroed_window(LANES[LAST], "early_dz")
+        gather_times(early_dz[:, 1, :], 1, 0, HALF)
+        interleave_pair(0, early_dz, slice(0, HALF))
         gather_times(third_dz, 2, 0, HALF)
         for pair, cols in zip(last_pairs, (low, high)):
             gather_times(pair[:, 1, :], LAST, cols.start, QUARTER)
@@ -221,6 +218,7 @@ def tile_attend_gex_pl_tnh_x_kernel(tc, dyT, hT, ts, wm, offs, out_0, out_1, out
             turn_pairs_back(rounded, first_turn_banks[j], second_words[:].bitcast(F32)[:, 2 * P * j : 2 * P * (j + 1)])
         quantize_dz(1, second_words[:])
         scatter(3, CUT, [cut_bank[:, CUT:HALF]], source("dx_cut", HALF - CUT, "rounded%d" % (BLOCKS - 1)))
+        zeroed_window(LANES[LAST], "rounded%d" % (BLOCKS - 1))
         late_dx = source("late_dx", 2 * N, "second_words")
         last_dx = late_dx[:, 0:N]
         scatter(1, HALF, [product(1, 1)[:]], last_dx[:, HALF:N])

@@ -169,9 +169,9 @@ def tile_attend_gex_pl_tnh_x_kernel(tc, dyT, hT, ts, wm, offs, out_0, out_1, out
         for pair, cols in zip(last_pairs, (low, high)):
             gather_times(pair[:, 1, :], LAST, cols.start, QUARTER)
             interleave_pair(2, pair, cols)
-        gather_dy(late_dy[:, LAST, :], LAST, HALF, HALF)
+        gather_times(late_dy[:, LAST, :], LAST, HALF, HALF)
         quantize_dz(0, first_words[:])
-        gather_dy(late_dy[:, 1, high], 1, HALF + QUARTER, QUARTER)
+        gather_times(late_dy[:, 1, high], 1, HALF + QUARTER, QUARTER)
         regroup_w(0, slice(1, 3))
         quantize_w(0, 1)
         quantize_w(1, 1)
@@ -207,18 +207,20 @@ def tile_attend_gex_pl_tnh_x_kernel(tc, dyT, hT, ts, wm, offs, out_0, out_1, out
         last_first_bank = product(0, 0)
 
         second_words = keep.tile([P, PACK * HALF], BF16, name="second_words", tag="second_words", align_bytes=ALIGN)
-        for j in range(BLOCKS):
+        for quarter, planes in ((high, slice(0, LAST, 2)), (low, slice(0, LAST))):
+            nc.gpsimd.tensor_tensor(late_products[:, planes, quarter], late_dy[:, planes, quarter], late_factors[:, planes, quarter], ALU.mult)
+        for j in (2, 3, 0, 1):
             cols = slice(j * P, (j + 1) * P)
-            nc.gpsimd.tensor_tensor(late_products[:, :, cols], late_dy[:, :, cols], late_factors[:, :, cols], ALU.mult)
             for t in range(PACK):
-                nc.tensor.transpose(first_turn_banks[j][:, t * P : (t + 1) * P], late_products[:, t, cols], identity[:])
+                whole = late_dy if t == LAST or (t == 1 and j >= 2) else late_products
+                nc.tensor.transpose(first_turn_banks[j][:, t * P : (t + 1) * P], whole[:, t, cols], identity[:])
             rounded = keep.tile([P, HALF], BF16, name="rounded_dz%d" % j, tag="rounded%d" % j, align_bytes=ALIGN)
             nc.scalar.activation(rounded[:].rearrange("c (u q e) -> c u q e", u=2, e=2), first_turn_banks[j][:].rearrange("c (u e q) -> c u q e", u=2, e=2),
                                  ACT.Copy, scale=minus_ts_columns[1][:, j : j + 1])
             turn_pairs_back(rounded, first_turn_banks[j], second_words[:].bitcast(F32)[:, 2 * P * j : 2 * P * (j + 1)])
         quantize_dz(1, second_words[:])
-        scatter(3, CUT, [cut_bank[:, CUT:HALF]], source("dx_cut", HALF - CUT, "rounded%d" % (BLOCKS - 1)))
-        zeroed_window(LANES[LAST], "rounded%d" % (BLOCKS - 1))
+        scatter(3, CUT, [cut_bank[:, CUT:HALF]], source("dx_cut", HALF - CUT, "rounded1"))
+        zeroed_window(LANES[LAST], "rounded1")
         late_dx = source("late_dx", 2 * N, "second_words")
         last_dx = late_dx[:, 0:N]
         scatter(1, HALF, [product(1, 1)[:]], last_dx[:, HALF:N])

@@ -30,8 +30,7 @@ TS_ROW = P - 1
 CUT = 256
 QUARTER = HALF // 2
 ROW = 5 * QUARTER
-W_LANES = (1, 2, 0, 3)
-LANES = (1, 2, 3, 0)
+LANES = (0, 2, 3, 1)
 ALIGN = 64
 
 
@@ -172,18 +171,17 @@ def tile_attend_gex_pl_tnh_x_kernel(tc, dyT, hT, ts, wm, offs, out_0, out_1, out
         gather_times(late_dy[:, LAST, :], LAST, HALF, HALF)
         quantize_dz(0, first_words[:])
         gather_times(late_dy[:, 1, high], 1, HALF + QUARTER, QUARTER)
-        regroup_w(0, slice(1, 3))
+        regroup_w(0, slice(0, 2))
         quantize_w(0, 1)
         quantize_w(1, 1)
         gather_dy(late_dy[:, 2, :], 2, HALF, HALF)
-        regroup_w(2, slice(0, PACK, LAST))
+        regroup_w(2, slice(2, PACK))
         quantize_w(2, 2)
 
         out_lanes = out_0.rearrange("(p j) c -> p j c", j=PACK)
 
         def product(lane, s):
-            place = W_LANES.index(lane)
-            bank, cols = product_banks[s][LANES.index(lane)], slice(place * P, (place + 1) * P)
+            bank, cols = product_banks[s][LANES.index(lane)], slice(lane * P, (lane + 1) * P)
             nc.tensor.matmul_mx(bank[:], lhsT=w_codes[:, cols].bitcast(E4M3), lhsT_scale=w_scales[:, cols],
                                 rhs=dz_codes[s][:].bitcast(E5M2), rhs_scale=dz_scales[s][:], start=True, stop=True)
             return bank
@@ -204,7 +202,7 @@ def tile_attend_gex_pl_tnh_x_kernel(tc, dyT, hT, ts, wm, offs, out_0, out_1, out
             scatter(lane, 0, [product(lane, 0)[:]], source("dx%d" % lane, HALF))
         cut_bank = product(3, 0)
         scatter(3, 0, [cut_bank[:, 0:CUT]], source("dx3", CUT))
-        last_first_bank = product(0, 0)
+        last_first_bank = product(1, 0)
 
         second_words = keep.tile([P, PACK * HALF], BF16, name="second_words", tag="second_words", align_bytes=ALIGN)
         for quarter, planes in ((high, slice(0, LAST, 2)), (low, slice(0, LAST))):
@@ -223,21 +221,21 @@ def tile_attend_gex_pl_tnh_x_kernel(tc, dyT, hT, ts, wm, offs, out_0, out_1, out
         zeroed_window(LANES[LAST], "rounded1")
         late_dx = source("late_dx", 2 * N, "second_words")
         last_dx = late_dx[:, 0:N]
-        scatter(1, HALF, [product(1, 1)[:]], last_dx[:, HALF:N])
+        scatter(0, HALF, [product(0, 1)[:]], last_dx[:, HALF:N])
         scatter(2, HALF, [product(2, 1)[:]], late_dx[:, N : N + HALF])
         scatter(3, HALF, [product(3, 1)[:]], late_dx[:, N + HALF : 2 * N])
 
         words = keep.tile([P, T, PACK], BF16, name="words", align_bytes=ALIGN)
         codes = keep.tile([P, T], U32, name="codes", align_bytes=ALIGN)
-        scales = keep.tile([P, T], U8, name="scales", align_bytes=ALIGN)
+        scales = keep.tile([P, RUN], U8, name="scales", align_bytes=ALIGN)
         low_tokens, high_tokens = slice(0, T // 2), slice(T // 2, T)
 
         def put_lane(copy, lane, cols):
             copy(words[:, cols, lane], windows[lane][:, cols])
 
-        put_lane(nc.scalar.copy, 1, low_tokens)
-        scatter(0, 0, [last_first_bank[:], product(0, 1)[:]], last_dx)
-        put_lane(nc.scalar.copy, 1, high_tokens)
+        put_lane(nc.scalar.copy, 0, low_tokens)
+        scatter(1, 0, [last_first_bank[:], product(1, 1)[:]], last_dx)
+        put_lane(nc.scalar.copy, 0, high_tokens)
         staged = keep.tile([P, 2, T // 2], BF16, name="staged")
         runs = [slice(b * RUN, (b + 1) * RUN) for b in range(QUADS)]
         for lane in (2, 3):
@@ -247,12 +245,14 @@ def tile_attend_gex_pl_tnh_x_kernel(tc, dyT, hT, ts, wm, offs, out_0, out_1, out
         for cols in runs[0:2]:
             nc.scalar.copy(words[:, cols, 2:PACK], staged[:, :, cols].rearrange("p e c -> p c e"))
         for b, cols in enumerate(runs):
-            put_lane(nc.vector.tensor_copy if b < 2 else nc.scalar.copy, 0, cols)
+            put_lane(nc.vector.tensor_copy if b < 2 else nc.scalar.copy, 1, cols)
         words_out = out_1[0].rearrange("p t l -> p (t l)").bitcast(I32)
-        for cols in runs:
-            nc.vector.quantize_mx(codes[:, cols].bitcast(E4M3), scales[:, cols], words[:, cols, :].rearrange("p c j -> p (c j)"))
+        for b, cols in enumerate(runs):
+            for piece in (low, high):
+                tokens = slice(cols.start + piece.start, cols.start + piece.stop)
+                nc.vector.quantize_mx(codes[:, tokens].bitcast(E4M3), scales[PACK * b : P, piece], words[:, tokens, :].rearrange("p c j -> p (c j)"))
             nc.sync.dma_start(words_out[:, cols], codes[:, cols].bitcast(I32))
         scales_out = out_2[0].bitcast(I32)
         for q in range(QUADS):
             queue = nc.sync if q == LAST else nc.scalar
-            queue.dma_start(scales_out[PACK * q : PACK * (q + 1), :], scales[QUAD * q : QUAD * q + PACK, :].bitcast(I32))
+            queue.dma_start(scales_out[PACK * q : PACK * (q + 1), :].rearrange("r (b c) -> b r c", b=QUADS), scales[QUAD * q : QUAD * q + QUADS * PACK, :].bitcast(I32))

@@ -62,7 +62,7 @@ def tile_attend_gex_pl_tnh_x_kernel(tc, dyT, hT, ts, wm, offs, out_0, out_1, out
 
         h_rows = hT.rearrange("(p j) c -> p j c", j=PACK)
         dy_rows = dyT.rearrange("(p j) c -> p j c", j=PACK)
-        h_planes = [keep.tile([P, T], F32, name="h_plane%d" % t) for t in range(PACK)]
+        h_planes = [keep.tile([P, T], F32, name="h_plane%d" % t, tag="h_plane%d" % t, align_bytes=ALIGN) for t in range(PACK)]
         dy_planes = [keep.tile([P, T], F32, name="dy_plane%d" % t, tag="dy_plane%d" % t) for t in range(PACK)]
         w_raw = keep.tile([P, PACK, D], F32, name="w_raw")
         for t in range(PACK):
@@ -77,7 +77,7 @@ def tile_attend_gex_pl_tnh_x_kernel(tc, dyT, hT, ts, wm, offs, out_0, out_1, out
             windows[lane] = keep.tile([P, T], F32, name="window%d" % lane, tag=slot, align_bytes=ALIGN)
             nc.gpsimd.memset(windows[lane][:], 0.0)
 
-        for lane in LANES[:LAST]:
+        for lane in LANES[:2]:
             zeroed_window(lane, "window%d" % lane)
 
         ts_listed = keep.tile([P, N], F32, name="ts_listed", tag="ts_listed")
@@ -100,8 +100,14 @@ def tile_attend_gex_pl_tnh_x_kernel(tc, dyT, hT, ts, wm, offs, out_0, out_1, out
         h_listed = keep.tile([P, PACK * N], F32, name="h_listed")
         factors = keep.tile([P, PACK * N], F32, name="factors", tag="ts_listed")
         low, high = slice(0, QUARTER), slice(QUARTER, HALF)
+        ts_factors = [part(factors, t, 0, HALF) for t in range(PACK)]
+
+        def times_ts(t, target):
+            nc.gpsimd.tensor_tensor(target, part(factors, t, 0, HALF), minus_ts_rows[:], ALU.mult)
+            ts_factors[t] = target
+
         for t in range(PACK):
-            width = HALF if t == LAST else N
+            width = N if t % 2 else HALF
             for first in range(0, N, width):
                 nc.vector.tensor_copy(part(h_listed, t, first, width), h_planes[t][:].indirect(entries(first, width)))
             listed_h, factor = part(h_listed, t, 0, HALF), part(factors, t, 0, HALF)
@@ -110,15 +116,21 @@ def tile_attend_gex_pl_tnh_x_kernel(tc, dyT, hT, ts, wm, offs, out_0, out_1, out
             nc.scalar.activation(factor[:, high], listed_h[:, high], ACT.Square)
             nc.scalar.activation(factor[:, low], first_square, ACT.Identity, bias=-1.0)
             nc.scalar.activation(factor[:, high], factor[:, high], ACT.Identity, bias=-1.0)
-            nc.gpsimd.tensor_tensor(factor, factor, minus_ts_rows[:], ALU.mult)
             nc.scalar.activation(part(factors, t, HALF, HALF), part(h_listed, t, HALF, HALF), ACT.Square)
+            if t == 0:
+                times_ts(0, factor)
+            elif t == 1:
+                zeroed_window(LANES[2], "h_plane1")
+            elif t == 2:
+                times_ts(1, keep.tile([P, HALF], F32, name="held_factor", tag="h_plane2", align_bytes=ALIGN)[:])
+                times_ts(2, factor)
         late_factors = factors[:].rearrange("p (t c) -> p t c", t=PACK)[:, :, HALF:N]
         nc.scalar.activation(late_factors, late_factors, ACT.Identity, bias=-1.0)
 
         stage = keep.tile([P, PACK * ROW], F32, name="stage", align_bytes=ALIGN)
         stage_rows = stage[:].rearrange("p (t c) -> p t c", t=PACK)
         late_dy = stage_rows[:, :, 0:HALF]
-        late_products = stage_rows[:, :, ROW - HALF : ROW]
+        late_products = [stage[:, 2 * ROW + HALF : 2 * ROW + N], stage[:, 2 * ROW + N : 3 * ROW]]
         early_dz = keep.tile([P, 2, HALF], F32, name="early_dz", tag="early_dz")
         third_dz = stage[:, HALF : 2 * HALF]
         last_pairs = [stage[:, first : first + 2 * step].rearrange("p (e c) -> p e c", e=2)[:, :, low]
@@ -136,7 +148,7 @@ def tile_attend_gex_pl_tnh_x_kernel(tc, dyT, hT, ts, wm, offs, out_0, out_1, out
             nc.vector.tensor_copy(target, dy_planes[t][:].indirect(entries(first, count)))
 
         def gather_times(target, t, first, count):
-            nc.vector.tensor_tensor(target, dy_planes[t][:].indirect(entries(first, count)), part(factors, t, first, count), ALU.mult)
+            nc.vector.tensor_tensor(target, dy_planes[t][:].indirect(entries(first, count)), ts_factors[t][:, first : first + count] if first < HALF else part(factors, t, first, count), ALU.mult)
 
         def interleave_pair(t, pair, cols):
             nc.scalar.copy(first_grouped[:, cols, t : t + 2], pair.rearrange("p e c -> p c e"))
@@ -158,8 +170,8 @@ def tile_attend_gex_pl_tnh_x_kernel(tc, dyT, hT, ts, wm, offs, out_0, out_1, out
                 nc.tensor.transpose(pairs[:, u * P : (u + 1) * P], rounded[:].bitcast(F32)[:, u * P : (u + 1) * P], identity[:])
             nc.scalar.copy(target.rearrange("q (t u) -> q t u", u=2), pairs.rearrange("q (u t) -> q t u", u=2))
 
-        gather_dy(early_dz[:, 0, :], 0, 0, HALF)
-        nc.gpsimd.tensor_tensor(early_dz[:, 0, :], early_dz[:, 0, :], part(factors, 0, 0, HALF), ALU.mult)
+        gather_times(early_dz[:, 0, :], 0, 0, HALF)
+        times_ts(LAST, ts_factors[0])
         gather_dy(late_dy[:, 0, :], 0, HALF, HALF)
         gather_dy(late_dy[:, 1, low], 1, HALF, QUARTER)
         gather_times(early_dz[:, 1, :], 1, 0, HALF)
@@ -174,7 +186,7 @@ def tile_attend_gex_pl_tnh_x_kernel(tc, dyT, hT, ts, wm, offs, out_0, out_1, out
         regroup_w(0, slice(0, 2))
         quantize_w(0, 1)
         quantize_w(1, 1)
-        gather_dy(late_dy[:, 2, :], 2, HALF, HALF)
+        gather_times(late_dy[:, 2, :], 2, HALF, HALF)
         regroup_w(2, slice(2, PACK))
         quantize_w(2, 2)
 
@@ -205,13 +217,13 @@ def tile_attend_gex_pl_tnh_x_kernel(tc, dyT, hT, ts, wm, offs, out_0, out_1, out
         last_first_bank = product(1, 0)
 
         second_words = keep.tile([P, PACK * HALF], BF16, name="second_words", tag="second_words", align_bytes=ALIGN)
-        for quarter, planes in ((high, slice(0, LAST, 2)), (low, slice(0, LAST))):
-            nc.gpsimd.tensor_tensor(late_products[:, planes, quarter], late_dy[:, planes, quarter], late_factors[:, planes, quarter], ALU.mult)
+        for t, cols in ((0, slice(0, HALF)), (1, low)):
+            nc.gpsimd.tensor_tensor(late_products[t], late_dy[:, t, cols], late_factors[:, t, cols], ALU.mult)
         for j in (2, 3, 0, 1):
             cols = slice(j * P, (j + 1) * P)
             for t in range(PACK):
-                whole = late_dy if t == LAST or (t == 1 and j >= 2) else late_products
-                nc.tensor.transpose(first_turn_banks[j][:, t * P : (t + 1) * P], whole[:, t, cols], identity[:])
+                whole = late_products[t] if t == 0 or (t == 1 and j < 2) else late_dy[:, t, :]
+                nc.tensor.transpose(first_turn_banks[j][:, t * P : (t + 1) * P], whole[:, cols], identity[:])
             rounded = keep.tile([P, HALF], BF16, name="rounded_dz%d" % j, tag="rounded%d" % j, align_bytes=ALIGN)
             nc.scalar.activation(rounded[:].rearrange("c (u q e) -> c u q e", u=2, e=2), first_turn_banks[j][:].rearrange("c (u e q) -> c u q e", u=2, e=2),
                                  ACT.Copy, scale=minus_ts_columns[1][:, j : j + 1])

@@ -48,7 +48,7 @@ def tile_attend_gex_pl_tnh_x_kernel(tc, dyT, hT, ts, wm, offs, out_0, out_1, out
 
         banks = [psum.tile([P, HALF], F32, name="bank%d" % i) for i in range(8)]
         column_banks, spread_bank = banks[0:2], banks[2]
-        product_banks = [[banks[3], banks[4], banks[5], banks[2]], [banks[3], banks[4], banks[5], banks[0]]]
+        product_banks = [[banks[3], banks[4], banks[5], banks[2]], [banks[3], banks[4], banks[1], banks[0]]]
         first_turn_banks = banks[0:2] + banks[6:8]
 
         identity = keep.tile([P, P], F32, name="identity")
@@ -63,7 +63,7 @@ def tile_attend_gex_pl_tnh_x_kernel(tc, dyT, hT, ts, wm, offs, out_0, out_1, out
         h_rows = hT.rearrange("(p j) c -> p j c", j=PACK)
         dy_rows = dyT.rearrange("(p j) c -> p j c", j=PACK)
         h_planes = [keep.tile([P, T], F32, name="h_plane%d" % t, tag="h_plane%d" % t, align_bytes=ALIGN) for t in range(PACK)]
-        dy_planes = [keep.tile([P, T], F32, name="dy_plane%d" % t, tag="dy_plane%d" % t) for t in range(PACK)]
+        dy_planes = [keep.tile([P, T], F32, name="dy_plane%d" % t, tag="dy_plane%d" % t, align_bytes=ALIGN) for t in range(PACK)]
         w_raw = keep.tile([P, PACK, D], F32, name="w_raw")
         for t in range(PACK):
             nc.sync.dma_start(h_planes[t][:], h_rows[:, t, :])
@@ -80,7 +80,7 @@ def tile_attend_gex_pl_tnh_x_kernel(tc, dyT, hT, ts, wm, offs, out_0, out_1, out
         for lane in LANES[:2]:
             zeroed_window(lane, "window%d" % lane)
 
-        ts_listed = keep.tile([P, N], F32, name="ts_listed", tag="ts_listed")
+        ts_listed = keep.tile([P, N], F32, name="ts_listed", tag="ts_listed", align_bytes=ALIGN)
         minus_ts_columns = [keep.tile([P, BLOCKS], F32, name="minus_ts_columns%d" % s) for s in range(2)]
         minus_ts_rows = keep.tile([P, HALF], F32, name="minus_ts_rows", tag="minus_ts_rows")
         for s in range(2):
@@ -89,6 +89,8 @@ def tile_attend_gex_pl_tnh_x_kernel(tc, dyT, hT, ts, wm, offs, out_0, out_1, out
                 first = s * HALF + c * P
                 nc.tensor.transpose(column_banks[s][:, c * P : (c + 1) * P], ts_listed[:, first : first + P], identity[:])
             nc.scalar.activation(minus_ts_columns[s][:], column_banks[s][:, TS_ROW:HALF:P], ACT.Copy, scale=-1.0)
+        ts_columns = keep.tile([P, BLOCKS], F32, name="ts_columns")
+        nc.scalar.copy(ts_columns[:], column_banks[0][:, TS_ROW:HALF:P])
         for c in range(BLOCKS):
             column = minus_ts_columns[0][:, c : c + 1].to_broadcast([P, P])
             nc.tensor.transpose(spread_bank[:, c * P : (c + 1) * P], column, identity[:])
@@ -98,36 +100,49 @@ def tile_attend_gex_pl_tnh_x_kernel(tc, dyT, hT, ts, wm, offs, out_0, out_1, out
             return tile[:, t * N + first : t * N + first + count]
 
         h_listed = keep.tile([P, PACK * N], F32, name="h_listed")
-        factors = keep.tile([P, PACK * N], F32, name="factors", tag="ts_listed")
+        factors = keep.tile([P, PACK * N], F32, name="factors", tag="ts_listed", align_bytes=ALIGN)
         low, high = slice(0, QUARTER), slice(QUARTER, HALF)
-        ts_factors = [part(factors, t, 0, HALF) for t in range(PACK)]
+        late_factors = factors[:].rearrange("p (t c) -> p t c", t=PACK)[:, :, HALF:N]
+        held_factors = {}
 
-        def times_ts(t, target):
-            nc.gpsimd.tensor_tensor(target, part(factors, t, 0, HALF), minus_ts_rows[:], ALU.mult)
-            ts_factors[t] = target
+        def times_ts(t, cols, target):
+            nc.gpsimd.tensor_tensor(target, part(factors, t, 0, HALF)[:, cols], minus_ts_rows[:, cols], ALU.mult)
 
         for t in range(PACK):
-            width = N if t % 2 else HALF
+            width = N if t else HALF
             for first in range(0, N, width):
                 nc.vector.tensor_copy(part(h_listed, t, first, width), h_planes[t][:].indirect(entries(first, width)))
+            if t >= 2:
+                held_factors[t - 1] = keep.tile([P, QUARTER], F32, name="held_factor%d" % t, tag="h_plane%d" % t, align_bytes=ALIGN)[:]
+                times_ts(t - 1, high, held_factors[t - 1])
             listed_h, factor = part(h_listed, t, 0, HALF), part(factors, t, 0, HALF)
-            first_square = part(factors, t, HALF, QUARTER)
-            nc.scalar.activation(first_square, listed_h[:, low], ACT.Square)
-            nc.scalar.activation(factor[:, high], listed_h[:, high], ACT.Square)
-            nc.scalar.activation(factor[:, low], first_square, ACT.Identity, bias=-1.0)
-            nc.scalar.activation(factor[:, high], factor[:, high], ACT.Identity, bias=-1.0)
+            if t < LAST:
+                first_square = part(factors, t, HALF, QUARTER)
+                nc.scalar.activation(first_square, listed_h[:, low], ACT.Square)
+                nc.scalar.activation(factor[:, high], listed_h[:, high], ACT.Square)
+                nc.scalar.activation(factor[:, low], first_square, ACT.Identity, bias=-1.0)
+                nc.scalar.activation(factor[:, high], factor[:, high], ACT.Identity, bias=-1.0)
+                cols = low if t else slice(0, HALF)
+                times_ts(t, cols, factor[:, cols])
+            else:
+                nc.scalar.activation(factor, listed_h, ACT.Square)
             nc.scalar.activation(part(factors, t, HALF, HALF), part(h_listed, t, HALF, HALF), ACT.Square)
             if t == 0:
-                times_ts(0, factor)
-            elif t == 1:
-                zeroed_window(LANES[2], "h_plane1")
-            elif t == 2:
-                times_ts(1, keep.tile([P, HALF], F32, name="held_factor", tag="h_plane2", align_bytes=ALIGN)[:])
-                times_ts(2, factor)
-        late_factors = factors[:].rearrange("p (t c) -> p t c", t=PACK)[:, :, HALF:N]
-        nc.scalar.activation(late_factors, late_factors, ACT.Identity, bias=-1.0)
+                nc.scalar.activation(late_factors[:, 0, :], late_factors[:, 0, :], ACT.Identity, bias=-1.0)
+        first_words = keep.tile([P, HALF * PACK], BF16, name="first_words", align_bytes=ALIGN)
+        turned_factor = first_words[:].bitcast(F32)[:, 0:HALF]
+        blocks = [slice(c * P, (c + 1) * P) for c in range(BLOCKS)]
+        for cols in blocks:
+            nc.tensor.transpose(banks[6][:, cols], factor[:, cols], identity[:])
+        for c, cols in enumerate(blocks):
+            nc.scalar.activation(turned_factor[:, cols], banks[6][:, cols], ACT.Identity, scale=minus_ts_columns[0][:, c : c + 1], bias=ts_columns[:, c : c + 1])
+        for cols in blocks:
+            nc.tensor.transpose(banks[7][:, cols], turned_factor[:, cols], identity[:])
+        nc.scalar.activation(late_factors[:, 1:LAST, :], late_factors[:, 1:LAST, :], ACT.Identity, bias=-1.0)
+        nc.vector.tensor_scalar_add(late_factors[:, LAST, :], late_factors[:, LAST, :], -1.0)
+        nc.scalar.copy(factor, banks[7][:])
 
-        stage = keep.tile([P, PACK * ROW], F32, name="stage", align_bytes=ALIGN)
+        stage = keep.tile([P, PACK * ROW], F32, name="stage", tag="stage", align_bytes=ALIGN)
         stage_rows = stage[:].rearrange("p (t c) -> p t c", t=PACK)
         late_dy = stage_rows[:, :, 0:HALF]
         late_products = [stage[:, 2 * ROW + HALF : 2 * ROW + N], stage[:, 2 * ROW + N : 3 * ROW]]
@@ -137,7 +152,6 @@ def tile_attend_gex_pl_tnh_x_kernel(tc, dyT, hT, ts, wm, offs, out_0, out_1, out
                       for first, step in ((HALF, HALF), (HALF + QUARTER, ROW - HALF))]
         w_grouped = stage[:, 2 * ROW + QUARTER : 3 * ROW].bitcast(BF16)
 
-        first_words = keep.tile([P, HALF * PACK], BF16, name="first_words", align_bytes=ALIGN)
         first_grouped = first_words[:].rearrange("p (c j) -> p c j", j=PACK)
         dz_codes = [keep.tile([P, HALF], U32, name="dz_codes%d" % s, align_bytes=ALIGN) for s in range(2)]
         dz_scales = [keep.tile([P, HALF], U8, name="dz_scales%d" % s, align_bytes=ALIGN) for s in range(2)]
@@ -148,7 +162,7 @@ def tile_attend_gex_pl_tnh_x_kernel(tc, dyT, hT, ts, wm, offs, out_0, out_1, out
             nc.vector.tensor_copy(target, dy_planes[t][:].indirect(entries(first, count)))
 
         def gather_times(target, t, first, count):
-            nc.vector.tensor_tensor(target, dy_planes[t][:].indirect(entries(first, count)), ts_factors[t][:, first : first + count] if first < HALF else part(factors, t, first, count), ALU.mult)
+            nc.vector.tensor_tensor(target, dy_planes[t][:].indirect(entries(first, count)), held_factors[t] if first == QUARTER and t in held_factors else part(factors, t, first, count), ALU.mult)
 
         def interleave_pair(t, pair, cols):
             nc.scalar.copy(first_grouped[:, cols, t : t + 2], pair.rearrange("p e c -> p c e"))
@@ -170,13 +184,14 @@ def tile_attend_gex_pl_tnh_x_kernel(tc, dyT, hT, ts, wm, offs, out_0, out_1, out
                 nc.tensor.transpose(pairs[:, u * P : (u + 1) * P], rounded[:].bitcast(F32)[:, u * P : (u + 1) * P], identity[:])
             nc.scalar.copy(target.rearrange("q (t u) -> q t u", u=2), pairs.rearrange("q (u t) -> q t u", u=2))
 
-        gather_times(early_dz[:, 0, :], 0, 0, HALF)
-        times_ts(LAST, ts_factors[0])
         gather_dy(late_dy[:, 0, :], 0, HALF, HALF)
+        gather_times(early_dz[:, 0, :], 0, 0, HALF)
         gather_dy(late_dy[:, 1, low], 1, HALF, QUARTER)
-        gather_times(early_dz[:, 1, :], 1, 0, HALF)
+        for cols in (low, high):
+            gather_times(early_dz[:, 1, cols], 1, cols.start, QUARTER)
         interleave_pair(0, early_dz, slice(0, HALF))
-        gather_times(third_dz, 2, 0, HALF)
+        for cols in (low, high):
+            gather_times(third_dz[:, cols], 2, cols.start, QUARTER)
         for pair, cols in zip(last_pairs, (low, high)):
             gather_times(pair[:, 1, :], LAST, cols.start, QUARTER)
             interleave_pair(2, pair, cols)
@@ -212,13 +227,14 @@ def tile_attend_gex_pl_tnh_x_kernel(tc, dyT, hT, ts, wm, offs, out_0, out_1, out
 
         for lane in LANES[:2]:
             scatter(lane, 0, [product(lane, 0)[:]], source("dx%d" % lane, HALF))
+        for t, cols in ((0, slice(0, HALF)), (1, low)):
+            nc.gpsimd.tensor_tensor(late_products[t], late_dy[:, t, cols], late_factors[:, t, cols], ALU.mult)
+        zeroed_window(LANES[2], "ts_listed")
         cut_bank = product(3, 0)
         scatter(3, 0, [cut_bank[:, 0:CUT]], source("dx3", CUT))
         last_first_bank = product(1, 0)
 
         second_words = keep.tile([P, PACK * HALF], BF16, name="second_words", tag="second_words", align_bytes=ALIGN)
-        for t, cols in ((0, slice(0, HALF)), (1, low)):
-            nc.gpsimd.tensor_tensor(late_products[t], late_dy[:, t, cols], late_factors[:, t, cols], ALU.mult)
         for j in (2, 3, 0, 1):
             cols = slice(j * P, (j + 1) * P)
             for t in range(PACK):
@@ -229,13 +245,13 @@ def tile_attend_gex_pl_tnh_x_kernel(tc, dyT, hT, ts, wm, offs, out_0, out_1, out
                                  ACT.Copy, scale=minus_ts_columns[1][:, j : j + 1])
             turn_pairs_back(rounded, first_turn_banks[j], second_words[:].bitcast(F32)[:, 2 * P * j : 2 * P * (j + 1)])
         quantize_dz(1, second_words[:])
-        scatter(3, CUT, [cut_bank[:, CUT:HALF]], source("dx_cut", HALF - CUT, "rounded1"))
-        zeroed_window(LANES[LAST], "rounded1")
+        zeroed_window(LANES[LAST], "stage")
+        scatter(1, 0, [last_first_bank[:, 0:CUT]], source("dx_cut", CUT, "rounded1"))
         late_dx = source("late_dx", 2 * N, "second_words")
-        last_dx = late_dx[:, 0:N]
-        scatter(0, HALF, [product(0, 1)[:]], last_dx[:, HALF:N])
-        scatter(2, HALF, [product(2, 1)[:]], late_dx[:, N : N + HALF])
-        scatter(3, HALF, [product(3, 1)[:]], late_dx[:, N + HALF : 2 * N])
+        last_dx = late_dx[:, 0 : N - CUT]
+        scatter(0, HALF, [product(0, 1)[:]], last_dx[:, HALF - CUT : N - CUT])
+        scatter(2, HALF, [product(2, 1)[:]], late_dx[:, N - CUT : N - CUT + HALF])
+        scatter(3, CUT, [cut_bank[:, CUT:HALF], product(3, 1)[:]], late_dx[:, N + CUT : 2 * N])
 
         words = keep.tile([P, T, PACK], BF16, name="words", align_bytes=ALIGN)
         codes = keep.tile([P, T], U32, name="codes", align_bytes=ALIGN)
@@ -246,7 +262,7 @@ def tile_attend_gex_pl_tnh_x_kernel(tc, dyT, hT, ts, wm, offs, out_0, out_1, out
             copy(words[:, cols, lane], windows[lane][:, cols])
 
         put_lane(nc.scalar.copy, 0, low_tokens)
-        scatter(1, 0, [last_first_bank[:], product(1, 1)[:]], last_dx)
+        scatter(1, CUT, [last_first_bank[:, CUT:HALF], product(1, 1)[:]], last_dx)
         put_lane(nc.scalar.copy, 0, high_tokens)
         staged = keep.tile([P, 2, T // 2], BF16, name="staged")
         runs = [slice(b * RUN, (b + 1) * RUN) for b in range(QUADS)]

@@ -29,6 +29,7 @@ STRIPE = 16
 TS_ROW = P - 1
 CUT = 256
 QUARTER = HALF // 2
+COVER = 352
 ROW = 5 * QUARTER
 LANES = (0, 2, 3, 1)
 ALIGN = 64
@@ -227,31 +228,32 @@ def tile_attend_gex_pl_tnh_x_kernel(tc, dyT, hT, ts, wm, offs, out_0, out_1, out
 
         for lane in LANES[:2]:
             scatter(lane, 0, [product(lane, 0)[:]], source("dx%d" % lane, HALF))
-        for t, cols in ((0, slice(0, HALF)), (1, low)):
-            nc.gpsimd.tensor_tensor(late_products[t], late_dy[:, t, cols], late_factors[:, t, cols], ALU.mult)
+        nc.gpsimd.tensor_tensor(late_products[1], late_dy[:, 0, high], late_factors[:, 0, high], ALU.mult)
+        early_pair = late_products[0].rearrange("p (t c) -> p t c", t=2)
+        nc.gpsimd.tensor_tensor(early_pair, late_dy[:, 0:2, low], late_factors[:, 0:2, low], ALU.mult)
         zeroed_window(LANES[2], "ts_listed")
         cut_bank = product(3, 0)
-        scatter(3, 0, [cut_bank[:, 0:CUT]], source("dx3", CUT))
         last_first_bank = product(1, 0)
 
         second_words = keep.tile([P, PACK * HALF], BF16, name="second_words", tag="second_words", align_bytes=ALIGN)
         for j in (2, 3, 0, 1):
             cols = slice(j * P, (j + 1) * P)
             for t in range(PACK):
-                whole = late_products[t] if t == 0 or (t == 1 and j < 2) else late_dy[:, t, :]
-                nc.tensor.transpose(first_turn_banks[j][:, t * P : (t + 1) * P], whole[:, cols], identity[:])
+                inside = slice((j % 2) * P, (j % 2 + 1) * P)
+                block = early_pair[:, t, inside] if t < 2 and j < 2 else late_products[1][:, inside] if t == 0 else late_dy[:, t, cols]
+                nc.tensor.transpose(first_turn_banks[j][:, t * P : (t + 1) * P], block, identity[:])
             rounded = keep.tile([P, HALF], BF16, name="rounded_dz%d" % j, tag="rounded%d" % j, align_bytes=ALIGN)
             nc.scalar.activation(rounded[:].rearrange("c (u q e) -> c u q e", u=2, e=2), first_turn_banks[j][:].rearrange("c (u e q) -> c u q e", u=2, e=2),
                                  ACT.Copy, scale=minus_ts_columns[1][:, j : j + 1])
             turn_pairs_back(rounded, first_turn_banks[j], second_words[:].bitcast(F32)[:, 2 * P * j : 2 * P * (j + 1)])
         quantize_dz(1, second_words[:])
-        zeroed_window(LANES[LAST], "stage")
-        scatter(1, 0, [last_first_bank[:, 0:CUT]], source("dx_cut", CUT, "rounded1"))
-        late_dx = source("late_dx", 2 * N, "second_words")
-        last_dx = late_dx[:, 0 : N - CUT]
-        scatter(0, HALF, [product(0, 1)[:]], last_dx[:, HALF - CUT : N - CUT])
-        scatter(2, HALF, [product(2, 1)[:]], late_dx[:, N - CUT : N - CUT + HALF])
-        scatter(3, CUT, [cut_bank[:, CUT:HALF], product(3, 1)[:]], late_dx[:, N + CUT : 2 * N])
+        scatter(3, 0, [cut_bank[:, 0:COVER]], source("dx_cut", COVER, "rounded1"))
+        zeroed_window(LANES[LAST], "rounded1")
+        late_dx = source("late_dx", 3 * N, "second_words")
+        last_dx = late_dx[:, 0:N]
+        scatter(0, HALF, [product(0, 1)[:]], last_dx[:, HALF:N])
+        scatter(2, HALF, [product(2, 1)[:]], late_dx[:, N : N + HALF])
+        scatter(3, COVER, [cut_bank[:, COVER:HALF], product(3, 1)[:]], late_dx[:, 2 * N + COVER : 3 * N])
 
         words = keep.tile([P, T, PACK], BF16, name="words", align_bytes=ALIGN)
         codes = keep.tile([P, T], U32, name="codes", align_bytes=ALIGN)
@@ -262,7 +264,7 @@ def tile_attend_gex_pl_tnh_x_kernel(tc, dyT, hT, ts, wm, offs, out_0, out_1, out
             copy(words[:, cols, lane], windows[lane][:, cols])
 
         put_lane(nc.scalar.copy, 0, low_tokens)
-        scatter(1, CUT, [last_first_bank[:, CUT:HALF], product(1, 1)[:]], last_dx)
+        scatter(1, 0, [last_first_bank[:], product(1, 1)[:]], last_dx)
         put_lane(nc.scalar.copy, 0, high_tokens)
         staged = keep.tile([P, 2, T // 2], BF16, name="staged")
         runs = [slice(b * RUN, (b + 1) * RUN) for b in range(QUADS)]

@@ -29,7 +29,8 @@ STRIPE = 16
 TS_ROW = P - 1
 CUT = 256
 QUARTER = HALF // 2
-COVER = 352
+COVER = 320
+SECOND = 416
 ROW = 5 * QUARTER
 LANES = (0, 2, 3, 1)
 ALIGN = 64
@@ -49,7 +50,7 @@ def tile_attend_gex_pl_tnh_x_kernel(tc, dyT, hT, ts, wm, offs, out_0, out_1, out
 
         banks = [psum.tile([P, HALF], F32, name="bank%d" % i) for i in range(8)]
         column_banks, spread_bank = banks[0:2], banks[2]
-        product_banks = [[banks[3], banks[4], banks[5], banks[2]], [banks[3], banks[4], banks[1], banks[0]]]
+        product_banks = [[banks[3], banks[4], banks[5], banks[2]], [banks[3], banks[6], banks[1], banks[0]]]
         first_turn_banks = banks[0:2] + banks[6:8]
 
         identity = keep.tile([P, P], F32, name="identity")
@@ -226,14 +227,18 @@ def tile_attend_gex_pl_tnh_x_kernel(tc, dyT, hT, ts, wm, offs, out_0, out_1, out
         def source(name, count, slot=None):
             return keep.tile([P, count], F32, name=name, tag=slot or name, align_bytes=ALIGN)[:]
 
-        for lane in LANES[:2]:
-            scatter(lane, 0, [product(lane, 0)[:]], source("dx%d" % lane, HALF))
-        nc.gpsimd.tensor_tensor(late_products[1], late_dy[:, 0, high], late_factors[:, 0, high], ALU.mult)
+        scatter(0, 0, [product(0, 0)[:]], source("dx0", HALF))
+        second_bank = product(2, 0)
+        scatter(2, 0, [second_bank[:, 0:SECOND]], source("dx2", SECOND))
+        for first in (0, P):
+            cols = slice(QUARTER + first, QUARTER + first + P)
+            nc.gpsimd.tensor_tensor(late_products[1][:, first : first + P], late_dy[:, 0, cols], late_factors[:, 0, cols], ALU.mult)
         early_pair = late_products[0].rearrange("p (t c) -> p t c", t=2)
         nc.gpsimd.tensor_tensor(early_pair, late_dy[:, 0:2, low], late_factors[:, 0:2, low], ALU.mult)
-        zeroed_window(LANES[2], "ts_listed")
-        cut_bank = product(3, 0)
+        zeroed_window(LANES[LAST], "ts_listed")
         last_first_bank = product(1, 0)
+        scatter(1, 0, [last_first_bank[:, 0:CUT]], source("dx1", CUT))
+        cut_bank = product(3, 0)
 
         second_words = keep.tile([P, PACK * HALF], BF16, name="second_words", tag="second_words", align_bytes=ALIGN)
         for j in (2, 3, 0, 1):
@@ -247,12 +252,12 @@ def tile_attend_gex_pl_tnh_x_kernel(tc, dyT, hT, ts, wm, offs, out_0, out_1, out
                                  ACT.Copy, scale=minus_ts_columns[1][:, j : j + 1])
             turn_pairs_back(rounded, first_turn_banks[j], second_words[:].bitcast(F32)[:, 2 * P * j : 2 * P * (j + 1)])
         quantize_dz(1, second_words[:])
+        zeroed_window(LANES[2], "stage")
         scatter(3, 0, [cut_bank[:, 0:COVER]], source("dx_cut", COVER, "rounded1"))
-        zeroed_window(LANES[LAST], "rounded1")
         late_dx = source("late_dx", 3 * N, "second_words")
-        last_dx = late_dx[:, 0:N]
-        scatter(0, HALF, [product(0, 1)[:]], last_dx[:, HALF:N])
-        scatter(2, HALF, [product(2, 1)[:]], late_dx[:, N : N + HALF])
+        last_dx = late_dx[:, 0 : N - CUT]
+        scatter(0, HALF, [product(0, 1)[:]], last_dx[:, HALF - CUT : N - CUT])
+        scatter(2, SECOND, [second_bank[:, SECOND:HALF], product(2, 1)[:]], late_dx[:, N : 2 * N - SECOND])
         scatter(3, COVER, [cut_bank[:, COVER:HALF], product(3, 1)[:]], late_dx[:, 2 * N + COVER : 3 * N])
 
         words = keep.tile([P, T, PACK], BF16, name="words", align_bytes=ALIGN)
@@ -264,12 +269,15 @@ def tile_attend_gex_pl_tnh_x_kernel(tc, dyT, hT, ts, wm, offs, out_0, out_1, out
             copy(words[:, cols, lane], windows[lane][:, cols])
 
         put_lane(nc.scalar.copy, 0, low_tokens)
-        scatter(1, 0, [last_first_bank[:], product(1, 1)[:]], last_dx)
-        put_lane(nc.scalar.copy, 0, high_tokens)
+        scatter(1, CUT, [last_first_bank[:, CUT:HALF], product(1, 1)[:]], last_dx)
+        put_lane(nc.gpsimd.tensor_copy, 0, high_tokens)
         staged = keep.tile([P, 2, T // 2], BF16, name="staged")
         runs = [slice(b * RUN, (b + 1) * RUN) for b in range(QUADS)]
         for lane in (2, 3):
-            for cols in runs[0:2]:
+            first = QUARTER if lane == 2 else 0
+            if first:
+                nc.gpsimd.tensor_copy(staged[:, 0, 0:first], windows[lane][:, 0:first])
+            for cols in (slice(first, RUN), runs[1]):
                 nc.scalar.copy(staged[:, lane - 2, cols], windows[lane][:, cols])
             put_lane(nc.gpsimd.tensor_copy, lane, high_tokens)
         for cols in runs[0:2]:

@@ -274,16 +274,17 @@ def tile_attend_gex_pl_tnh_x_kernel(tc, dyT, hT, ts, wm, offs, out_0, out_1, out
         staged = keep.tile([P, 2, T // 2], BF16, name="staged")
         runs = [slice(b * RUN, (b + 1) * RUN) for b in range(QUADS)]
         for lane in (2, 3):
-            first = QUARTER if lane == 2 else 0
-            if first:
-                nc.gpsimd.tensor_copy(staged[:, 0, 0:first], windows[lane][:, 0:first])
-            for cols in (slice(first, RUN), runs[1]):
+            by_gpsimd, by_scalar = (low, (high, runs[1])) if lane == 2 else (runs[1], (low, high))
+            nc.gpsimd.tensor_copy(staged[:, lane - 2, by_gpsimd], windows[lane][:, by_gpsimd])
+            for cols in by_scalar:
                 nc.scalar.copy(staged[:, lane - 2, cols], windows[lane][:, cols])
             put_lane(nc.gpsimd.tensor_copy, lane, high_tokens)
         for cols in runs[0:2]:
             nc.scalar.copy(words[:, cols, 2:PACK], staged[:, :, cols].rearrange("p e c -> p c e"))
-        for b, cols in enumerate(runs):
-            put_lane(nc.vector.tensor_copy if b < 2 else nc.scalar.copy, 1, cols)
+        for cols in runs[0:2]:
+            put_lane(nc.vector.tensor_copy, 1, cols)
+        for cols in (runs[2], slice(T - RUN, T - QUARTER), slice(T - QUARTER, T)):
+            put_lane(nc.scalar.copy, 1, cols)
         words_out = out_1[0].rearrange("p t l -> p (t l)").bitcast(I32)
         for b, cols in enumerate(runs):
             for piece in (low, high):

@@ -21,18 +21,15 @@ P = 128
 PACK = 4
 LAST = PACK - 1
 HALF = 512
+QUARTER = HALF // 2
 QUAD = 32
 QUADS = P // QUAD
 RUN = T // QUADS
 BLOCKS = HALF // P
 STRIPE = 16
+LINE = 4
 TS_ROW = P - 1
-CUT = 256
-QUARTER = HALF // 2
-COVER = 320
-SECOND = 416
-ROW = 5 * QUARTER
-LANES = (0, 2, 3, 1)
+WIDE = 384
 ALIGN = 64
 
 
@@ -42,6 +39,9 @@ def tile_attend_gex_pl_tnh_x_kernel(tc, dyT, hT, ts, wm, offs, out_0, out_1, out
         keep = ctx.enter_context(tc.tile_pool(name="keep", bufs=1))
         psum = ctx.enter_context(tc.psum_pool(name="psum", bufs=1))
 
+        def held(name, columns, dtype=F32, slot=None):
+            return keep.tile([P, columns], dtype, name=name, tag=slot or name, align_bytes=ALIGN)
+
         offsets = keep.tile([P, N // STRIPE], U16, name="offsets")
         nc.sync.dma_start(offsets[:], offs)
 
@@ -49,14 +49,12 @@ def tile_attend_gex_pl_tnh_x_kernel(tc, dyT, hT, ts, wm, offs, out_0, out_1, out
             return offsets[:, first // STRIPE : (first + count) // STRIPE]
 
         banks = [psum.tile([P, HALF], F32, name="bank%d" % i) for i in range(8)]
-        column_banks, spread_bank = banks[0:2], banks[2]
-        product_banks = [[banks[3], banks[4], banks[5], banks[2]], [banks[3], banks[6], banks[1], banks[0]]]
-        first_turn_banks = banks[0:2] + banks[6:8]
+        column_banks, spread_banks = banks[0:2], banks[2:4]
 
         identity = keep.tile([P, P], F32, name="identity")
         make_identity(nc, identity[:])
 
-        ts_window = keep.tile([P, T], F32, name="ts_window")
+        ts_window = held("ts_window", T)
         nc.sync.dma_start(ts_window[TS_ROW:P, :], ts[TS_ROW:P, :])
         nc.gpsimd.memset(ts_window[0:TS_ROW, T // 2 : T], 0.0)
         nc.vector.memset(ts_window[0:TS_ROW, 0 : T // 2 - 1], 0.0)
@@ -64,8 +62,8 @@ def tile_attend_gex_pl_tnh_x_kernel(tc, dyT, hT, ts, wm, offs, out_0, out_1, out
 
         h_rows = hT.rearrange("(p j) c -> p j c", j=PACK)
         dy_rows = dyT.rearrange("(p j) c -> p j c", j=PACK)
-        h_planes = [keep.tile([P, T], F32, name="h_plane%d" % t, tag="h_plane%d" % t, align_bytes=ALIGN) for t in range(PACK)]
-        dy_planes = [keep.tile([P, T], F32, name="dy_plane%d" % t, tag="dy_plane%d" % t, align_bytes=ALIGN) for t in range(PACK)]
+        h_planes = [held("h_plane%d" % t, T) for t in range(PACK)]
+        dy_planes = [held("dy_plane%d" % t, T) for t in range(PACK)]
         w_raw = keep.tile([P, PACK, D], F32, name="w_raw")
         for t in range(PACK):
             nc.sync.dma_start(h_planes[t][:], h_rows[:, t, :])
@@ -73,223 +71,175 @@ def tile_attend_gex_pl_tnh_x_kernel(tc, dyT, hT, ts, wm, offs, out_0, out_1, out
             nc.sync.dma_start(dy_planes[t][:], dy_rows[:, t, :])
         nc.sync.dma_start(w_raw[:], wm[0].rearrange("(p j) d -> p j d", j=PACK))
 
-        windows = {}
-
-        def zeroed_window(lane, slot):
-            windows[lane] = keep.tile([P, T], F32, name="window%d" % lane, tag=slot, align_bytes=ALIGN)
+        windows = [held("window%d" % lane, T) for lane in range(PACK)]
+        for lane in range(PACK):
             nc.gpsimd.memset(windows[lane][:], 0.0)
 
-        for lane in LANES[:2]:
-            zeroed_window(lane, "window%d" % lane)
-
-        ts_listed = keep.tile([P, N], F32, name="ts_listed", tag="ts_listed", align_bytes=ALIGN)
-        minus_ts_columns = [keep.tile([P, BLOCKS], F32, name="minus_ts_columns%d" % s) for s in range(2)]
-        minus_ts_rows = keep.tile([P, HALF], F32, name="minus_ts_rows", tag="minus_ts_rows")
+        ts_listed = held("ts_listed", N)
         for s in range(2):
             nc.vector.tensor_copy(ts_listed[:, s * HALF : (s + 1) * HALF], ts_window[:].indirect(entries(s * HALF, HALF)))
+        for s in range(2):
             for c in range(BLOCKS):
                 first = s * HALF + c * P
                 nc.tensor.transpose(column_banks[s][:, c * P : (c + 1) * P], ts_listed[:, first : first + P], identity[:])
-            nc.scalar.activation(minus_ts_columns[s][:], column_banks[s][:, TS_ROW:HALF:P], ACT.Copy, scale=-1.0)
-        ts_columns = keep.tile([P, BLOCKS], F32, name="ts_columns")
-        nc.scalar.copy(ts_columns[:], column_banks[0][:, TS_ROW:HALF:P])
-        for c in range(BLOCKS):
-            column = minus_ts_columns[0][:, c : c + 1].to_broadcast([P, P])
-            nc.tensor.transpose(spread_bank[:, c * P : (c + 1) * P], column, identity[:])
-        nc.scalar.copy(minus_ts_rows[:], spread_bank[:])
+            minus_ts = keep.tile([P, BLOCKS], F32, name="minus_ts%d" % s)
+            nc.vector.tensor_scalar_mul(minus_ts[:], column_banks[s][:, TS_ROW:HALF:P], -1.0)
+            for c in range(BLOCKS):
+                nc.tensor.transpose(spread_banks[s][:, c * P : (c + 1) * P], minus_ts[:, c : c + 1].to_broadcast([P, P]), identity[:])
 
-        def part(tile, t, first, count):
-            return tile[:, t * N + first : t * N + first + count]
+        def plane(tile, t):
+            return tile[:, t * HALF : (t + 1) * HALF]
 
-        h_listed = keep.tile([P, PACK * N], F32, name="h_listed")
-        factors = keep.tile([P, PACK * N], F32, name="factors", tag="ts_listed", align_bytes=ALIGN)
+        factors = held("factors", 2 * PACK * HALF)
+        second = [plane(factors, t) for t in range(PACK)]
+        first_in = [second[LAST], plane(factors, 4), plane(factors, 5), plane(factors, 6)]
+        first_out = first_in[0:LAST] + [first_in[1]]
+        second_in = second[0:LAST] + [plane(factors, 7)]
+
+        def slope(s, source, target):
+            nc.vector.scalar_tensor_tensor(target, source, 1.0, spread_banks[s][:], ALU.subtract, ALU.mult)
+
+        dz_first = held("dz_first", PACK * HALF)
+        dy_second = held("dy_second", PACK * HALF)
         low, high = slice(0, QUARTER), slice(QUARTER, HALF)
-        late_factors = factors[:].rearrange("p (t c) -> p t c", t=PACK)[:, :, HALF:N]
-        held_factors = {}
 
-        def times_ts(t, cols, target):
-            nc.gpsimd.tensor_tensor(target, part(factors, t, 0, HALF)[:, cols], minus_ts_rows[:, cols], ALU.mult)
+        def gather_dy(t):
+            for cols in (slice(0, HALF),) if t < LAST else (low, high):
+                count = cols.stop - cols.start
+                nc.vector.tensor_tensor(plane(dz_first, t)[:, cols], dy_planes[t][:].indirect(entries(cols.start, count)), first_out[t][:, cols], ALU.mult)
+            nc.scalar.activation(plane(dy_second, t), dy_planes[t][:].indirect(entries(HALF, HALF)), ACT.Copy)
 
         for t in range(PACK):
-            width = N if t else HALF
-            for first in range(0, N, width):
-                nc.vector.tensor_copy(part(h_listed, t, first, width), h_planes[t][:].indirect(entries(first, width)))
-            if t >= 2:
-                held_factors[t - 1] = keep.tile([P, QUARTER], F32, name="held_factor%d" % t, tag="h_plane%d" % t, align_bytes=ALIGN)[:]
-                times_ts(t - 1, high, held_factors[t - 1])
-            listed_h, factor = part(h_listed, t, 0, HALF), part(factors, t, 0, HALF)
+            listed = [first_in[t], second_in[t]]
+            for s in (0, 1) if t < LAST else (1, 0):
+                if t == 0 and s == 0:
+                    nc.vector.tensor_copy(listed[s], h_planes[t][:].indirect(entries(s * HALF, HALF)))
+                else:
+                    nc.scalar.activation(listed[s], h_planes[t][:].indirect(entries(s * HALF, HALF)), ACT.Copy)
+            for s in (0, 1) if t < LAST else (1, 0):
+                if t == LAST or (t == 0 and s == 1):
+                    nc.scalar.activation(listed[s], listed[s], ACT.Square)
+                else:
+                    nc.vector.tensor_tensor(listed[s], listed[s], listed[s], ALU.mult)
             if t < LAST:
-                first_square = part(factors, t, HALF, QUARTER)
-                nc.scalar.activation(first_square, listed_h[:, low], ACT.Square)
-                nc.scalar.activation(factor[:, high], listed_h[:, high], ACT.Square)
-                nc.scalar.activation(factor[:, low], first_square, ACT.Identity, bias=-1.0)
-                nc.scalar.activation(factor[:, high], factor[:, high], ACT.Identity, bias=-1.0)
-                cols = low if t else slice(0, HALF)
-                times_ts(t, cols, factor[:, cols])
-            else:
-                nc.scalar.activation(factor, listed_h, ACT.Square)
-            nc.scalar.activation(part(factors, t, HALF, HALF), part(h_listed, t, HALF, HALF), ACT.Square)
-            if t == 0:
-                nc.scalar.activation(late_factors[:, 0, :], late_factors[:, 0, :], ACT.Identity, bias=-1.0)
-        first_words = keep.tile([P, HALF * PACK], BF16, name="first_words", align_bytes=ALIGN)
-        turned_factor = first_words[:].bitcast(F32)[:, 0:HALF]
-        blocks = [slice(c * P, (c + 1) * P) for c in range(BLOCKS)]
-        for cols in blocks:
-            nc.tensor.transpose(banks[6][:, cols], factor[:, cols], identity[:])
-        for c, cols in enumerate(blocks):
-            nc.scalar.activation(turned_factor[:, cols], banks[6][:, cols], ACT.Identity, scale=minus_ts_columns[0][:, c : c + 1], bias=ts_columns[:, c : c + 1])
-        for cols in blocks:
-            nc.tensor.transpose(banks[7][:, cols], turned_factor[:, cols], identity[:])
-        nc.scalar.activation(late_factors[:, 1:LAST, :], late_factors[:, 1:LAST, :], ACT.Identity, bias=-1.0)
-        nc.vector.tensor_scalar_add(late_factors[:, LAST, :], late_factors[:, LAST, :], -1.0)
-        nc.scalar.copy(factor, banks[7][:])
+                for s in (0, 1) if t else (1, 0):
+                    slope(s, listed[s], listed[s])
+        gather_dy(0)
+        slope(1, second_in[LAST], second[LAST])
+        gather_dy(1)
+        slope(0, first_in[LAST], first_out[LAST])
+        gather_dy(2)
+        gather_dy(LAST)
 
-        stage = keep.tile([P, PACK * ROW], F32, name="stage", tag="stage", align_bytes=ALIGN)
-        stage_rows = stage[:].rearrange("p (t c) -> p t c", t=PACK)
-        late_dy = stage_rows[:, :, 0:HALF]
-        late_products = [stage[:, 2 * ROW + HALF : 2 * ROW + N], stage[:, 2 * ROW + N : 3 * ROW]]
-        early_dz = keep.tile([P, 2, HALF], F32, name="early_dz", tag="early_dz")
-        third_dz = stage[:, HALF : 2 * HALF]
-        last_pairs = [stage[:, first : first + 2 * step].rearrange("p (e c) -> p e c", e=2)[:, :, low]
-                      for first, step in ((HALF, HALF), (HALF + QUARTER, ROW - HALF))]
-        w_grouped = stage[:, 2 * ROW + QUARTER : 3 * ROW].bitcast(BF16)
+        def by_planes(tile, cols):
+            return tile[:, 0 : PACK * HALF].rearrange("p (t c i) -> p c t i", t=PACK, i=LINE)[:, cols.start // LINE : cols.stop // LINE]
 
-        first_grouped = first_words[:].rearrange("p (c j) -> p c j", j=PACK)
-        dz_codes = [keep.tile([P, HALF], U32, name="dz_codes%d" % s, align_bytes=ALIGN) for s in range(2)]
-        dz_scales = [keep.tile([P, HALF], U8, name="dz_scales%d" % s, align_bytes=ALIGN) for s in range(2)]
-        w_codes = keep.tile([P, D], U32, name="w_codes", align_bytes=ALIGN)
-        w_scales = keep.tile([P, D], U8, name="w_scales", align_bytes=ALIGN)
+        def by_words(tile, cols):
+            return tile[:].rearrange("p (c i t) -> p c t i", t=PACK, i=LINE)[:, cols.start // LINE : cols.stop // LINE]
 
-        def gather_dy(target, t, first, count):
-            nc.vector.tensor_copy(target, dy_planes[t][:].indirect(entries(first, count)))
+        dz_words = [held("dz_words%d" % s, PACK * HALF, BF16) for s in range(2)]
+        dz_codes = [held("dz_codes%d" % s, HALF, U32) for s in range(2)]
+        dz_scales = [held("dz_scales%d" % s, HALF, U8) for s in range(2)]
+        w_grouped = [held("w_grouped%d" % e, 2 * PACK * P, BF16) for e in range(2)]
+        w_codes = [held("w_codes%d" % e, 2 * P, U32) for e in range(2)]
+        w_scales = [held("w_scales%d" % e, 2 * P, U8) for e in range(2)]
 
-        def gather_times(target, t, first, count):
-            nc.vector.tensor_tensor(target, dy_planes[t][:].indirect(entries(first, count)), held_factors[t] if first == QUARTER and t in held_factors else part(factors, t, first, count), ALU.mult)
+        def quantize_dz(s):
+            nc.vector.quantize_mx(dz_codes[s][:].bitcast(E5M2), dz_scales[s][:], dz_words[s][:])
 
-        def interleave_pair(t, pair, cols):
-            nc.scalar.copy(first_grouped[:, cols, t : t + 2], pair.rearrange("p e c -> p c e"))
+        def regroup_w(e):
+            target = w_grouped[e][:].rearrange("p (u m j) -> p m j u", u=2, j=PACK)
+            nc.scalar.copy(target, w_raw[:].rearrange("p j (m e u) -> p m j u e", u=2, e=2)[:, :, :, :, e])
 
-        def quantize_dz(s, words):
-            nc.vector.quantize_mx(dz_codes[s][:].bitcast(E5M2), dz_scales[s][:], words)
+        def quantize_w(e):
+            nc.vector.quantize_mx(w_codes[e][:].bitcast(E4M3), w_scales[e][:], w_grouped[e][:])
 
-        def regroup_w(place, lanes):
-            target = w_grouped.rearrange("p (t m j) -> p m j t", t=PACK, j=PACK)[:, :, :, place : place + 2]
-            nc.scalar.copy(target, w_raw[:].rearrange("p j (m t) -> p m j t", t=PACK)[:, :, :, lanes])
-
-        def quantize_w(place, count):
-            cols = slice(place * P, (place + count) * P)
-            nc.vector.quantize_mx(w_codes[:, cols].bitcast(E4M3), w_scales[:, cols], w_grouped[:, PACK * cols.start : PACK * cols.stop])
-
-        def turn_pairs_back(rounded, bank, target):
-            pairs = bank[:, 0 : 2 * P]
-            for u in range(2):
-                nc.tensor.transpose(pairs[:, u * P : (u + 1) * P], rounded[:].bitcast(F32)[:, u * P : (u + 1) * P], identity[:])
-            nc.scalar.copy(target.rearrange("q (t u) -> q t u", u=2), pairs.rearrange("q (u t) -> q t u", u=2))
-
-        gather_dy(late_dy[:, 0, :], 0, HALF, HALF)
-        gather_times(early_dz[:, 0, :], 0, 0, HALF)
-        gather_dy(late_dy[:, 1, low], 1, HALF, QUARTER)
-        for cols in (low, high):
-            gather_times(early_dz[:, 1, cols], 1, cols.start, QUARTER)
-        interleave_pair(0, early_dz, slice(0, HALF))
-        for cols in (low, high):
-            gather_times(third_dz[:, cols], 2, cols.start, QUARTER)
-        for pair, cols in zip(last_pairs, (low, high)):
-            gather_times(pair[:, 1, :], LAST, cols.start, QUARTER)
-            interleave_pair(2, pair, cols)
-        gather_times(late_dy[:, LAST, :], LAST, HALF, HALF)
-        quantize_dz(0, first_words[:])
-        gather_times(late_dy[:, 1, high], 1, HALF + QUARTER, QUARTER)
-        regroup_w(0, slice(0, 2))
-        quantize_w(0, 1)
-        quantize_w(1, 1)
-        gather_times(late_dy[:, 2, :], 2, HALF, HALF)
-        regroup_w(2, slice(2, PACK))
-        quantize_w(2, 2)
+        nc.scalar.copy(by_words(dz_words[0], low), by_planes(dz_first, low))
+        regroup_w(0)
+        nc.scalar.copy(by_words(dz_words[0], high), by_planes(dz_first, high))
+        whole = slice(0, HALF)
+        nc.vector.tensor_tensor(by_words(dz_words[1], whole), by_planes(dy_second, whole), by_planes(factors, whole), ALU.mult)
+        quantize_w(0)
+        quantize_dz(1)
+        quantize_dz(0)
 
         out_lanes = out_0.rearrange("(p j) c -> p j c", j=PACK)
+        order = [(0, 1), (1, 1), (0, 0), (1, 0), (2, 1), (2, 0), (3, 1), (3, 0)]
+        product_banks = {key: banks[(i + 4) % 8] for i, key in enumerate(order)}
 
         def product(lane, s):
-            bank, cols = product_banks[s][LANES.index(lane)], slice(lane * P, (lane + 1) * P)
-            nc.tensor.matmul_mx(bank[:], lhsT=w_codes[:, cols].bitcast(E4M3), lhsT_scale=w_scales[:, cols],
+            cols = slice((lane % 2) * P, (lane % 2 + 1) * P)
+            nc.tensor.matmul_mx(product_banks[lane, s][:], lhsT=w_codes[lane // 2][:, cols].bitcast(E4M3), lhsT_scale=w_scales[lane // 2][:, cols],
                                 rhs=dz_codes[s][:].bitcast(E5M2), rhs_scale=dz_scales[s][:], start=True, stop=True)
-            return bank
 
-        def scatter(lane, first, pieces, dx):
-            done = 0
-            for piece in pieces:
-                nc.scalar.copy(dx[:, done : done + piece.shape[1]], piece)
-                done += piece.shape[1]
-            nc.vector.tensor_copy(windows[lane][:].indirect(entries(first, done)), dx)
-            if first + done == N:
-                nc.sync.dma_start(out_lanes[:, lane, :], windows[lane][:])
+        for lane, s in order[0:4]:
+            product(lane, s)
 
-        def source(name, count, slot=None):
-            return keep.tile([P, count], F32, name=name, tag=slot or name, align_bytes=ALIGN)[:]
+        dx = [held("dx%d" % lane, N) for lane in range(PACK)]
 
-        scatter(0, 0, [product(0, 0)[:]], source("dx0", HALF))
-        second_bank = product(2, 0)
-        scatter(2, 0, [second_bank[:, 0:SECOND]], source("dx2", SECOND))
-        for first in (0, P):
-            cols = slice(QUARTER + first, QUARTER + first + P)
-            nc.gpsimd.tensor_tensor(late_products[1][:, first : first + P], late_dy[:, 0, cols], late_factors[:, 0, cols], ALU.mult)
-        early_pair = late_products[0].rearrange("p (t c) -> p t c", t=2)
-        nc.gpsimd.tensor_tensor(early_pair, late_dy[:, 0:2, low], late_factors[:, 0:2, low], ALU.mult)
-        zeroed_window(LANES[LAST], "ts_listed")
-        last_first_bank = product(1, 0)
-        scatter(1, 0, [last_first_bank[:, 0:CUT]], source("dx1", CUT))
-        cut_bank = product(3, 0)
+        def leave_bank(copy, lane, s, cols=whole):
+            copy(dx[lane][:, s * HALF + cols.start : s * HALF + cols.stop], product_banks[lane, s][:, cols])
 
-        second_words = keep.tile([P, PACK * HALF], BF16, name="second_words", tag="second_words", align_bytes=ALIGN)
-        for j in (2, 3, 0, 1):
-            cols = slice(j * P, (j + 1) * P)
-            for t in range(PACK):
-                inside = slice((j % 2) * P, (j % 2 + 1) * P)
-                block = early_pair[:, t, inside] if t < 2 and j < 2 else late_products[1][:, inside] if t == 0 else late_dy[:, t, cols]
-                nc.tensor.transpose(first_turn_banks[j][:, t * P : (t + 1) * P], block, identity[:])
-            rounded = keep.tile([P, HALF], BF16, name="rounded_dz%d" % j, tag="rounded%d" % j, align_bytes=ALIGN)
-            nc.scalar.activation(rounded[:].rearrange("c (u q e) -> c u q e", u=2, e=2), first_turn_banks[j][:].rearrange("c (u e q) -> c u q e", u=2, e=2),
-                                 ACT.Copy, scale=minus_ts_columns[1][:, j : j + 1])
-            turn_pairs_back(rounded, first_turn_banks[j], second_words[:].bitcast(F32)[:, 2 * P * j : 2 * P * (j + 1)])
-        quantize_dz(1, second_words[:])
-        zeroed_window(LANES[2], "stage")
-        scatter(3, 0, [cut_bank[:, 0:COVER]], source("dx_cut", COVER, "rounded1"))
-        late_dx = source("late_dx", 3 * N, "second_words")
-        last_dx = late_dx[:, 0 : N - CUT]
-        scatter(0, HALF, [product(0, 1)[:]], last_dx[:, HALF - CUT : N - CUT])
-        scatter(2, SECOND, [second_bank[:, SECOND:HALF], product(2, 1)[:]], late_dx[:, N : 2 * N - SECOND])
-        scatter(3, COVER, [cut_bank[:, COVER:HALF], product(3, 1)[:]], late_dx[:, 2 * N + COVER : 3 * N])
+        def vector_scatter(lane, first, count):
+            nc.vector.tensor_copy(windows[lane][:].indirect(entries(first, count)), dx[lane][:, first : first + count])
 
-        words = keep.tile([P, T, PACK], BF16, name="words", align_bytes=ALIGN)
-        codes = keep.tile([P, T], U32, name="codes", align_bytes=ALIGN)
-        scales = keep.tile([P, RUN], U8, name="scales", align_bytes=ALIGN)
-        low_tokens, high_tokens = slice(0, T // 2), slice(T // 2, T)
+        def scalar_scatter(lane, first, count):
+            nc.scalar.activation(windows[lane][:].indirect(entries(first, count)), dx[lane][:, first : first + count], ACT.Copy)
 
-        def put_lane(copy, lane, cols):
-            copy(words[:, cols, lane], windows[lane][:, cols])
+        def store(lane):
+            nc.sync.dma_start(out_lanes[:, lane, :], windows[lane][:])
 
-        put_lane(nc.scalar.copy, 0, low_tokens)
-        scatter(1, CUT, [last_first_bank[:, CUT:HALF], product(1, 1)[:]], last_dx)
-        put_lane(nc.gpsimd.tensor_copy, 0, high_tokens)
-        staged = keep.tile([P, 2, T // 2], BF16, name="staged")
-        runs = [slice(b * RUN, (b + 1) * RUN) for b in range(QUADS)]
+        pairs = [held("pairs%d" % b, PACK * RUN, BF16) for b in range(QUADS)]
+
+        def pair_lane(b, lane):
+            view = pairs[b][:].rearrange("p (u c e) -> p u c e", u=2, e=2)
+            return view[:, lane // 2, :, lane % 2], windows[lane][:, b * RUN : (b + 1) * RUN]
+
+        leave_bank(nc.scalar.copy, 0, 1)
+        vector_scatter(0, HALF, HALF)
+        leave_bank(nc.scalar.copy, 1, 1)
+        regroup_w(1)
+        quantize_w(1)
+        for lane, s in order[4:]:
+            product(lane, s)
+        leave_bank(nc.scalar.copy, 0, 0)
+        vector_scatter(0, 0, HALF)
+        store(0)
+        scalar_scatter(1, N - WIDE, WIDE)
+        leave_bank(nc.scalar.copy, 1, 0)
+        scalar_scatter(1, QUARTER, WIDE)
+        scalar_scatter(1, 0, QUARTER)
+        store(1)
+        leave_bank(nc.vector.tensor_copy, 2, 1)
+        leave_bank(nc.vector.tensor_copy, 2, 0)
+        vector_scatter(2, 0, N)
+        store(2)
+        for lane in range(2):
+            for b in range(QUADS):
+                nc.gpsimd.tensor_scalar(*pair_lane(b, lane), 1.0, -0.0, ALU.mult, ALU.add)
+        leave_bank(nc.scalar.copy, 3, 1)
+        scalar_scatter(3, N - WIDE, WIDE)
+        leave_bank(nc.scalar.copy, 3, 0)
+        scalar_scatter(3, QUARTER, WIDE)
+        scalar_scatter(3, 0, QUARTER)
+        store(3)
+
+        words = held("words", T * PACK, BF16)
+        codes = held("codes", T, U32)
+        scales = held("scales", RUN, U8)
         for lane in (2, 3):
-            by_gpsimd, by_scalar = (low, (high, runs[1])) if lane == 2 else (runs[1], (low, high))
-            nc.gpsimd.tensor_copy(staged[:, lane - 2, by_gpsimd], windows[lane][:, by_gpsimd])
-            for cols in by_scalar:
-                nc.scalar.copy(staged[:, lane - 2, cols], windows[lane][:, cols])
-            put_lane(nc.gpsimd.tensor_copy, lane, high_tokens)
-        for cols in runs[0:2]:
-            nc.scalar.copy(words[:, cols, 2:PACK], staged[:, :, cols].rearrange("p e c -> p c e"))
-        for cols in runs[0:2]:
-            put_lane(nc.vector.tensor_copy, 1, cols)
-        for cols in (runs[2], slice(T - RUN, T - QUARTER), slice(T - QUARTER, T)):
-            put_lane(nc.scalar.copy, 1, cols)
+            for b in range(QUADS):
+                nc.vector.tensor_copy(*pair_lane(b, lane))
+        for b in range(QUADS):
+            copy = nc.vector.tensor_copy if b == 1 else nc.scalar.copy
+            target = words[:, PACK * b * RUN : PACK * (b + 1) * RUN].bitcast(F32).rearrange("p (c i u) -> p c u i", u=2, i=LINE)
+            copy(target, pairs[b][:].bitcast(F32).rearrange("p (u c i) -> p c u i", u=2, i=LINE))
         words_out = out_1[0].rearrange("p t l -> p (t l)").bitcast(I32)
-        for b, cols in enumerate(runs):
+        for b in range(QUADS):
+            cols = slice(b * RUN, (b + 1) * RUN)
             for piece in (low, high):
                 tokens = slice(cols.start + piece.start, cols.start + piece.stop)
-                nc.vector.quantize_mx(codes[:, tokens].bitcast(E4M3), scales[PACK * b : P, piece], words[:, tokens, :].rearrange("p c j -> p (c j)"))
+                nc.vector.quantize_mx(codes[:, tokens].bitcast(E4M3), scales[PACK * b : P, piece], words[:, PACK * tokens.start : PACK * tokens.stop])
             nc.sync.dma_start(words_out[:, cols], codes[:, cols].bitcast(I32))
         scales_out = out_2[0].bitcast(I32)
         for q in range(QUADS):

@@ -64,42 +64,48 @@ def tile_attend_gex_pl_tnh_x_kernel(tc, dyT, hT, ts, wm, offs, out_0, out_1, out
         dy_rows = dyT.rearrange("(p j) c -> p j c", j=PACK)
         h_planes = [held("h_plane%d" % t, T) for t in range(PACK)]
         dy_planes = [held("dy_plane%d" % t, T) for t in range(PACK)]
-        w_raw = keep.tile([P, PACK, D], F32, name="w_raw")
+        w_raw = held("w_raw", PACK * D)
         for t in range(PACK):
             nc.sync.dma_start(h_planes[t][:], h_rows[:, t, :])
         for t in range(PACK):
             nc.sync.dma_start(dy_planes[t][:], dy_rows[:, t, :])
-        nc.sync.dma_start(w_raw[:], wm[0].rearrange("(p j) d -> p j d", j=PACK))
+        nc.sync.dma_start(w_raw[:], wm[0].rearrange("(p j) d -> p (j d)", j=PACK))
 
-        windows = [held("window%d" % lane, T) for lane in range(PACK)]
-        for lane in range(PACK):
-            nc.gpsimd.memset(windows[lane][:], 0.0)
+        windows = []
 
-        ts_listed = held("ts_listed", N)
-        for s in range(2):
-            nc.vector.tensor_copy(ts_listed[:, s * HALF : (s + 1) * HALF], ts_window[:].indirect(entries(s * HALF, HALF)))
-        for s in range(2):
-            for c in range(BLOCKS):
-                first = s * HALF + c * P
-                nc.tensor.transpose(column_banks[s][:, c * P : (c + 1) * P], ts_listed[:, first : first + P], identity[:])
-            minus_ts = keep.tile([P, BLOCKS], F32, name="minus_ts%d" % s)
-            nc.vector.tensor_scalar_mul(minus_ts[:], column_banks[s][:, TS_ROW:HALF:P], -1.0)
-            for c in range(BLOCKS):
-                nc.tensor.transpose(spread_banks[s][:, c * P : (c + 1) * P], minus_ts[:, c : c + 1].to_broadcast([P, P]), identity[:])
+        def zeroed_window(slot=None):
+            windows.append(held("window%d" % len(windows), T, slot=slot))
+            nc.gpsimd.memset(windows[-1][:], 0.0)
+
+        for lane in range(LAST):
+            zeroed_window()
 
         def plane(tile, t):
             return tile[:, t * HALF : (t + 1) * HALF]
 
-        factors = held("factors", 2 * PACK * HALF)
+        factors = held("factors", PACK * HALF)
+        ts_listed = [held("ts_listed%d" % s, HALF)[:] for s in range(2)]
+        nc.vector.tensor_copy(ts_listed[0], ts_window[:].indirect(entries(0, HALF)))
+        nc.scalar.activation(ts_listed[1], ts_window[:].indirect(entries(HALF, HALF)), ACT.Copy)
+        for c in range(BLOCKS):
+            for s in range(2):
+                nc.tensor.transpose(column_banks[s][:, c * P : (c + 1) * P], ts_listed[s][:, c * P : (c + 1) * P], identity[:])
+        minus_ts = [keep.tile([P, BLOCKS], F32, name="minus_ts%d" % s) for s in range(2)]
+        for s in range(2):
+            nc.scalar.activation(minus_ts[s][:], column_banks[s][:, TS_ROW:HALF:P], ACT.Copy, scale=-1.0)
+        for c in range(BLOCKS):
+            for s in range(2):
+                nc.tensor.transpose(spread_banks[s][:, c * P : (c + 1) * P], minus_ts[s][:, c : c + 1].to_broadcast([P, P]), identity[:])
+
         second = [plane(factors, t) for t in range(PACK)]
-        first_in = [second[LAST], plane(factors, 4), plane(factors, 5), plane(factors, 6)]
-        first_out = first_in[0:LAST] + [first_in[1]]
-        second_in = second[0:LAST] + [plane(factors, 7)]
+        first_in = [held("first_h%d" % t, HALF)[:] for t in range(PACK)]
+        first_out = [second[LAST], first_in[1], held("first_factor2", HALF)[:], first_in[1]]
+        dz_first = held("dz_first", PACK * HALF)
+        second_in = [plane(dz_first, 1), ts_listed[0], plane(dz_first, 0), plane(dz_first, LAST)]
 
         def slope(s, source, target):
             nc.vector.scalar_tensor_tensor(target, source, 1.0, spread_banks[s][:], ALU.subtract, ALU.mult)
 
-        dz_first = held("dz_first", PACK * HALF)
         dy_second = held("dy_second", PACK * HALF)
         low, high = slice(0, QUARTER), slice(QUARTER, HALF)
 
@@ -109,82 +115,105 @@ def tile_attend_gex_pl_tnh_x_kernel(tc, dyT, hT, ts, wm, offs, out_0, out_1, out
                 nc.vector.tensor_tensor(plane(dz_first, t)[:, cols], dy_planes[t][:].indirect(entries(cols.start, count)), first_out[t][:, cols], ALU.mult)
             nc.scalar.activation(plane(dy_second, t), dy_planes[t][:].indirect(entries(HALF, HALF)), ACT.Copy)
 
-        for t in range(PACK):
-            listed = [first_in[t], second_in[t]]
-            for s in (0, 1) if t < LAST else (1, 0):
-                if t == 0 and s == 0:
-                    nc.vector.tensor_copy(listed[s], h_planes[t][:].indirect(entries(s * HALF, HALF)))
-                else:
-                    nc.scalar.activation(listed[s], h_planes[t][:].indirect(entries(s * HALF, HALF)), ACT.Copy)
-            for s in (0, 1) if t < LAST else (1, 0):
-                if t == LAST or (t == 0 and s == 1):
-                    nc.scalar.activation(listed[s], listed[s], ACT.Square)
-                else:
-                    nc.vector.tensor_tensor(listed[s], listed[s], listed[s], ALU.mult)
-            if t < LAST:
-                for s in (0, 1) if t else (1, 0):
-                    slope(s, listed[s], listed[s])
+        def gather_h(t, s):
+            target, window = (first_in, second_in)[s][t], h_planes[t][:].indirect(entries(s * HALF, HALF))
+            if t < 2 and s == 0:
+                nc.vector.tensor_copy(target, window)
+            else:
+                nc.scalar.activation(target, window, ACT.Copy)
+            return target
+
+        for t in range(2):
+            first_h, second_h = gather_h(t, 0), gather_h(t, 1)
+            square = second_h if t else ts_listed[1]
+            nc.scalar.activation(square, second_h, ACT.Square)
+            nc.vector.tensor_tensor(first_h, first_h, first_h, ALU.mult)
+            slope(0, first_h, first_out[t])
+            slope(1, square, second[t])
+        both = [(gather_h(2, 0), first_out[2]), (gather_h(2, 1), second[2])]
+        for s, (listed, target) in enumerate(both):
+            slope(s, listed, target)
+        for listed, target in both:
+            nc.vector.scalar_tensor_tensor(target, listed, 1.0, target, ALU.add, ALU.mult)
+        for listed in [gather_h(LAST, 1), gather_h(LAST, 0)]:
+            nc.scalar.activation(listed, listed, ACT.Square)
+
+        def by_planes(tile, cols):
+            return tile[:].rearrange("p (t c i) -> p c t i", t=PACK, i=LINE)[:, cols.start // LINE : cols.stop // LINE]
+
+        def by_words(words):
+            return words.rearrange("p (c i t) -> p c t i", t=PACK, i=LINE)
+
+        whole = slice(0, HALF)
+        low_words = held("low_words", PACK * QUARTER, BF16)[:]
+        second_words = held("second_words", PACK * HALF, BF16)[:]
+
+        def weave_pair(u):
+            planes = slice(2 * u, 2 * u + 2)
+            nc.scalar.copy(by_words(low_words)[:, :, planes], by_planes(dz_first, low)[:, :, planes])
+
         gather_dy(0)
         slope(1, second_in[LAST], second[LAST])
         gather_dy(1)
         slope(0, first_in[LAST], first_out[LAST])
+        weave_pair(0)
         gather_dy(2)
         gather_dy(LAST)
+        weave_pair(1)
 
-        def by_planes(tile, cols):
-            return tile[:, 0 : PACK * HALF].rearrange("p (t c i) -> p c t i", t=PACK, i=LINE)[:, cols.start // LINE : cols.stop // LINE]
-
-        def by_words(tile, cols):
-            return tile[:].rearrange("p (c i t) -> p c t i", t=PACK, i=LINE)[:, cols.start // LINE : cols.stop // LINE]
-
-        dz_words = [held("dz_words%d" % s, PACK * HALF, BF16) for s in range(2)]
-        dz_codes = [held("dz_codes%d" % s, HALF, U32) for s in range(2)]
+        dz_codes = [held("dz_codes0", HALF, U32)]
         dz_scales = [held("dz_scales%d" % s, HALF, U8) for s in range(2)]
-        w_grouped = [held("w_grouped%d" % e, 2 * PACK * P, BF16) for e in range(2)]
+        w_grouped = {}
         w_codes = [held("w_codes%d" % e, 2 * P, U32) for e in range(2)]
         w_scales = [held("w_scales%d" % e, 2 * P, U8) for e in range(2)]
 
-        def quantize_dz(s):
-            nc.vector.quantize_mx(dz_codes[s][:].bitcast(E5M2), dz_scales[s][:], dz_words[s][:])
+        def quantize_dz(s, cols, words):
+            nc.vector.quantize_mx(dz_codes[s][:, cols].bitcast(E5M2), dz_scales[s][:, cols], words)
 
-        def regroup_w(e):
+        def regroup_w(e, copy):
+            w_grouped[e] = held("w_grouped%d" % e, 2 * PACK * P, BF16, slot="w_grouped%d" % e)
             target = w_grouped[e][:].rearrange("p (u m j) -> p m j u", u=2, j=PACK)
-            nc.scalar.copy(target, w_raw[:].rearrange("p j (m e u) -> p m j u e", u=2, e=2)[:, :, :, :, e])
+            copy(target, w_raw[:].rearrange("p (j m e u) -> p m j u e", j=PACK, u=2, e=2)[:, :, :, :, e])
 
         def quantize_w(e):
             nc.vector.quantize_mx(w_codes[e][:].bitcast(E4M3), w_scales[e][:], w_grouped[e][:])
 
-        nc.scalar.copy(by_words(dz_words[0], low), by_planes(dz_first, low))
-        regroup_w(0)
-        nc.scalar.copy(by_words(dz_words[0], high), by_planes(dz_first, high))
-        whole = slice(0, HALF)
-        nc.vector.tensor_tensor(by_words(dz_words[1], whole), by_planes(dy_second, whole), by_planes(factors, whole), ALU.mult)
+        def second_product(cols):
+            words = second_words[:, PACK * cols.start : PACK * cols.stop]
+            nc.vector.tensor_tensor(by_words(words), by_planes(dy_second, cols), by_planes(factors, cols), ALU.mult)
+
+        second_product(low)
+        regroup_w(0, nc.scalar.copy)
+        quantize_dz(0, low, low_words)
         quantize_w(0)
-        quantize_dz(1)
-        quantize_dz(0)
+        regroup_w(1, nc.scalar.copy)
+        second_product(high)
+        dz_codes.append(held("dz_codes1", HALF, U32, slot="w_grouped0"))
+        quantize_dz(1, whole, second_words)
+        high_words = held("high_words", PACK * QUARTER, BF16, slot="w_raw")[:]
+        nc.vector.tensor_copy(by_words(high_words), by_planes(dz_first, high))
+        quantize_w(1)
+        quantize_dz(0, high, high_words)
+        zeroed_window("w_grouped1")
 
         out_lanes = out_0.rearrange("(p j) c -> p j c", j=PACK)
-        order = [(0, 1), (1, 1), (0, 0), (1, 0), (2, 1), (2, 0), (3, 1), (3, 0)]
-        product_banks = {key: banks[(i + 4) % 8] for i, key in enumerate(order)}
+        product_banks = {(lane, s): banks[(2 * lane + s + 4) % 8] for lane in range(PACK) for s in range(2)}
 
-        def product(lane, s):
-            cols = slice((lane % 2) * P, (lane % 2 + 1) * P)
-            nc.tensor.matmul_mx(product_banks[lane, s][:], lhsT=w_codes[lane // 2][:, cols].bitcast(E4M3), lhsT_scale=w_scales[lane // 2][:, cols],
-                                rhs=dz_codes[s][:].bitcast(E5M2), rhs_scale=dz_scales[s][:], start=True, stop=True)
+        def product(lane, s, cols=whole):
+            block = slice((lane % 2) * P, (lane % 2 + 1) * P)
+            nc.tensor.matmul_mx(product_banks[lane, s][:, cols], lhsT=w_codes[lane // 2][:, block].bitcast(E4M3), lhsT_scale=w_scales[lane // 2][:, block],
+                                rhs=dz_codes[s][:, cols].bitcast(E5M2), rhs_scale=dz_scales[s][:, cols], start=True, stop=True)
 
-        for lane, s in order[0:4]:
-            product(lane, s)
+        sources = held("sources", 9 * QUARTER)
 
-        dx = [held("dx%d" % lane, N) for lane in range(PACK)]
+        def leave_bank(copy, place, lane, s, cols=whole):
+            copy(sources[:, place : place + cols.stop - cols.start], product_banks[lane, s][:, cols])
 
-        def leave_bank(copy, lane, s, cols=whole):
-            copy(dx[lane][:, s * HALF + cols.start : s * HALF + cols.stop], product_banks[lane, s][:, cols])
+        def vector_scatter(lane, first, count, place):
+            nc.vector.tensor_copy(windows[lane][:].indirect(entries(first, count)), sources[:, place : place + count])
 
-        def vector_scatter(lane, first, count):
-            nc.vector.tensor_copy(windows[lane][:].indirect(entries(first, count)), dx[lane][:, first : first + count])
-
-        def scalar_scatter(lane, first, count):
-            nc.scalar.activation(windows[lane][:].indirect(entries(first, count)), dx[lane][:, first : first + count], ACT.Copy)
+        def scalar_scatter(lane, first, count, place):
+            nc.scalar.activation(windows[lane][:].indirect(entries(first, count)), sources[:, place : place + count], ACT.Copy)
 
         def store(lane):
             nc.sync.dma_start(out_lanes[:, lane, :], windows[lane][:])
@@ -195,33 +224,41 @@ def tile_attend_gex_pl_tnh_x_kernel(tc, dyT, hT, ts, wm, offs, out_0, out_1, out
             view = pairs[b][:].rearrange("p (u c e) -> p u c e", u=2, e=2)
             return view[:, lane // 2, :, lane % 2], windows[lane][:, b * RUN : (b + 1) * RUN]
 
-        leave_bank(nc.scalar.copy, 0, 1)
-        vector_scatter(0, HALF, HALF)
-        leave_bank(nc.scalar.copy, 1, 1)
-        regroup_w(1)
-        quantize_w(1)
-        for lane, s in order[4:]:
-            product(lane, s)
-        leave_bank(nc.scalar.copy, 0, 0)
-        vector_scatter(0, 0, HALF)
+        lane2, lane0, lane1 = 0, HALF, 5 * QUARTER
+        for lane, place in ((1, lane1), (0, lane0)):
+            product(lane, 0, low)
+            leave_bank(nc.scalar.copy, place, lane, 0, low)
+        scalar_scatter(1, 0, QUARTER, lane1)
+        vector_scatter(0, 0, QUARTER, lane0)
+        for lane, place in ((0, lane0 + QUARTER), (1, lane1 + HALF)):
+            product(lane, 1)
+            leave_bank(nc.scalar.copy, place, lane, 1)
+        scalar_scatter(1, N - WIDE, WIDE, lane1 + N - WIDE)
+        for lane in range(2):
+            product(lane, 0, high)
+        leave_bank(nc.vector.tensor_copy, lane0, 0, 0, high)
+        vector_scatter(0, QUARTER, N - QUARTER, lane0)
         store(0)
-        scalar_scatter(1, N - WIDE, WIDE)
-        leave_bank(nc.scalar.copy, 1, 0)
-        scalar_scatter(1, QUARTER, WIDE)
-        scalar_scatter(1, 0, QUARTER)
+        leave_bank(nc.scalar.copy, lane1 + QUARTER, 1, 0, high)
+        scalar_scatter(1, QUARTER, WIDE, lane1 + QUARTER)
         store(1)
-        leave_bank(nc.vector.tensor_copy, 2, 1)
-        leave_bank(nc.vector.tensor_copy, 2, 0)
-        vector_scatter(2, 0, N)
+        for lane in (2, 3):
+            for s in range(2):
+                product(lane, s)
+        leave_bank(nc.scalar.copy, lane2, 2, 0)
+        leave_bank(nc.vector.tensor_copy, lane2 + HALF, 2, 1)
+        vector_scatter(2, 0, N, lane2)
         store(2)
         for lane in range(2):
             for b in range(QUADS):
                 nc.gpsimd.tensor_scalar(*pair_lane(b, lane), 1.0, -0.0, ALU.mult, ALU.add)
-        leave_bank(nc.scalar.copy, 3, 1)
-        scalar_scatter(3, N - WIDE, WIDE)
-        leave_bank(nc.scalar.copy, 3, 0)
-        scalar_scatter(3, QUARTER, WIDE)
-        scalar_scatter(3, 0, QUARTER)
+        leave_bank(nc.scalar.copy, lane1 + N - WIDE, 3, 1, slice(HALF - WIDE, HALF))
+        scalar_scatter(3, N - WIDE, WIDE, lane1 + N - WIDE)
+        leave_bank(nc.scalar.copy, lane1 + QUARTER, 3, 0, high)
+        leave_bank(nc.scalar.copy, lane1 + HALF, 3, 1, slice(0, P))
+        scalar_scatter(3, QUARTER, WIDE, lane1 + QUARTER)
+        leave_bank(nc.scalar.copy, lane1, 3, 0, low)
+        scalar_scatter(3, 0, QUARTER, lane1)
         store(3)
 
         words = held("words", T * PACK, BF16)

@@ -204,7 +204,7 @@ def tile_attend_gex_pl_tnh_x_kernel(tc, dyT, hT, ts, wm, offs, out_0, out_1, out
             nc.tensor.matmul_mx(product_banks[lane, s][:, cols], lhsT=w_codes[lane // 2][:, block].bitcast(E4M3), lhsT_scale=w_scales[lane // 2][:, block],
                                 rhs=dz_codes[s][:, cols].bitcast(E5M2), rhs_scale=dz_scales[s][:, cols], start=True, stop=True)
 
-        sources = held("sources", 9 * QUARTER)
+        sources = held("sources", 3 * N)
 
         def leave_bank(copy, place, lane, s, cols=whole):
             copy(sources[:, place : place + cols.stop - cols.start], product_banks[lane, s][:, cols])
@@ -215,8 +215,8 @@ def tile_attend_gex_pl_tnh_x_kernel(tc, dyT, hT, ts, wm, offs, out_0, out_1, out
         def scalar_scatter(lane, first, count, place):
             nc.scalar.activation(windows[lane][:].indirect(entries(first, count)), sources[:, place : place + count], ACT.Copy)
 
-        def store(lane):
-            nc.sync.dma_start(out_lanes[:, lane, :], windows[lane][:])
+        def store(lane, queue=nc.sync):
+            queue.dma_start(out_lanes[:, lane, :], windows[lane][:])
 
         pairs = [held("pairs%d" % b, PACK * RUN, BF16) for b in range(QUADS)]
 
@@ -224,29 +224,30 @@ def tile_attend_gex_pl_tnh_x_kernel(tc, dyT, hT, ts, wm, offs, out_0, out_1, out
             view = pairs[b][:].rearrange("p (u c e) -> p u c e", u=2, e=2)
             return view[:, lane // 2, :, lane % 2], windows[lane][:, b * RUN : (b + 1) * RUN]
 
-        lane2, lane0, lane1 = 0, HALF, 5 * QUARTER
-        for lane, place in ((1, lane1), (0, lane0)):
+        lane0, lane1, lane2 = 0, N, 2 * N
+        for lane in (1, 0):
             product(lane, 0, low)
-            leave_bank(nc.scalar.copy, place, lane, 0, low)
+            leave_bank(nc.scalar.copy, lane * N, lane, 0, low)
         scalar_scatter(1, 0, QUARTER, lane1)
         vector_scatter(0, 0, QUARTER, lane0)
-        for lane, place in ((0, lane0 + QUARTER), (1, lane1 + HALF)):
+        for lane in range(2):
             product(lane, 1)
-            leave_bank(nc.scalar.copy, place, lane, 1)
-        scalar_scatter(1, N - WIDE, WIDE, lane1 + N - WIDE)
+            leave_bank(nc.scalar.copy, lane * N + HALF, lane, 1)
+        product(2, 1)
         for lane in range(2):
             product(lane, 0, high)
-        leave_bank(nc.vector.tensor_copy, lane0, 0, 0, high)
-        vector_scatter(0, QUARTER, N - QUARTER, lane0)
+        leave_bank(nc.scalar.copy, lane0 + QUARTER, 0, 0, high)
+        scalar_scatter(1, N - WIDE, WIDE, lane1 + N - WIDE)
+        product(2, 0)
+        for s in (1, 0):
+            leave_bank(nc.vector.tensor_copy, lane2 + s * HALF, 2, s)
+        vector_scatter(0, QUARTER, N - QUARTER, lane0 + QUARTER)
         store(0)
         leave_bank(nc.scalar.copy, lane1 + QUARTER, 1, 0, high)
         scalar_scatter(1, QUARTER, WIDE, lane1 + QUARTER)
         store(1)
-        for lane in (2, 3):
-            for s in range(2):
-                product(lane, s)
-        leave_bank(nc.scalar.copy, lane2, 2, 0)
-        leave_bank(nc.vector.tensor_copy, lane2 + HALF, 2, 1)
+        for s in (1, 0):
+            product(3, s)
         vector_scatter(2, 0, N, lane2)
         store(2)
         for lane in range(2):
@@ -259,7 +260,7 @@ def tile_attend_gex_pl_tnh_x_kernel(tc, dyT, hT, ts, wm, offs, out_0, out_1, out
         scalar_scatter(3, QUARTER, WIDE, lane1 + QUARTER)
         leave_bank(nc.scalar.copy, lane1, 3, 0, low)
         scalar_scatter(3, 0, QUARTER, lane1)
-        store(3)
+        store(3, nc.scalar)
 
         words = held("words", T * PACK, BF16)
         codes = held("codes", T, U32)

@@ -218,11 +218,12 @@ def tile_attend_gex_pl_tnh_x_kernel(tc, dyT, hT, ts, wm, offs, out_0, out_1, out
         def store(lane, queue=nc.sync):
             queue.dma_start(out_lanes[:, lane, :], windows[lane][:])
 
-        pairs = [held("pairs%d" % b, PACK * RUN, BF16) for b in range(QUADS)]
+        pairs = held("pairs", PACK * T, BF16)
 
-        def pair_lane(b, lane):
-            view = pairs[b][:].rearrange("p (u c e) -> p u c e", u=2, e=2)
-            return view[:, lane // 2, :, lane % 2], windows[lane][:, b * RUN : (b + 1) * RUN]
+        def pair_lane(lane, tokens):
+            return pairs[:].rearrange("p (u c e) -> p u c e", u=2, e=2)[:, lane // 2, tokens, lane % 2], windows[lane][:, tokens]
+
+        runs = [slice(b * RUN, (b + 1) * RUN) for b in range(QUADS)]
 
         lane0, lane1, lane2 = 0, N, 2 * N
         for lane in (1, 0):
@@ -230,20 +231,19 @@ def tile_attend_gex_pl_tnh_x_kernel(tc, dyT, hT, ts, wm, offs, out_0, out_1, out
             leave_bank(nc.scalar.copy, lane * N, lane, 0, low)
         scalar_scatter(1, 0, QUARTER, lane1)
         vector_scatter(0, 0, QUARTER, lane0)
-        for lane in range(2):
+        for lane in (1, 0):
             product(lane, 1)
             leave_bank(nc.scalar.copy, lane * N + HALF, lane, 1)
         product(2, 1)
         for lane in range(2):
             product(lane, 0, high)
-        leave_bank(nc.scalar.copy, lane0 + QUARTER, 0, 0, high)
+            leave_bank(nc.vector.tensor_copy, lane * N + QUARTER, lane, 0, high)
         scalar_scatter(1, N - WIDE, WIDE, lane1 + N - WIDE)
         product(2, 0)
         for s in (1, 0):
             leave_bank(nc.vector.tensor_copy, lane2 + s * HALF, 2, s)
         vector_scatter(0, QUARTER, N - QUARTER, lane0 + QUARTER)
         store(0)
-        leave_bank(nc.scalar.copy, lane1 + QUARTER, 1, 0, high)
         scalar_scatter(1, QUARTER, WIDE, lane1 + QUARTER)
         store(1)
         for s in (1, 0):
@@ -251,8 +251,7 @@ def tile_attend_gex_pl_tnh_x_kernel(tc, dyT, hT, ts, wm, offs, out_0, out_1, out
         vector_scatter(2, 0, N, lane2)
         store(2)
         for lane in range(2):
-            for b in range(QUADS):
-                nc.gpsimd.tensor_scalar(*pair_lane(b, lane), 1.0, -0.0, ALU.mult, ALU.add)
+            nc.gpsimd.tensor_scalar(*pair_lane(lane, slice(0, T)), 1.0, -0.0, ALU.mult, ALU.add)
         leave_bank(nc.scalar.copy, lane1 + N - WIDE, 3, 1, slice(HALF - WIDE, HALF))
         scalar_scatter(3, N - WIDE, WIDE, lane1 + N - WIDE)
         leave_bank(nc.scalar.copy, lane1 + QUARTER, 3, 0, high)
@@ -265,20 +264,23 @@ def tile_attend_gex_pl_tnh_x_kernel(tc, dyT, hT, ts, wm, offs, out_0, out_1, out
         words = held("words", T * PACK, BF16)
         codes = held("codes", T, U32)
         scales = held("scales", RUN, U8)
-        for lane in (2, 3):
-            for b in range(QUADS):
-                nc.vector.tensor_copy(*pair_lane(b, lane))
+        nc.vector.tensor_copy(*pair_lane(2, slice(0, T)))
+        for run in runs:
+            nc.vector.tensor_copy(*pair_lane(LAST, run))
         for b in range(QUADS):
             copy = nc.vector.tensor_copy if b == 1 else nc.scalar.copy
             target = words[:, PACK * b * RUN : PACK * (b + 1) * RUN].bitcast(F32).rearrange("p (c i u) -> p c u i", u=2, i=LINE)
-            copy(target, pairs[b][:].bitcast(F32).rearrange("p (u c i) -> p c u i", u=2, i=LINE))
+            copy(target, pairs[:].bitcast(F32).rearrange("p (u c i) -> p c u i", u=2, i=LINE)[:, b * RUN // LINE : (b + 1) * RUN // LINE])
         words_out = out_1[0].rearrange("p t l -> p (t l)").bitcast(I32)
         for b in range(QUADS):
             cols = slice(b * RUN, (b + 1) * RUN)
             for piece in (low, high):
                 tokens = slice(cols.start + piece.start, cols.start + piece.stop)
                 nc.vector.quantize_mx(codes[:, tokens].bitcast(E4M3), scales[PACK * b : P, piece], words[:, PACK * tokens.start : PACK * tokens.stop])
-            nc.sync.dma_start(words_out[:, cols], codes[:, cols].bitcast(I32))
+                if b == LAST:
+                    nc.sync.dma_start(words_out[:, tokens], codes[:, tokens].bitcast(I32))
+            if b < LAST:
+                nc.sync.dma_start(words_out[:, cols], codes[:, cols].bitcast(I32))
         scales_out = out_2[0].bitcast(I32)
         for q in range(QUADS):
             queue = nc.sync if q == LAST else nc.scalar

@@ -51,6 +51,10 @@ def tile_attend_gex_pl_tnh_x_kernel(tc, dyT, hT, ts, wm, offs, out_0, out_1, out
         banks = [psum.tile([P, HALF], F32, name="bank%d" % i) for i in range(8)]
         column_banks, spread_banks = banks[0:2], banks[2:4]
 
+        warm = keep.tile([P, 2], F32, name="warm")
+        nc.gpsimd.memset(warm[:, 0:1], 0.0)
+        nc.scalar.activation(warm[:, 1:2], warm[:, 0:1], ACT.Square)
+
         identity = keep.tile([P, P], F32, name="identity")
         make_identity(nc, identity[:])
 
@@ -84,7 +88,9 @@ def tile_attend_gex_pl_tnh_x_kernel(tc, dyT, hT, ts, wm, offs, out_0, out_1, out
             return tile[:, t * HALF : (t + 1) * HALF]
 
         factors = held("factors", PACK * HALF)
-        ts_listed = [held("ts_listed%d" % s, HALF)[:] for s in range(2)]
+        ts_room = held("ts_room", 3 * HALF)
+        ts_listed = [held("ts_first", HALF)[:], ts_room[:, HALF:N]]
+        middle = N - P // 2
         nc.vector.tensor_copy(ts_listed[0], ts_window[:].indirect(entries(0, HALF)))
         nc.scalar.activation(ts_listed[1], ts_window[:].indirect(entries(HALF, HALF)), ACT.Copy)
         for c in range(BLOCKS):
@@ -101,7 +107,7 @@ def tile_attend_gex_pl_tnh_x_kernel(tc, dyT, hT, ts, wm, offs, out_0, out_1, out
         first_in = [held("first_h%d" % t, HALF)[:] for t in range(PACK)]
         first_out = [second[LAST], first_in[1], held("first_factor2", HALF)[:], first_in[1]]
         dz_first = held("dz_first", PACK * HALF)
-        second_in = [plane(dz_first, 1), ts_listed[0], plane(dz_first, 0), plane(dz_first, LAST)]
+        second_in = [plane(dz_first, 1), ts_room[:, middle : middle + HALF], plane(dz_first, 0), plane(dz_first, LAST)]
 
         def slope(s, source, target):
             nc.vector.scalar_tensor_tensor(target, source, 1.0, spread_banks[s][:], ALU.subtract, ALU.mult)
@@ -125,7 +131,7 @@ def tile_attend_gex_pl_tnh_x_kernel(tc, dyT, hT, ts, wm, offs, out_0, out_1, out
 
         for t in range(2):
             first_h, second_h = gather_h(t, 0), gather_h(t, 1)
-            square = second_h if t else ts_listed[1]
+            square = second_h if t else ts_room[:, middle - HALF : middle]
             nc.scalar.activation(square, second_h, ACT.Square)
             nc.vector.tensor_tensor(first_h, first_h, first_h, ALU.mult)
             slope(0, first_h, first_out[t])
@@ -145,56 +151,57 @@ def tile_attend_gex_pl_tnh_x_kernel(tc, dyT, hT, ts, wm, offs, out_0, out_1, out
             return words.rearrange("p (c i t) -> p c t i", t=PACK, i=LINE)
 
         whole = slice(0, HALF)
-        low_words = held("low_words", PACK * QUARTER, BF16)[:]
+        first_words = held("first_words", PACK * HALF, BF16)[:]
         second_words = held("second_words", PACK * HALF, BF16)[:]
 
-        def weave_pair(u):
+        def words_of(words, cols):
+            return words[:, PACK * cols.start : PACK * cols.stop]
+
+        def weave_pair(copy, u, cols):
             planes = slice(2 * u, 2 * u + 2)
-            nc.scalar.copy(by_words(low_words)[:, :, planes], by_planes(dz_first, low)[:, :, planes])
+            copy(by_words(words_of(first_words, cols))[:, :, planes], by_planes(dz_first, cols)[:, :, planes])
 
         gather_dy(0)
         slope(1, second_in[LAST], second[LAST])
         gather_dy(1)
         slope(0, first_in[LAST], first_out[LAST])
-        weave_pair(0)
+        weave_pair(nc.scalar.copy, 0, low)
+        weave_pair(nc.vector.tensor_copy, 0, high)
         gather_dy(2)
         gather_dy(LAST)
-        weave_pair(1)
+        weave_pair(nc.scalar.copy, 1, low)
 
-        dz_codes = [held("dz_codes0", HALF, U32)]
+        dz_codes = {(0, low.start): held("dz_codes_low", QUARTER, U32)[:], (1, 0): held("dz_codes_second", HALF, U32)[:]}
         dz_scales = [held("dz_scales%d" % s, HALF, U8) for s in range(2)]
-        w_grouped = {}
+        w_grouped = [words_of(second_words, high), held("w_late", 2 * PACK * P, BF16)[:]]
         w_codes = [held("w_codes%d" % e, 2 * P, U32) for e in range(2)]
         w_scales = [held("w_scales%d" % e, 2 * P, U8) for e in range(2)]
 
         def quantize_dz(s, cols, words):
-            nc.vector.quantize_mx(dz_codes[s][:, cols].bitcast(E5M2), dz_scales[s][:, cols], words)
+            nc.vector.quantize_mx(dz_codes[s, cols.start].bitcast(E5M2), dz_scales[s][:, cols], words_of(words, cols))
 
-        def regroup_w(e, copy):
-            w_grouped[e] = held("w_grouped%d" % e, 2 * PACK * P, BF16, slot="w_grouped%d" % e)
-            target = w_grouped[e][:].rearrange("p (u m j) -> p m j u", u=2, j=PACK)
-            copy(target, w_raw[:].rearrange("p (j m e u) -> p m j u e", j=PACK, u=2, e=2)[:, :, :, :, e])
+        def regroup_w(e):
+            target = w_grouped[e].rearrange("p (u m j) -> p m j u", u=2, j=PACK)
+            nc.scalar.copy(target, w_raw[:].rearrange("p (j m e u) -> p m j u e", j=PACK, u=2, e=2)[:, :, :, :, e])
 
         def quantize_w(e):
-            nc.vector.quantize_mx(w_codes[e][:].bitcast(E4M3), w_scales[e][:], w_grouped[e][:])
+            nc.vector.quantize_mx(w_codes[e][:].bitcast(E4M3), w_scales[e][:], w_grouped[e])
 
         def second_product(cols):
-            words = second_words[:, PACK * cols.start : PACK * cols.stop]
-            nc.vector.tensor_tensor(by_words(words), by_planes(dy_second, cols), by_planes(factors, cols), ALU.mult)
+            nc.vector.tensor_tensor(by_words(words_of(second_words, cols)), by_planes(dy_second, cols), by_planes(factors, cols), ALU.mult)
 
         second_product(low)
-        regroup_w(0, nc.scalar.copy)
-        quantize_dz(0, low, low_words)
+        regroup_w(0)
+        quantize_dz(0, low, first_words)
+        weave_pair(nc.vector.tensor_copy, 1, high)
         quantize_w(0)
-        regroup_w(1, nc.scalar.copy)
+        regroup_w(1)
         second_product(high)
-        dz_codes.append(held("dz_codes1", HALF, U32, slot="w_grouped0"))
+        dz_codes.setdefault((0, high.start), held("dz_codes_high", QUARTER, U32, slot="w_raw")[:])
+        quantize_dz(0, high, first_words)
         quantize_dz(1, whole, second_words)
-        high_words = held("high_words", PACK * QUARTER, BF16, slot="w_raw")[:]
-        nc.vector.tensor_copy(by_words(high_words), by_planes(dz_first, high))
         quantize_w(1)
-        quantize_dz(0, high, high_words)
-        zeroed_window("w_grouped1")
+        zeroed_window("w_late")
 
         out_lanes = out_0.rearrange("(p j) c -> p j c", j=PACK)
         product_banks = {(lane, s): banks[(2 * lane + s + 4) % 8] for lane in range(PACK) for s in range(2)}
@@ -202,7 +209,7 @@ def tile_attend_gex_pl_tnh_x_kernel(tc, dyT, hT, ts, wm, offs, out_0, out_1, out
         def product(lane, s, cols=whole):
             block = slice((lane % 2) * P, (lane % 2 + 1) * P)
             nc.tensor.matmul_mx(product_banks[lane, s][:, cols], lhsT=w_codes[lane // 2][:, block].bitcast(E4M3), lhsT_scale=w_scales[lane // 2][:, block],
-                                rhs=dz_codes[s][:, cols].bitcast(E5M2), rhs_scale=dz_scales[s][:, cols], start=True, stop=True)
+                                rhs=dz_codes[s, cols.start].bitcast(E5M2), rhs_scale=dz_scales[s][:, cols], start=True, stop=True)
 
         sources = held("sources", 3 * N)
 
@@ -231,23 +238,23 @@ def tile_attend_gex_pl_tnh_x_kernel(tc, dyT, hT, ts, wm, offs, out_0, out_1, out
             leave_bank(nc.scalar.copy, lane * N, lane, 0, low)
         scalar_scatter(1, 0, QUARTER, lane1)
         vector_scatter(0, 0, QUARTER, lane0)
-        for lane in (1, 0):
-            product(lane, 1)
-            leave_bank(nc.scalar.copy, lane * N + HALF, lane, 1)
+        for s, cols in ((0, high), (1, whole)):
+            for lane in (1, 0):
+                product(lane, s, cols)
+                leave_bank(nc.scalar.copy, lane * N + s * HALF + cols.start, lane, s, cols)
         product(2, 1)
-        for lane in range(2):
-            product(lane, 0, high)
-            leave_bank(nc.vector.tensor_copy, lane * N + QUARTER, lane, 0, high)
         scalar_scatter(1, N - WIDE, WIDE, lane1 + N - WIDE)
-        product(2, 0)
+        for cols in (low, high):
+            product(2, 0, cols)
         for s in (1, 0):
             leave_bank(nc.vector.tensor_copy, lane2 + s * HALF, 2, s)
         vector_scatter(0, QUARTER, N - QUARTER, lane0 + QUARTER)
         store(0)
         scalar_scatter(1, QUARTER, WIDE, lane1 + QUARTER)
         store(1)
-        for s in (1, 0):
-            product(3, s)
+        product(3, 1)
+        for cols in (low, high):
+            product(3, 0, cols)
         vector_scatter(2, 0, N, lane2)
         store(2)
         for lane in range(2):

@@ -51,10 +51,6 @@ def tile_attend_gex_pl_tnh_x_kernel(tc, dyT, hT, ts, wm, offs, out_0, out_1, out
         banks = [psum.tile([P, HALF], F32, name="bank%d" % i) for i in range(8)]
         column_banks, spread_banks = banks[0:2], banks[2:4]
 
-        warm = keep.tile([P, 2], F32, name="warm")
-        nc.gpsimd.memset(warm[:, 0:1], 0.0)
-        nc.scalar.activation(warm[:, 1:2], warm[:, 0:1], ACT.Square)
-
         identity = keep.tile([P, P], F32, name="identity")
         make_identity(nc, identity[:])
 
@@ -258,14 +254,17 @@ def tile_attend_gex_pl_tnh_x_kernel(tc, dyT, hT, ts, wm, offs, out_0, out_1, out
         vector_scatter(2, 0, N, lane2)
         store(2)
         for lane in range(2):
-            nc.gpsimd.tensor_scalar(*pair_lane(lane, slice(0, T)), 1.0, -0.0, ALU.mult, ALU.add)
+            nc.gpsimd.tensor_scalar(*pair_lane(lane, slice(0, T - P)), 1.0, -0.0, ALU.mult, ALU.add)
         leave_bank(nc.scalar.copy, lane1 + N - WIDE, 3, 1, slice(HALF - WIDE, HALF))
         scalar_scatter(3, N - WIDE, WIDE, lane1 + N - WIDE)
-        leave_bank(nc.scalar.copy, lane1 + QUARTER, 3, 0, high)
-        leave_bank(nc.scalar.copy, lane1 + HALF, 3, 1, slice(0, P))
-        scalar_scatter(3, QUARTER, WIDE, lane1 + QUARTER)
-        leave_bank(nc.scalar.copy, lane1, 3, 0, low)
-        scalar_scatter(3, 0, QUARTER, lane1)
+        middle_source = pairs[:].bitcast(F32)[:, T - P : T + QUARTER]
+        nc.scalar.copy(middle_source[:, 0:QUARTER], product_banks[3, 0][:, high])
+        nc.scalar.copy(middle_source[:, QUARTER:WIDE], product_banks[3, 1][:, 0:P])
+        nc.scalar.activation(windows[3][:].indirect(entries(QUARTER, WIDE)), middle_source, ACT.Copy)
+        leave_bank(nc.scalar.copy, lane1 + N - WIDE, 3, 0, low)
+        for lane in range(2):
+            nc.scalar.copy(*pair_lane(lane, slice(T - P, T)))
+        scalar_scatter(3, 0, QUARTER, lane1 + N - WIDE)
         store(3, nc.scalar)
 
         words = held("words", T * PACK, BF16)
@@ -276,8 +275,8 @@ def tile_attend_gex_pl_tnh_x_kernel(tc, dyT, hT, ts, wm, offs, out_0, out_1, out
             nc.vector.tensor_copy(*pair_lane(LAST, run))
         for b in range(QUADS):
             copy = nc.vector.tensor_copy if b == 1 else nc.scalar.copy
-            target = words[:, PACK * b * RUN : PACK * (b + 1) * RUN].bitcast(F32).rearrange("p (c i u) -> p c u i", u=2, i=LINE)
-            copy(target, pairs[:].bitcast(F32).rearrange("p (u c i) -> p c u i", u=2, i=LINE)[:, b * RUN // LINE : (b + 1) * RUN // LINE])
+            target = words[:, PACK * b * RUN : PACK * (b + 1) * RUN].bitcast(F32).rearrange("p (c u) -> p c u", u=2)
+            copy(target, pairs[:].bitcast(F32).rearrange("p (u c) -> p c u", u=2)[:, runs[b]])
         words_out = out_1[0].rearrange("p t l -> p (t l)").bitcast(I32)
         for b in range(QUADS):
             cols = slice(b * RUN, (b + 1) * RUN)

@@ -27,7 +27,7 @@ QUADS = P // QUAD
 RUN = T // QUADS
 BLOCKS = HALF // P
 STRIPE = 16
-LINE = 4
+LINE = 2
 TS_ROW = P - 1
 WIDE = 384
 ALIGN = 64
@@ -237,7 +237,8 @@ def tile_attend_gex_pl_tnh_x_kernel(tc, dyT, hT, ts, wm, offs, out_0, out_1, out
         for s, cols in ((0, high), (1, whole)):
             for lane in (1, 0):
                 product(lane, s, cols)
-                leave_bank(nc.scalar.copy, lane * N + s * HALF + cols.start, lane, s, cols)
+                copy = nc.vector.tensor_copy if (lane, s) == (0, 0) else nc.scalar.copy
+                leave_bank(copy, lane * N + s * HALF + cols.start, lane, s, cols)
         product(2, 1)
         scalar_scatter(1, N - WIDE, WIDE, lane1 + N - WIDE)
         for cols in (low, high):
@@ -273,10 +274,10 @@ def tile_attend_gex_pl_tnh_x_kernel(tc, dyT, hT, ts, wm, offs, out_0, out_1, out
         nc.vector.tensor_copy(*pair_lane(2, slice(0, T)))
         for run in runs:
             nc.vector.tensor_copy(*pair_lane(LAST, run))
-        for b in range(QUADS):
-            copy = nc.vector.tensor_copy if b == 1 else nc.scalar.copy
-            target = words[:, PACK * b * RUN : PACK * (b + 1) * RUN].bitcast(F32).rearrange("p (c u) -> p c u", u=2)
-            copy(target, pairs[:].bitcast(F32).rearrange("p (u c) -> p c u", u=2)[:, runs[b]])
+        for first, count in ((0, RUN), (RUN, RUN), (2 * RUN, RUN), (LAST * RUN, QUARTER), (T - QUARTER, QUARTER)):
+            copy = nc.vector.tensor_copy if first == RUN else nc.scalar.copy
+            target = words[:, PACK * first : PACK * (first + count)].bitcast(F32).rearrange("p (c u) -> p c u", u=2)
+            copy(target, pairs[:].bitcast(F32).rearrange("p (u c) -> p c u", u=2)[:, first : first + count])
         words_out = out_1[0].rearrange("p t l -> p (t l)").bitcast(I32)
         for b in range(QUADS):
             cols = slice(b * RUN, (b + 1) * RUN)

@@ -237,14 +237,14 @@ def tile_attend_gex_pl_tnh_x_kernel(tc, dyT, hT, ts, wm, offs, out_0, out_1, out
         for s, cols in ((0, high), (1, whole)):
             for lane in (1, 0):
                 product(lane, s, cols)
-                copy = nc.vector.tensor_copy if (lane, s) == (0, 0) else nc.scalar.copy
+                copy = nc.vector.tensor_copy if s == 0 else nc.scalar.copy
                 leave_bank(copy, lane * N + s * HALF + cols.start, lane, s, cols)
         product(2, 1)
         scalar_scatter(1, N - WIDE, WIDE, lane1 + N - WIDE)
         for cols in (low, high):
             product(2, 0, cols)
-        for s in (1, 0):
-            leave_bank(nc.vector.tensor_copy, lane2 + s * HALF, 2, s)
+        leave_bank(nc.vector.tensor_copy, lane2 + HALF, 2, 1)
+        leave_bank(nc.scalar.copy, lane2, 2, 0)
         vector_scatter(0, QUARTER, N - QUARTER, lane0 + QUARTER)
         store(0)
         scalar_scatter(1, QUARTER, WIDE, lane1 + QUARTER)

@@ -51,6 +51,10 @@ def tile_attend_gex_pl_tnh_x_kernel(tc, dyT, hT, ts, wm, offs, out_0, out_1, out
         banks = [psum.tile([P, HALF], F32, name="bank%d" % i) for i in range(8)]
         column_banks, spread_banks = banks[0:2], banks[2:4]
 
+        warm = keep.tile([P, 2], F32, name="warm")
+        nc.gpsimd.memset(warm[:, 0:1], 0.0)
+        nc.scalar.activation(warm[:, 1:2], warm[:, 0:1], ACT.Square)
+
         identity = keep.tile([P, P], F32, name="identity")
         make_identity(nc, identity[:])
 
@@ -226,8 +230,6 @@ def tile_attend_gex_pl_tnh_x_kernel(tc, dyT, hT, ts, wm, offs, out_0, out_1, out
         def pair_lane(lane, tokens):
             return pairs[:].rearrange("p (u c e) -> p u c e", u=2, e=2)[:, lane // 2, tokens, lane % 2], windows[lane][:, tokens]
 
-        runs = [slice(b * RUN, (b + 1) * RUN) for b in range(QUADS)]
-
         lane0, lane1, lane2 = 0, N, 2 * N
         for lane in (1, 0):
             product(lane, 0, low)
@@ -272,10 +274,11 @@ def tile_attend_gex_pl_tnh_x_kernel(tc, dyT, hT, ts, wm, offs, out_0, out_1, out
         codes = held("codes", T, U32)
         scales = held("scales", RUN, U8)
         nc.vector.tensor_copy(*pair_lane(2, slice(0, T)))
-        for run in runs:
-            nc.vector.tensor_copy(*pair_lane(LAST, run))
-        for first, count in ((0, RUN), (RUN, RUN), (2 * RUN, RUN), (LAST * RUN, QUARTER), (T - QUARTER, QUARTER)):
-            copy = nc.vector.tensor_copy if first == RUN else nc.scalar.copy
+        own = 5 * P
+        for first, count in ((0, QUARTER), (QUARTER, own - QUARTER), (own, N - own), (2 * RUN, RUN), (LAST * RUN, RUN)):
+            nc.vector.tensor_copy(*pair_lane(LAST, slice(first, first + count)))
+        for first, count in ((0, QUARTER), (QUARTER, own - QUARTER), (own, N - own), (2 * RUN, RUN), (LAST * RUN, QUARTER), (T - QUARTER, QUARTER)):
+            copy = nc.vector.tensor_copy if first == own else nc.scalar.copy
             target = words[:, PACK * first : PACK * (first + count)].bitcast(F32).rearrange("p (c u) -> p c u", u=2)
             copy(target, pairs[:].bitcast(F32).rearrange("p (u c) -> p c u", u=2)[:, first : first + count])
         words_out = out_1[0].rearrange("p t l -> p (t l)").bitcast(I32)

@@ -239,7 +239,7 @@ def tile_attend_gex_pl_tnh_x_kernel(tc, dyT, hT, ts, wm, offs, out_0, out_1, out
         for s, cols in ((0, high), (1, whole)):
             for lane in (1, 0):
                 product(lane, s, cols)
-                copy = nc.vector.tensor_copy if s == 0 else nc.scalar.copy
+                copy = nc.vector.tensor_copy if (lane, s) == (0, 0) else nc.scalar.copy
                 leave_bank(copy, lane * N + s * HALF + cols.start, lane, s, cols)
         product(2, 1)
         scalar_scatter(1, N - WIDE, WIDE, lane1 + N - WIDE)
@@ -265,14 +265,14 @@ def tile_attend_gex_pl_tnh_x_kernel(tc, dyT, hT, ts, wm, offs, out_0, out_1, out
         nc.scalar.copy(middle_source[:, QUARTER:WIDE], product_banks[3, 1][:, 0:P])
         nc.scalar.activation(windows[3][:].indirect(entries(QUARTER, WIDE)), middle_source, ACT.Copy)
         leave_bank(nc.scalar.copy, lane1 + N - WIDE, 3, 0, low)
-        for lane in range(2):
-            nc.scalar.copy(*pair_lane(lane, slice(T - P, T)))
         scalar_scatter(3, 0, QUARTER, lane1 + N - WIDE)
         store(3, nc.scalar)
 
         words = held("words", T * PACK, BF16)
         codes = held("codes", T, U32)
         scales = held("scales", RUN, U8)
+        for lane in range(2):
+            nc.vector.tensor_copy(*pair_lane(lane, slice(T - P, T)))
         nc.vector.tensor_copy(*pair_lane(2, slice(0, T)))
         own = 5 * P
         for first, count in ((0, QUARTER), (QUARTER, own - QUARTER), (own, N - own), (2 * RUN, RUN), (LAST * RUN, RUN)):

@@ -104,19 +104,19 @@ def tile_attend_gex_pl_tnh_x_kernel(tc, dyT, hT, ts, wm, offs, out_0, out_1, out
                 nc.tensor.transpose(spread_banks[s][:, c * P : (c + 1) * P], minus_ts[s][:, c : c + 1].to_broadcast([P, P]), identity[:])
 
         second = [plane(factors, t) for t in range(PACK)]
-        first_in = [held("first_h%d" % t, HALF)[:] for t in range(PACK)]
-        first_out = [second[LAST], first_in[1], held("first_factor2", HALF)[:], first_in[1]]
         dz_first = held("dz_first", PACK * HALF)
-        second_in = [plane(dz_first, 1), ts_room[:, middle : middle + HALF], plane(dz_first, 0), plane(dz_first, LAST)]
+        first_in = [plane(dz_first, 0) if t == 2 else held("first_h%d" % t, HALF)[:] for t in range(PACK)]
+        first_out = [second[LAST], first_in[1], held("first_factor2", HALF)[:], first_in[1]]
+        second_in = [plane(dz_first, 1), ts_room[:, middle : middle + HALF], held("second_h2", HALF)[:], plane(dz_first, LAST)]
 
-        def slope(s, source, target):
-            nc.vector.scalar_tensor_tensor(target, source, 1.0, spread_banks[s][:], ALU.subtract, ALU.mult)
+        def slope(s, source, target, cols=slice(0, HALF)):
+            nc.vector.scalar_tensor_tensor(target[:, cols], source[:, cols], 1.0, spread_banks[s][:, cols], ALU.subtract, ALU.mult)
 
         dy_second = held("dy_second", PACK * HALF)
         low, high = slice(0, QUARTER), slice(QUARTER, HALF)
 
         def gather_dy(t):
-            for cols in (slice(0, HALF),) if t < LAST else (low, high):
+            for cols in (slice(0, HALF),) if t == 2 else (low, high):
                 count = cols.stop - cols.start
                 nc.vector.tensor_tensor(plane(dz_first, t)[:, cols], dy_planes[t][:].indirect(entries(cols.start, count)), first_out[t][:, cols], ALU.mult)
             nc.scalar.activation(plane(dy_second, t), dy_planes[t][:].indirect(entries(HALF, HALF)), ACT.Copy)
@@ -152,7 +152,8 @@ def tile_attend_gex_pl_tnh_x_kernel(tc, dyT, hT, ts, wm, offs, out_0, out_1, out
 
         whole = slice(0, HALF)
         first_words = held("first_words", PACK * HALF, BF16)[:]
-        second_words = held("second_words", PACK * HALF, BF16)[:]
+        second_room = held("second_words", PACK * (HALF + P), BF16)
+        second_words = second_room[:, 0 : PACK * HALF]
 
         def words_of(words, cols):
             return words[:, PACK * cols.start : PACK * cols.stop]
@@ -162,9 +163,11 @@ def tile_attend_gex_pl_tnh_x_kernel(tc, dyT, hT, ts, wm, offs, out_0, out_1, out
             copy(by_words(words_of(first_words, cols))[:, :, planes], by_planes(dz_first, cols)[:, :, planes])
 
         gather_dy(0)
-        slope(1, second_in[LAST], second[LAST])
+        for cols in (low, high):
+            slope(1, second_in[LAST], second[LAST], cols)
         gather_dy(1)
-        slope(0, first_in[LAST], first_out[LAST])
+        for cols in (low, high):
+            slope(0, first_in[LAST], first_out[LAST], cols)
         weave_pair(nc.scalar.copy, 0, low)
         weave_pair(nc.vector.tensor_copy, 0, high)
         gather_dy(2)
@@ -173,7 +176,7 @@ def tile_attend_gex_pl_tnh_x_kernel(tc, dyT, hT, ts, wm, offs, out_0, out_1, out
 
         dz_codes = {(0, low.start): held("dz_codes_low", QUARTER, U32)[:], (1, 0): held("dz_codes_second", HALF, U32)[:]}
         dz_scales = [held("dz_scales%d" % s, HALF, U8) for s in range(2)]
-        w_grouped = [words_of(second_words, high), held("w_late", 2 * PACK * P, BF16)[:]]
+        w_grouped = [second_room[:, PACK * (HALF - P) : PACK * (HALF + P)], held("w_late", 2 * PACK * P, BF16)[:]]
         w_codes = [held("w_codes%d" % e, 2 * P, U32) for e in range(2)]
         w_scales = [held("w_scales%d" % e, 2 * P, U8) for e in range(2)]
 
@@ -194,7 +197,9 @@ def tile_attend_gex_pl_tnh_x_kernel(tc, dyT, hT, ts, wm, offs, out_0, out_1, out
         regroup_w(0)
         quantize_dz(0, low, first_words)
         weave_pair(nc.vector.tensor_copy, 1, high)
-        quantize_w(0)
+        for u in range(2):
+            block = slice(u * P, (u + 1) * P)
+            nc.vector.quantize_mx(w_codes[0][:, block].bitcast(E4M3), w_scales[0][:, block], words_of(w_grouped[0], block))
         regroup_w(1)
         second_product(high)
         dz_codes.setdefault((0, high.start), held("dz_codes_high", QUARTER, U32, slot="w_raw")[:])
@@ -207,7 +212,7 @@ def tile_attend_gex_pl_tnh_x_kernel(tc, dyT, hT, ts, wm, offs, out_0, out_1, out
         product_banks = {(lane, s): banks[(2 * lane + s + 4) % 8] for lane in range(PACK) for s in range(2)}
 
         def product(lane, s, cols=whole):
-            block = slice((lane % 2) * P, (lane % 2 + 1) * P)
+            block = slice((1 - lane % 2) * P, (2 - lane % 2) * P)
             nc.tensor.matmul_mx(product_banks[lane, s][:, cols], lhsT=w_codes[lane // 2][:, block].bitcast(E4M3), lhsT_scale=w_scales[lane // 2][:, block],
                                 rhs=dz_codes[s, cols.start].bitcast(E5M2), rhs_scale=dz_scales[s][:, cols], start=True, stop=True)
 
@@ -223,12 +228,12 @@ def tile_attend_gex_pl_tnh_x_kernel(tc, dyT, hT, ts, wm, offs, out_0, out_1, out
             nc.scalar.activation(windows[lane][:].indirect(entries(first, count)), sources[:, place : place + count], ACT.Copy)
 
         def store(lane, queue=nc.sync):
-            queue.dma_start(out_lanes[:, lane, :], windows[lane][:])
+            queue.dma_start(out_lanes[:, lane ^ 1, :], windows[lane][:])
 
         pairs = held("pairs", PACK * T, BF16)
 
         def pair_lane(lane, tokens):
-            return pairs[:].rearrange("p (u c e) -> p u c e", u=2, e=2)[:, lane // 2, tokens, lane % 2], windows[lane][:, tokens]
+            return pairs[:].rearrange("p (u c e) -> p u c e", u=2, e=2)[:, lane // 2, tokens, 1 - lane % 2], windows[lane][:, tokens]
 
         lane0, lane1, lane2 = 0, N, 2 * N
         for lane in (1, 0):
@@ -271,9 +276,8 @@ def tile_attend_gex_pl_tnh_x_kernel(tc, dyT, hT, ts, wm, offs, out_0, out_1, out
         words = held("words", T * PACK, BF16)
         codes = held("codes", T, U32)
         scales = held("scales", RUN, U8)
-        for lane in range(2):
-            nc.vector.tensor_copy(*pair_lane(lane, slice(T - P, T)))
-        nc.vector.tensor_copy(*pair_lane(2, slice(0, T)))
+        for lane, first in ((0, T - P), (2, 0), (1, T - P)):
+            nc.vector.tensor_copy(*pair_lane(lane, slice(first, T)))
         own = 5 * P
         for first, count in ((0, QUARTER), (QUARTER, own - QUARTER), (own, N - own), (2 * RUN, RUN), (LAST * RUN, RUN)):
             nc.vector.tensor_copy(*pair_lane(LAST, slice(first, first + count)))

@@ -264,20 +264,21 @@ def tile_attend_gex_pl_tnh_x_kernel(tc, dyT, hT, ts, wm, offs, out_0, out_1, out
         for lane in range(2):
             nc.gpsimd.tensor_scalar(*pair_lane(lane, slice(0, T - P)), 1.0, -0.0, ALU.mult, ALU.add)
         leave_bank(nc.scalar.copy, lane1 + N - WIDE, 3, 1, slice(HALF - WIDE, HALF))
-        scalar_scatter(3, N - WIDE, WIDE, lane1 + N - WIDE)
         middle_source = pairs[:].bitcast(F32)[:, T - P : T + QUARTER]
         nc.scalar.copy(middle_source[:, 0:QUARTER], product_banks[3, 0][:, high])
         nc.scalar.copy(middle_source[:, QUARTER:WIDE], product_banks[3, 1][:, 0:P])
+        scalar_scatter(3, N - WIDE, WIDE, lane1 + N - WIDE)
+        leave_bank(nc.scalar.copy, lane1 + QUARTER, 3, 0, low)
         nc.scalar.activation(windows[3][:].indirect(entries(QUARTER, WIDE)), middle_source, ACT.Copy)
-        leave_bank(nc.scalar.copy, lane1 + N - WIDE, 3, 0, low)
-        scalar_scatter(3, 0, QUARTER, lane1 + N - WIDE)
+        scalar_scatter(3, 0, QUARTER, lane1 + QUARTER)
         store(3, nc.scalar)
 
         words = held("words", T * PACK, BF16)
         codes = held("codes", T, U32)
         scales = held("scales", RUN, U8)
-        for lane, first in ((0, T - P), (2, 0), (1, T - P)):
-            nc.vector.tensor_copy(*pair_lane(lane, slice(first, T)))
+        for lane in range(2):
+            nc.scalar.copy(*pair_lane(lane, slice(T - P, T)))
+        nc.vector.tensor_copy(*pair_lane(2, slice(0, T)))
         own = 5 * P
         for first, count in ((0, QUARTER), (QUARTER, own - QUARTER), (own, N - own), (2 * RUN, RUN), (LAST * RUN, RUN)):
             nc.vector.tensor_copy(*pair_lane(LAST, slice(first, first + count)))

@@ -119,7 +119,9 @@ def tile_attend_gex_pl_tnh_x_kernel(tc, dyT, hT, ts, wm, offs, out_0, out_1, out
             for cols in (slice(0, HALF),) if t == 2 else (low, high):
                 count = cols.stop - cols.start
                 nc.vector.tensor_tensor(plane(dz_first, t)[:, cols], dy_planes[t][:].indirect(entries(cols.start, count)), first_out[t][:, cols], ALU.mult)
-            nc.scalar.activation(plane(dy_second, t), dy_planes[t][:].indirect(entries(HALF, HALF)), ACT.Copy)
+            for cols in (slice(0, HALF),) if t < LAST else (low, high):
+                count = cols.stop - cols.start
+                nc.scalar.activation(plane(dy_second, t)[:, cols], dy_planes[t][:].indirect(entries(HALF + cols.start, count)), ACT.Copy)
 
         def gather_h(t, s):
             target, window = (first_in, second_in)[s][t], h_planes[t][:].indirect(entries(s * HALF, HALF))
@@ -162,6 +164,10 @@ def tile_attend_gex_pl_tnh_x_kernel(tc, dyT, hT, ts, wm, offs, out_0, out_1, out
             planes = slice(2 * u, 2 * u + 2)
             copy(by_words(words_of(first_words, cols))[:, :, planes], by_planes(dz_first, cols)[:, :, planes])
 
+        def second_product(cols, planes=slice(0, PACK)):
+            views = by_words(words_of(second_words, cols)), by_planes(dy_second, cols), by_planes(factors, cols)
+            nc.vector.tensor_tensor(*[view[:, :, planes] for view in views], ALU.mult)
+
         gather_dy(0)
         for cols in (low, high):
             slope(1, second_in[LAST], second[LAST], cols)
@@ -170,6 +176,7 @@ def tile_attend_gex_pl_tnh_x_kernel(tc, dyT, hT, ts, wm, offs, out_0, out_1, out
             slope(0, first_in[LAST], first_out[LAST], cols)
         weave_pair(nc.scalar.copy, 0, low)
         weave_pair(nc.vector.tensor_copy, 0, high)
+        second_product(low, slice(0, 2))
         gather_dy(2)
         gather_dy(LAST)
         weave_pair(nc.scalar.copy, 1, low)
@@ -183,6 +190,9 @@ def tile_attend_gex_pl_tnh_x_kernel(tc, dyT, hT, ts, wm, offs, out_0, out_1, out
         def quantize_dz(s, cols, words):
             nc.vector.quantize_mx(dz_codes[s, cols.start].bitcast(E5M2), dz_scales[s][:, cols], words_of(words, cols))
 
+        def quantize_second(cols):
+            nc.vector.quantize_mx(dz_codes[1, 0][:, cols].bitcast(E5M2), dz_scales[1][:, cols], words_of(second_words, cols))
+
         def regroup_w(e):
             target = w_grouped[e].rearrange("p (u m j) -> p m j u", u=2, j=PACK)
             nc.scalar.copy(target, w_raw[:].rearrange("p (j m e u) -> p m j u e", j=PACK, u=2, e=2)[:, :, :, :, e])
@@ -190,21 +200,20 @@ def tile_attend_gex_pl_tnh_x_kernel(tc, dyT, hT, ts, wm, offs, out_0, out_1, out
         def quantize_w(e):
             nc.vector.quantize_mx(w_codes[e][:].bitcast(E4M3), w_scales[e][:], w_grouped[e])
 
-        def second_product(cols):
-            nc.vector.tensor_tensor(by_words(words_of(second_words, cols)), by_planes(dy_second, cols), by_planes(factors, cols), ALU.mult)
-
-        second_product(low)
+        second_product(low, slice(2, PACK))
         regroup_w(0)
         quantize_dz(0, low, first_words)
         weave_pair(nc.vector.tensor_copy, 1, high)
+        second_product(slice(QUARTER, QUARTER + P // 2))
+        quantize_second(low)
         for u in range(2):
             block = slice(u * P, (u + 1) * P)
             nc.vector.quantize_mx(w_codes[0][:, block].bitcast(E4M3), w_scales[0][:, block], words_of(w_grouped[0], block))
         regroup_w(1)
-        second_product(high)
+        second_product(slice(QUARTER + P // 2, HALF))
         dz_codes.setdefault((0, high.start), held("dz_codes_high", QUARTER, U32, slot="w_raw")[:])
         quantize_dz(0, high, first_words)
-        quantize_dz(1, whole, second_words)
+        quantize_second(high)
         quantize_w(1)
         zeroed_window("w_late")
 
@@ -244,7 +253,7 @@ def tile_attend_gex_pl_tnh_x_kernel(tc, dyT, hT, ts, wm, offs, out_0, out_1, out
         for s, cols in ((0, high), (1, whole)):
             for lane in (1, 0):
                 product(lane, s, cols)
-                copy = nc.vector.tensor_copy if (lane, s) == (0, 0) else nc.scalar.copy
+                copy = nc.vector.tensor_copy if s == 0 else nc.scalar.copy
                 leave_bank(copy, lane * N + s * HALF + cols.start, lane, s, cols)
         product(2, 1)
         scalar_scatter(1, N - WIDE, WIDE, lane1 + N - WIDE)

from contextlib import ExitStack

import concourse.mybir as mybir
from concourse.masks import make_identity

N, T, D, DV = 1024, 2048, 512, 512
FLOPS = 2 * DV * D * N

F32 = mybir.dt.float32
BF16 = mybir.dt.bfloat16
I32 = mybir.dt.int32
U32 = mybir.dt.uint32
U16 = mybir.dt.uint16
U8 = mybir.dt.uint8
E4M3 = mybir.dt.float8_e4m3fn_x4
E5M2 = mybir.dt.float8_e5m2_x4
ALU = mybir.AluOpType
ACT = mybir.ActivationFunctionType

P = 128
PACK = 4
LAST = PACK - 1
HALF = 512
QUARTER = HALF // 2
QUAD = 32
QUADS = P // QUAD
RUN = T // QUADS
BLOCKS = HALF // P
STRIPE = 16
LINE = 2
TS_ROW = P - 1
WIDE = 384
ALIGN = 64


def tile_attend_gex_pl_tnh_x_kernel(tc, dyT, hT, ts, wm, offs, out_0, out_1, out_2):
    nc = tc.nc
    with ExitStack() as ctx:
        keep = ctx.enter_context(tc.tile_pool(name="keep", bufs=1))
        psum = ctx.enter_context(tc.psum_pool(name="psum", bufs=1))

        def held(name, columns, dtype=F32, slot=None):
            return keep.tile([P, columns], dtype, name=name, tag=slot or name, align_bytes=ALIGN)

        offsets = keep.tile([P, N // STRIPE], U16, name="offsets")
        nc.sync.dma_start(offsets[:], offs)

        def entries(first, count):
            return offsets[:, first // STRIPE : (first + count) // STRIPE]

        banks = [psum.tile([P, HALF], F32, name="bank%d" % i) for i in range(8)]
        column_banks, spread_banks = banks[0:2], banks[2:4]

        warm = keep.tile([P, 2], F32, name="warm")
        nc.gpsimd.memset(warm[:, 0:1], 0.0)
        nc.scalar.activation(warm[:, 1:2], warm[:, 0:1], ACT.Square)

        identity = keep.tile([P, P], F32, name="identity")
        make_identity(nc, identity[:])

        ts_window = held("ts_window", T)
        nc.sync.dma_start(ts_window[TS_ROW:P, :], ts[TS_ROW:P, :])
        nc.gpsimd.memset(ts_window[0:TS_ROW, T // 2 : T], 0.0)
        nc.vector.memset(ts_window[0:TS_ROW, 0 : T // 2 - 1], 0.0)
        nc.vector.memset(ts_window[0:TS_ROW, T // 2 - 1 : T // 2], 0.0)

        h_rows = hT.rearrange("(p j) c -> p j c", j=PACK)
        dy_rows = dyT.rearrange("(p j) c -> p j c", j=PACK)
        h_planes = [held("h_plane%d" % t, T) for t in range(PACK)]
        dy_planes = [held("dy_plane%d" % t, T) for t in range(PACK)]
        w_raw = held("w_raw", PACK * D)
        for t in range(PACK):
            nc.sync.dma_start(h_planes[t][:], h_rows[:, t, :])
        for t in range(PACK):
            nc.sync.dma_start(dy_planes[t][:], dy_rows[:, t, :])
        nc.sync.dma_start(w_raw[:], wm[0].rearrange("(p j) d -> p (j d)", j=PACK))

        windows = []

        def zeroed_window(slot=None):
            windows.append(held("window%d" % len(windows), T, slot=slot))
            nc.gpsimd.memset(windows[-1][:], 0.0)

        for lane in range(LAST):
            zeroed_window()

        def plane(tile, t):
            return tile[:, t * HALF : (t + 1) * HALF]

        factors = held("factors", PACK * HALF)
        ts_room = held("ts_room", 3 * HALF)
        ts_listed = [held("ts_first", HALF)[:], ts_room[:, HALF:N]]
        middle = N - P // 2
        nc.vector.tensor_copy(ts_listed[0], ts_window[:].indirect(entries(0, HALF)))
        nc.scalar.activation(ts_listed[1], ts_window[:].indirect(entries(HALF, HALF)), ACT.Copy)
        for c in range(BLOCKS):
            for s in range(2):
                nc.tensor.transpose(column_banks[s][:, c * P : (c + 1) * P], ts_listed[s][:, c * P : (c + 1) * P], identity[:])
        minus_ts = [keep.tile([P, BLOCKS], F32, name="minus_ts%d" % s) for s in range(2)]
        for s in range(2):
            nc.scalar.activation(minus_ts[s][:], column_banks[s][:, TS_ROW:HALF:P], ACT.Copy, scale=-1.0)
        for c in range(BLOCKS):
            for s in range(2):
                nc.tensor.transpose(spread_banks[s][:, c * P : (c + 1) * P], minus_ts[s][:, c : c + 1].to_broadcast([P, P]), identity[:])

        second = [plane(factors, t) for t in range(PACK)]
        dz_first = held("dz_first", PACK * HALF)
        first_in = [plane(dz_first, 0) if t == 2 else held("first_h%d" % t, HALF)[:] for t in range(PACK)]
        first_out = [second[LAST], first_in[1], held("first_factor2", HALF)[:], first_in[1]]
        second_in = [plane(dz_first, 1), ts_room[:, middle : middle + HALF], held("second_h2", HALF)[:], plane(dz_first, LAST)]

        def slope(s, source, target, cols=slice(0, HALF)):
            nc.vector.scalar_tensor_tensor(target[:, cols], source[:, cols], 1.0, spread_banks[s][:, cols], ALU.subtract, ALU.mult)

        dy_second = held("dy_second", PACK * HALF)
        low, high = slice(0, QUARTER), slice(QUARTER, HALF)

        def gather_dy(t):
            for cols in (slice(0, HALF),) if t == 2 else (low, high):
                count = cols.stop - cols.start
                nc.vector.tensor_tensor(plane(dz_first, t)[:, cols], dy_planes[t][:].indirect(entries(cols.start, count)), first_out[t][:, cols], ALU.mult)
            for cols in (slice(0, HALF),) if t < LAST else (low, high):
                count = cols.stop - cols.start
                nc.scalar.activation(plane(dy_second, t)[:, cols], dy_planes[t][:].indirect(entries(HALF + cols.start, count)), ACT.Copy)

        def gather_h(t, s):
            target, window = (first_in, second_in)[s][t], h_planes[t][:].indirect(entries(s * HALF, HALF))
            if t < 2 and s == 0:
                nc.vector.tensor_copy(target, window)
            else:
                nc.scalar.activation(target, window, ACT.Copy)
            return target

        for t in range(2):
            first_h, second_h = gather_h(t, 0), gather_h(t, 1)
            square = second_h if t else ts_room[:, middle - HALF : middle]
            nc.scalar.activation(square, second_h, ACT.Square)
            nc.vector.tensor_tensor(first_h, first_h, first_h, ALU.mult)
            slope(0, first_h, first_out[t])
            slope(1, square, second[t])
        both = [(gather_h(2, 0), first_out[2]), (gather_h(2, 1), second[2])]
        for s, (listed, target) in enumerate(both):
            slope(s, listed, target)
        for listed, target in both:
            nc.vector.scalar_tensor_tensor(target, listed, 1.0, target, ALU.add, ALU.mult)
        for listed in [gather_h(LAST, 1), gather_h(LAST, 0)]:
            nc.scalar.activation(listed, listed, ACT.Square)

        def by_planes(tile, cols):
            return tile[:].rearrange("p (t c i) -> p c t i", t=PACK, i=LINE)[:, cols.start // LINE : cols.stop // LINE]

        def by_words(words):
            return words.rearrange("p (c i t) -> p c t i", t=PACK, i=LINE)

        whole = slice(0, HALF)
        first_words = held("first_words", PACK * HALF, BF16)[:]
        second_room = held("second_words", PACK * (HALF + P), BF16)
        second_words = second_room[:, 0 : PACK * HALF]

        def words_of(words, cols):
            return words[:, PACK * cols.start : PACK * cols.stop]

        def weave_pair(copy, u, cols):
            planes = slice(2 * u, 2 * u + 2)
            copy(by_words(words_of(first_words, cols))[:, :, planes], by_planes(dz_first, cols)[:, :, planes])

        def second_product(cols, planes=slice(0, PACK)):
            views = by_words(words_of(second_words, cols)), by_planes(dy_second, cols), by_planes(factors, cols)
            nc.vector.tensor_tensor(*[view[:, :, planes] for view in views], ALU.mult)

        gather_dy(0)
        for cols in (low, high):
            slope(1, second_in[LAST], second[LAST], cols)
        gather_dy(1)
        for cols in (low, high):
            slope(0, first_in[LAST], first_out[LAST], cols)
        weave_pair(nc.scalar.copy, 0, low)
        weave_pair(nc.vector.tensor_copy, 0, high)
        second_product(low, slice(0, 2))
        gather_dy(2)
        gather_dy(LAST)
        weave_pair(nc.scalar.copy, 1, low)

        dz_codes = {(0, low.start): held("dz_codes_low", QUARTER, U32)[:], (1, 0): held("dz_codes_second", HALF, U32)[:]}
        dz_scales = [held("dz_scales%d" % s, HALF, U8) for s in range(2)]
        w_grouped = [second_room[:, PACK * (HALF - P) : PACK * (HALF + P)], held("w_late", 2 * PACK * P, BF16)[:]]
        w_codes = [held("w_codes%d" % e, 2 * P, U32) for e in range(2)]
        w_scales = [held("w_scales%d" % e, 2 * P, U8) for e in range(2)]

        def quantize_dz(s, cols, words):
            nc.vector.quantize_mx(dz_codes[s, cols.start].bitcast(E5M2), dz_scales[s][:, cols], words_of(words, cols))

        def quantize_second(cols):
            nc.vector.quantize_mx(dz_codes[1, 0][:, cols].bitcast(E5M2), dz_scales[1][:, cols], words_of(second_words, cols))

        def regroup_w(e):
            target = w_grouped[e].rearrange("p (u m j) -> p m j u", u=2, j=PACK)
            nc.scalar.copy(target, w_raw[:].rearrange("p (j m e u) -> p m j u e", j=PACK, u=2, e=2)[:, :, :, :, e])

        def quantize_w(e):
            nc.vector.quantize_mx(w_codes[e][:].bitcast(E4M3), w_scales[e][:], w_grouped[e])

        second_product(low, slice(2, PACK))
        regroup_w(0)
        quantize_dz(0, low, first_words)
        weave_pair(nc.vector.tensor_copy, 1, high)
        second_product(slice(QUARTER, QUARTER + P // 2))
        quantize_second(low)
        for u in range(2):
            block = slice(u * P, (u + 1) * P)
            nc.vector.quantize_mx(w_codes[0][:, block].bitcast(E4M3), w_scales[0][:, block], words_of(w_grouped[0], block))
        regroup_w(1)
        second_product(slice(QUARTER + P // 2, HALF))
        dz_codes.setdefault((0, high.start), held("dz_codes_high", QUARTER, U32, slot="w_raw")[:])
        quantize_dz(0, high, first_words)
        quantize_second(high)
        quantize_w(1)
        zeroed_window("w_late")

        out_lanes = out_0.rearrange("(p j) c -> p j c", j=PACK)
        product_banks = {(lane, s): banks[(2 * lane + s + 4) % 8] for lane in range(PACK) for s in range(2)}

        def product(lane, s, cols=whole):
            block = slice((1 - lane % 2) * P, (2 - lane % 2) * P)
            nc.tensor.matmul_mx(product_banks[lane, s][:, cols], lhsT=w_codes[lane // 2][:, block].bitcast(E4M3), lhsT_scale=w_scales[lane // 2][:, block],
                                rhs=dz_codes[s, cols.start].bitcast(E5M2), rhs_scale=dz_scales[s][:, cols], start=True, stop=True)

        sources = held("sources", 3 * N)

        def leave_bank(copy, place, lane, s, cols=whole):
            copy(sources[:, place : place + cols.stop - cols.start], product_banks[lane, s][:, cols])

        def vector_scatter(lane, first, count, place):
            nc.vector.tensor_copy(windows[lane][:].indirect(entries(first, count)), sources[:, place : place + count])

        def scalar_scatter(lane, first, count, place):
            nc.scalar.activation(windows[lane][:].indirect(entries(first, count)), sources[:, place : place + count], ACT.Copy)

        def store(lane, queue=nc.sync):
            queue.dma_start(out_lanes[:, lane ^ 1, :], windows[lane][:])

        pairs = held("pairs", PACK * T, BF16)

        def pair_lane(lane, tokens):
            return pairs[:].rearrange("p (u c e) -> p u c e", u=2, e=2)[:, lane // 2, tokens, 1 - lane % 2], windows[lane][:, tokens]

        lane0, lane1, lane2 = 0, N, 2 * N
        for lane in (1, 0):
            product(lane, 0, low)
            leave_bank(nc.scalar.copy, lane * N, lane, 0, low)
        scalar_scatter(1, 0, QUARTER, lane1)
        vector_scatter(0, 0, QUARTER, lane0)
        for s, cols in ((0, high), (1, whole)):
            for lane in (1, 0):
                product(lane, s, cols)
                copy = nc.vector.tensor_copy if s == 0 else nc.scalar.copy
                leave_bank(copy, lane * N + s * HALF + cols.start, lane, s, cols)
        product(2, 1)
        scalar_scatter(1, N - WIDE, WIDE, lane1 + N - WIDE)
        for cols in (low, high):
            product(2, 0, cols)
        leave_bank(nc.vector.tensor_copy, lane2 + HALF, 2, 1)
        leave_bank(nc.scalar.copy, lane2, 2, 0)
        vector_scatter(0, QUARTER, N - QUARTER, lane0 + QUARTER)
        store(0)
        scalar_scatter(1, QUARTER, WIDE, lane1 + QUARTER)
        store(1)
        product(3, 1)
        for cols in (low, high):
            product(3, 0, cols)
        vector_scatter(2, 0, N, lane2)
        store(2)
        for lane in range(2):
            nc.gpsimd.tensor_scalar(*pair_lane(lane, slice(0, T - P)), 1.0, -0.0, ALU.mult, ALU.add)
        leave_bank(nc.scalar.copy, lane1 + N - WIDE, 3, 1, slice(HALF - WIDE, HALF))
        middle_source = pairs[:].bitcast(F32)[:, T - P : T + QUARTER]
        nc.scalar.copy(middle_source[:, 0:QUARTER], product_banks[3, 0][:, high])
        nc.scalar.copy(middle_source[:, QUARTER:WIDE], product_banks[3, 1][:, 0:P])
        scalar_scatter(3, N - WIDE, WIDE, lane1 + N - WIDE)
        leave_bank(nc.scalar.copy, lane1 + QUARTER, 3, 0, low)
        nc.scalar.activation(windows[3][:].indirect(entries(QUARTER, WIDE)), middle_source, ACT.Copy)
        scalar_scatter(3, 0, QUARTER, lane1 + QUARTER)
        store(3, nc.scalar)

        words = held("words", T * PACK, BF16)
        codes = held("codes", T, U32)
        scales = held("scales", RUN, U8)
        for lane in range(2):
            nc.scalar.copy(*pair_lane(lane, slice(T - P, T)))
        nc.vector.tensor_copy(*pair_lane(2, slice(0, T)))
        own = 5 * P
        for first, count in ((0, QUARTER), (QUARTER, own - QUARTER), (own, N - own), (2 * RUN, RUN), (LAST * RUN, RUN)):
            nc.vector.tensor_copy(*pair_lane(LAST, slice(first, first + count)))
        for first, count in ((0, QUARTER), (QUARTER, own - QUARTER), (own, N - own), (2 * RUN, RUN), (LAST * RUN, QUARTER), (T - QUARTER, QUARTER)):
            copy = nc.vector.tensor_copy if first == own else nc.scalar.copy
            target = words[:, PACK * first : PACK * (first + count)].bitcast(F32).rearrange("p (c u) -> p c u", u=2)
            copy(target, pairs[:].bitcast(F32).rearrange("p (u c) -> p c u", u=2)[:, first : first + count])
        words_out = out_1[0].rearrange("p t l -> p (t l)").bitcast(I32)
        for b in range(QUADS):
            cols = slice(b * RUN, (b + 1) * RUN)
            for piece in (low, high):
                tokens = slice(cols.start + piece.start, cols.start + piece.stop)
                nc.vector.quantize_mx(codes[:, tokens].bitcast(E4M3), scales[PACK * b : P, piece], words[:, PACK * tokens.start : PACK * tokens.stop])
                if b == LAST:
                    nc.sync.dma_start(words_out[:, tokens], codes[:, tokens].bitcast(I32))
            if b < LAST:
                nc.sync.dma_start(words_out[:, cols], codes[:, cols].bitcast(I32))
        scales_out = out_2[0].bitcast(I32)
        for q in range(QUADS):
            queue = nc.sync if q == LAST else nc.scalar
            queue.dma_start(scales_out[PACK * q : PACK * (q + 1), :].rearrange("r (b c) -> b r c", b=QUADS), scales[QUAD * q : QUAD * q + QUADS * PACK, :].bitcast(I32))
